import numpy as np
import ml_dtypes


def mxq(x, axis, fmt="e4m3"):
    dtype, down = {"e4m3": (ml_dtypes.float8_e4m3fn, 7), "e5m2": (ml_dtypes.float8_e5m2, 14)}[fmt]
    v = np.moveaxis(np.asarray(x, np.float32).astype(ml_dtypes.bfloat16).astype(np.float64), axis, -1)
    blocks = v.reshape(v.shape[:-1] + (-1, 32))
    amax = np.abs(blocks).max(-1, keepdims=True)
    byte = np.maximum(np.where(amax > 0, np.frexp(amax)[1] - 1 + 127, 0) - down, 1)
    scale = np.exp2(byte - 127.0)
    codes = (blocks / scale).astype(np.float32).astype(dtype).astype(np.float64)
    return np.moveaxis((codes * scale).reshape(v.shape), -1, axis)


WIDE = False


def mx_kscale(k):
    if not WIDE:
        return np.ones(k)
    levels = np.array([10, -10, 5, -5, 0])
    if k % 512:
        return np.exp2(np.random.permutation(np.resize(levels, k // 32))).repeat(32)
    a = np.empty((k // 512, 16))
    for p in range(k // 512):
        a[p, :8] = np.random.permutation(np.resize(levels, 8))
        for g in range(8):
            far = levels[np.abs(levels - a[p, g]) >= 10]
            a[p, g + 8] = far[np.random.randint(len(far))]
    return np.exp2(a.ravel()).repeat(32)


def f64(x):
    return np.asarray(x).astype(np.float64)


def striped(idx):
    return np.tile(idx.reshape(-1, 16).T, (8, 1)).astype(np.uint16)


def unstriped(offs):
    return offs[:16].T.reshape(-1).astype(np.int64)


E2M1 = np.array([0.0, 0.5, 1.0, 1.5, 2.0, 3.0, 4.0, 6.0, -0.0, -0.5, -1.0, -1.5, -2.0, -3.0, -4.0, -6.0])


def pack_weight(w, fmt):
    k, n = w.shape
    w = f64(np.asarray(w, np.float32).astype(ml_dtypes.bfloat16)).reshape(k // 32, 32, n)
    amax = np.abs(w).max(1)
    if fmt == "e4m3":
        byte = np.frexp(amax)[1] - 1 + 127 - 7
    else:
        mant, ex = np.frexp(amax / 6.0)
        byte = np.where(mant > 0.5, ex, ex - 1) + 127
    byte = np.clip(np.where(amax > 0, byte, 1), 1, 254)
    scaled = (w * np.exp2(127.0 - byte)[:, None, :]).reshape(k, n).astype(np.float32)
    by_word = np.ascontiguousarray(scaled.reshape(k // 512, 128, 4, n).transpose(0, 1, 3, 2))
    if fmt == "e4m3":
        words = by_word.astype(ml_dtypes.float8_e4m3fn).view(np.uint8)
    else:
        c = by_word.astype(ml_dtypes.float4_e2m1fn).view(np.uint8) & 0xF
        words = (c[..., 0::2] | (c[..., 1::2] << 4)).reshape(k // 512, 128, 2 * n)
    return np.ascontiguousarray(words), np.ascontiguousarray(byte.astype(np.uint8).reshape(k // 512, 16, n))


def unpack_weight(words, scales, fmt):
    g, _, n = scales.shape
    words = np.ascontiguousarray(words).reshape(g, 128, n, -1)
    if fmt == "e4m3":
        vals = words.view(ml_dtypes.float8_e4m3fn).astype(np.float64)
    else:
        nib = np.empty((g, 128, n, 4), np.uint8)
        nib[..., 0::2] = words & 0xF
        nib[..., 1::2] = words >> 4
        vals = E2M1[nib]
    vals = vals * np.repeat(np.exp2(scales.astype(np.float64) - 127.0), 8, axis=1)[..., None]
    return vals.transpose(0, 1, 3, 2).reshape(g * 512, n)


def gelu(v):
    return 0.5 * v * (1.0 + np.tanh(np.sqrt(2.0 / np.pi) * (v + 0.044715 * v**3)))


K, T, S, P, H = 1024, 4096, 1536, 768, 512

def setup_inputs():
    n = np.random.standard_normal
    s = mx_kscale(K)[:, None]
    u = mx_kscale(H)[:, None]
    tab_words, tab_scales = pack_weight(n((K, T)) * s, "e4m3")
    w2_words, w2_scales = pack_weight(n((H, H)) / np.sqrt(H) / u, "e2m1")
    return {
        "tab_words": tab_words, "tab_scales": tab_scales,
        "offs": striped(np.random.permutation(T)[:S]),
        "pos1": striped(np.random.permutation(S)[:P]),
        "pos2": striped(np.random.permutation(S)[:P]),
        "w1": (n((K, H)) / np.sqrt(K) / s).astype(np.float32),
        "gain": (np.exp(0.3 * n(H)) * u[:, 0]).astype(np.float32),
        "w2_words": w2_words, "w2_scales": w2_scales,
    }

def reference(tab_words, tab_scales, offs, pos1, pos2, w1, gain, w2_words, w2_scales):
    v = unpack_weight(tab_words, tab_scales, "e4m3")[:, unstriped(offs)]
    h = mxq(f64(w1), 0, "e4m3").T @ v
    a = h[:, unstriped(pos1)]
    b = h[:, unstriped(pos2)]
    z = f64(gain)[:, None] * np.tanh(a - b)
    w2 = unpack_weight(w2_words, w2_scales, "e2m1")
    y = w2.T @ mxq(z, 0, "e4m3")
    return a + y

@@ -1,0 +1,283 @@
+from contextlib import ExitStack
+
+import concourse.mybir as mybir
+
+K, T, S, NP, H = 1024, 4096, 1536, 768, 512
+FLOPS = 2 * K * H * S + 2 * H * H * NP
+
+F32 = mybir.dt.float32
+BF16 = mybir.dt.bfloat16
+I32 = mybir.dt.int32
+U32 = mybir.dt.uint32
+U16 = mybir.dt.uint16
+U8 = mybir.dt.uint8
+FP8X4 = mybir.dt.float8_e4m3fn_x4
+FP4X4 = mybir.dt.float4_e2m1fn_x4
+ALU = mybir.AluOpType
+ACT = mybir.ActivationFunctionType
+
+P = 128
+PACK = 4
+PASSES = K // (P * PACK)
+BANK = 512
+SLICES = S // BANK
+CHUNK = 256
+
+
+def tile_list_pairwise_state_correction_kernel(
+    tc, tab_words, tab_scales, offs, pos1, pos2, w1, gain, w2_words, w2_scales, out
+):
+    nc = tc.nc
+    with ExitStack() as ctx:
+        lists = ctx.enter_context(tc.tile_pool(name="lists", bufs=1))
+        keep = ctx.enter_context(tc.tile_pool(name="keep", bufs=1))
+        reuse = ctx.enter_context(tc.tile_pool(name="reuse", bufs=1))
+        psum = ctx.enter_context(tc.psum_pool(name="psum", bufs=1))
+
+        offs_sb = lists.tile([P, S // 16], U16, name="offs_sb")
+        pos1_sb = lists.tile([P, NP // 16], U16, name="pos1_sb")
+        pos2_sb = lists.tile([P, NP // 16], U16, name="pos2_sb")
+
+        words = [keep.tile([P, T], I32, name="words%d" % a, align_bytes=64) for a in range(PASSES)]
+        tscale = reuse.tile([P, T // 4], I32, name="tscale", align_bytes=64, offset=0)
+        w1_raw = [keep.tile([P, PACK, H], F32, name="w1_raw%d" % a) for a in range(PASSES)]
+        gain_sb = keep.tile([P, PACK], F32, name="gain_sb")
+        w2_raw = keep.tile([P, 2 * H // 4], I32, name="w2_raw")
+        w2s_raw = keep.tile([P, H // 4], I32, name="w2s_raw")
+        warm = keep.tile([P, 8], F32, name="warm")
+        warm_out = keep.tile([P, 8], F32, name="warm_out")
+
+        nc.vector.memset(tscale[:], 0)
+        nc.vector.memset(w2s_raw[:], 0)
+        nc.vector.memset(warm[:], 0.0)
+        nc.scalar.activation(warm_out[:], warm[:], ACT.Tanh)
+
+        def load_words(a):
+            nc.sync.dma_start(
+                out=words[a][:], in_=tab_words[a].rearrange("p n t -> p (n t)").bitcast(I32)
+            )
+
+        def load_w1(a, c0, c1):
+            rows = w1[a * P * PACK : (a + 1) * P * PACK, c0:c1]
+            nc.sync.dma_start(
+                out=w1_raw[a][:, :, c0:c1], in_=rows.rearrange("(p j) c -> p j c", j=PACK)
+            )
+
+        nc.sync.dma_start(offs_sb[:], offs)
+        nc.sync.dma_start(out=w2_raw[:], in_=w2_words[0].bitcast(I32))
+        load_words(0)
+        for q in range(4):
+            nc.gpsimd.dma_start(
+                out=tscale[32 * q : 32 * q + 4 * PASSES, :],
+                in_=tab_scales[:, 4 * q : 4 * q + 4, :].bitcast(I32),
+            )
+        load_w1(0, 0, H)
+        load_words(1)
+        load_w1(1, 0, H // 2)
+        load_w1(1, H // 2, H)
+        nc.sync.dma_start(pos1_sb[:], pos1)
+        nc.sync.dma_start(pos2_sb[:], pos2)
+        nc.sync.dma_start(out=gain_sb[:], in_=gain.rearrange("(p t) -> p t", t=PACK))
+        for q in range(4):
+            nc.gpsimd.dma_start(
+                out=w2s_raw[32 * q : 32 * q + 4, :],
+                in_=w2_scales[0, 4 * q : 4 * q + 4, :].bitcast(I32),
+            )
+
+        g_words = [
+            keep.tile([P, S], U32, name="g_words0", align_bytes=64),
+            reuse.tile([P, S], U32, name="g_words1", align_bytes=64, offset=4 * H),
+        ]
+        g_scale = keep.tile([P, S], U8, name="g_scale", align_bytes=64)
+        w1_bf = [keep.tile([P, PACK, P, PACK], BF16, name="w1_bf%d" % a, align_bytes=64) for a in range(PASSES)]
+        w1_codes = [
+            keep.tile([P, H], U32, name="w1_codes0", align_bytes=64),
+            reuse.tile([P, H], U32, name="w1_codes1", align_bytes=64, offset=0),
+        ]
+        w1_scales = keep.tile([P, PASSES, H], U8, name="w1_scales", align_bytes=64)
+
+        def gather_words(a, s0, s1):
+            nc.vector.tensor_copy(
+                g_words[a][:, s0:s1],
+                words[a][:].bitcast(U32).indirect(offs_sb[:, s0 // 16 : s1 // 16]),
+            )
+
+        def cast_w1(a, t0, t1, m0, m1):
+            nc.scalar.copy(
+                w1_bf[a][:, t0:t1, m0:m1, :].rearrange("p t m j -> p m t j"),
+                w1_raw[a][:].rearrange("p j (m t) -> p m t j", t=PACK)[:, m0:m1, t0:t1, :],
+            )
+
+        def quant_w1(a, t0, t1):
+            nc.vector.quantize_mx(
+                out=w1_codes[a][:, t0 * P : t1 * P].bitcast(FP8X4),
+                scales=w1_scales[:, a, t0 * P : t1 * P],
+                in_=w1_bf[a][:, t0:t1, :, :].rearrange("p t m j -> p (t m j)"),
+            )
+
+        groups = [(t, s) for t in range(PACK) for s in range(SLICES)]
+        banks = {}
+
+        def h_pass(t, s, a):
+            if a == 0:
+                g = groups.index((t, s))
+                banks[(t, s)] = psum.tile([P, BANK], F32, name="bank%d" % (g % 8))
+            cols = slice(s * BANK, (s + 1) * BANK)
+            nc.tensor.matmul_mx(
+                out=banks[(t, s)][:],
+                lhsT=w1_codes[a][:, t * P : (t + 1) * P].bitcast(FP8X4),
+                lhsT_scale=w1_scales[:, a, t * P : (t + 1) * P],
+                rhs=g_words[a][:, cols].bitcast(FP8X4),
+                rhs_scale=g_scale[4 * a :, cols],
+                start=(a == 0),
+                stop=(a == PASSES - 1),
+            )
+
+        h = [keep.tile([P, S], F32, name="h%d" % t) for t in range(PACK)]
+
+        def h_copy(t, s):
+            nc.scalar.copy(h[t][:, s * BANK : (s + 1) * BANK], banks[(t, s)][:])
+
+        w2_codes = keep.tile([P, PACK, 2 * P], U8, name="w2_codes", align_bytes=64)
+        w2_sc = keep.tile([P, PACK, P], U8, name="w2_sc", align_bytes=64)
+        nc.vector.tensor_copy(
+            w2_codes[:].rearrange("p t (m b) -> p t m b", b=2),
+            w2_raw[:].bitcast(U8).rearrange("p (m t b) -> p t m b", t=PACK, b=2),
+        )
+        nc.vector.tensor_copy(g_scale[:], tscale[:].bitcast(U8).indirect(offs_sb[:]))
+        gather_words(0, 0, S)
+        cast_w1(0, 0, 2, 0, P)
+        cast_w1(0, 2, 4, 0, P)
+        quant_w1(0, 0, 4)
+        nc.vector.tensor_copy(
+            w2_sc[:], w2s_raw[:].bitcast(U8).rearrange("p (m t) -> p t m", t=PACK)
+        )
+        for t, s in groups[:8]:
+            h_pass(t, s, 0)
+        cast_w1(1, 0, 4, 0, P // 2)
+        cast_w1(1, 0, 2, P // 2, P)
+        cast_w1(1, 2, 4, P // 2, P)
+        gather_words(1, 0, BANK)
+        gather_words(1, BANK, 2 * BANK)
+        gather_words(1, 2 * BANK, S)
+        quant_w1(1, 0, 2)
+        quant_w1(1, 2, 4)
+        for t, s in groups[:8]:
+            h_pass(t, s, 1)
+            h_copy(t, s)
+        for t, s in groups[8:]:
+            h_pass(t, s, 0)
+            h_pass(t, s, 1)
+            h_copy(t, s)
+
+        WIDE = 2 * CHUNK
+        a_wide = keep.tile([P, PACK, WIDE], F32, name="a_wide")
+        work = keep.tile([P, PACK, WIDE], F32, name="work")
+        th_sb = keep.tile([P, PACK, NP], F32, name="th_sb")
+        z_planes = keep.tile([P, PACK, NP], BF16, name="z_planes")
+        z_bf = keep.tile([P, NP, PACK], BF16, name="z_bf", align_bytes=64)
+        z_codes = keep.tile([P, NP], U32, name="z_codes", align_bytes=64)
+        z_scales = keep.tile([P, NP], U8, name="z_scales", align_bytes=64)
+        o_sb = keep.tile([P, PACK, NP], F32, name="o_sb")
+        out_v = out.rearrange("(p t) j -> p t j", t=PACK)
+
+        def a_of(t0, t1, j0, j1):
+            if j0 < WIDE:
+                return a_wide[:, t0:t1, j0:j1]
+            return work[:, t0:t1, j0 - WIDE : j1 - WIDE]
+
+        def b_of(t0, t1, j0, j1):
+            if j0 < WIDE:
+                return work[:, t0:t1, j0:j1]
+            return work[:, t0:t1, j0 - CHUNK : j1 - CHUNK]
+
+        def flat(ap):
+            return ap.rearrange("p t n -> p (t n)")
+
+        def pick(t, j0, j1):
+            nc.vector.tensor_copy(flat(a_of(t, t + 1, j0, j1)), h[t][:].indirect(pos1_sb[:, j0 // 16 : j1 // 16]))
+            nc.vector.tensor_copy(flat(b_of(t, t + 1, j0, j1)), h[t][:].indirect(pos2_sb[:, j0 // 16 : j1 // 16]))
+
+        def error(t, j0, j1, sub_eng, gain_on_scalar):
+            d = flat(b_of(t, t + 1, j0, j1))
+            sub_eng.tensor_tensor(d, flat(a_of(t, t + 1, j0, j1)), d, ALU.subtract)
+            nc.scalar.activation(th_sb[:, t, j0:j1], d, ACT.Tanh)
+            if gain_on_scalar:
+                nc.scalar.activation(
+                    z_planes[:, t, j0:j1], th_sb[:, t, j0:j1], ACT.Copy, scale=gain_sb[:, t : t + 1]
+                )
+            else:
+                nc.gpsimd.tensor_scalar(
+                    z_planes[:, t, j0:j1], th_sb[:, t, j0:j1], gain_sb[:, t : t + 1], 0.0, ALU.mult, ALU.add
+                )
+
+        def interleave(j0, j1, on_vector):
+            dst = z_bf[:, j0:j1, :].rearrange("p (c i) t -> p c t i", i=4)
+            src = z_planes[:, :, j0:j1].rearrange("p t (c i) -> p c t i", i=4)
+            if on_vector:
+                nc.vector.tensor_copy(dst, src)
+            else:
+                nc.scalar.copy(dst, src)
+
+        def quant_z(j0, j1):
+            nc.vector.quantize_mx(
+                out=z_codes[:, j0:j1].bitcast(FP8X4),
+                scales=z_scales[:, j0:j1],
+                in_=z_bf[:, j0:j1, :].rearrange("p n t -> p (n t)"),
+            )
+
+        ybanks = {}
+
+        def correct(c):
+            cols = slice(c * CHUNK, (c + 1) * CHUNK)
+            for u in range(2):
+                ybanks[(c, u)] = psum.tile([P, 2, CHUNK], F32, name="bank%d" % ((4 + 2 * c + u) % 8))
+                for v in range(2):
+                    t = 2 * u + v
+                    nc.tensor.matmul_mx(
+                        out=ybanks[(c, u)][:, v, :],
+                        lhsT=w2_codes[:, t, :].bitcast(FP4X4),
+                        lhsT_scale=w2_sc[:, t, :],
+                        rhs=z_codes[:, cols].bitcast(FP8X4),
+                        rhs_scale=z_scales[:, cols],
+                        start=True,
+                        stop=True,
+                    )
+
+        def finish(c, u):
+            j0, j1 = c * CHUNK, (c + 1) * CHUNK
+            nc.vector.tensor_tensor(
+                o_sb[:, 2 * u : 2 * u + 2, j0:j1], ybanks[(c, u)][:], a_of(2 * u, 2 * u + 2, j0, j1), ALU.add
+            )
+            nc.sync.dma_start(out=out_v[:, 2 * u : 2 * u + 2, j0:j1], in_=o_sb[:, 2 * u : 2 * u + 2, j0:j1])
+
+        for t in range(PACK - 1):
+            pick(t, 0, WIDE)
+            error(t, 0, WIDE, nc.gpsimd, True)
+        pick(3, 0, CHUNK)
+        error(3, 0, CHUNK, nc.gpsimd, False)
+        pick(3, CHUNK, WIDE)
+        error(3, CHUNK, WIDE, nc.gpsimd, False)
+        interleave(0, CHUNK, False)
+        pick(0, WIDE, NP)
+        error(0, WIDE, NP, nc.gpsimd, False)
+        interleave(CHUNK, WIDE, False)
+        pick(1, WIDE, NP)
+        error(1, WIDE, NP, nc.gpsimd, False)
+        quant_z(0, CHUNK)
+        correct(0)
+        pick(2, WIDE, NP)
+        error(2, WIDE, NP, nc.gpsimd, False)
+        pick(3, WIDE, NP)
+        error(3, WIDE, NP, nc.vector, True)
+        quant_z(CHUNK, WIDE)
+        correct(1)
+        finish(0, 0)
+        finish(0, 1)
+        interleave(WIDE, NP, True)
+        finish(1, 0)
+        quant_z(WIDE, NP)
+        correct(2)
+        finish(1, 1)
+        finish(2, 0)
+        finish(2, 1)

@@ -1,6 +1,7 @@
 from contextlib import ExitStack
 
 import concourse.mybir as mybir
+from concourse.masks import make_identity
 
 K, T, S, NP, H = 1024, 4096, 1536, 768, 512
 FLOPS = 2 * K * H * S + 2 * H * H * NP
@@ -63,6 +64,8 @@ def tile_list_pairwise_state_correction_kernel(
                 out=w1_raw[a][:, :, c0:c1], in_=rows.rearrange("(p j) c -> p j c", j=PACK)
             )
 
+        ident = keep.tile([P, P], F32, name="ident")
+        minus = keep.tile([P, 2 * CHUNK], F32, name="minus")
         nc.sync.dma_start(offs_sb[:], offs)
         nc.sync.dma_start(out=w2_raw[:], in_=w2_words[0].bitcast(I32))
         load_words(0)
@@ -79,17 +82,23 @@ def tile_list_pairwise_state_correction_kernel(
         nc.sync.dma_start(pos2_sb[:], pos2)
         nc.sync.dma_start(out=gain_sb[:], in_=gain.rearrange("(p t) -> p t", t=PACK))
         for q in range(4):
-            nc.gpsimd.dma_start(
+            nc.sync.dma_start(
                 out=w2s_raw[32 * q : 32 * q + 4, :],
                 in_=w2_scales[0, 4 * q : 4 * q + 4, :].bitcast(I32),
             )
 
+        nc.vector.memset(ident[:], 0.0)
+        make_identity(nc, ident[:], nomemset=True)
+        nc.vector.memset(minus[:], -1.0)
         g_words = [
             keep.tile([P, S], U32, name="g_words0", align_bytes=64),
             reuse.tile([P, S], U32, name="g_words1", align_bytes=64, offset=4 * H),
         ]
         g_scale = keep.tile([P, S], U8, name="g_scale", align_bytes=64)
-        w1_bf = [keep.tile([P, PACK, P, PACK], BF16, name="w1_bf%d" % a, align_bytes=64) for a in range(PASSES)]
+        w1_bf = [
+            keep.tile([P, PACK, P, PACK], BF16, name="w1_bf0", align_bytes=64),
+            reuse.tile([P, PACK, P, PACK], BF16, name="w1_bf1", align_bytes=64, offset=8192),
+        ]
         w1_codes = [
             keep.tile([P, H], U32, name="w1_codes0", align_bytes=64),
             reuse.tile([P, H], U32, name="w1_codes1", align_bytes=64, offset=0),
@@ -136,10 +145,13 @@ def tile_list_pairwise_state_correction_kernel(
         h = [keep.tile([P, S], F32, name="h%d" % t) for t in range(PACK)]
 
         def h_copy(t, s):
-            nc.scalar.copy(h[t][:, s * BANK : (s + 1) * BANK], banks[(t, s)][:])
+            if (t, s) == (0, 1):
+                nc.vector.tensor_copy(h[t][:, s * BANK : (s + 1) * BANK], banks[(t, s)][:])
+            else:
+                nc.scalar.copy(h[t][:, s * BANK : (s + 1) * BANK], banks[(t, s)][:])
 
         w2_codes = keep.tile([P, PACK, 2 * P], U8, name="w2_codes", align_bytes=64)
-        w2_sc = keep.tile([P, PACK, P], U8, name="w2_sc", align_bytes=64)
+        w2_sc = reuse.tile([P, PACK, P], U8, name="w2_sc", align_bytes=64, offset=8192 + 3584)
         nc.vector.tensor_copy(
             w2_codes[:].rearrange("p t (m b) -> p t m b", b=2),
             w2_raw[:].bitcast(U8).rearrange("p (m t b) -> p t m b", t=PACK, b=2),
@@ -149,9 +161,6 @@ def tile_list_pairwise_state_correction_kernel(
         cast_w1(0, 0, 2, 0, P)
         cast_w1(0, 2, 4, 0, P)
         quant_w1(0, 0, 4)
-        nc.vector.tensor_copy(
-            w2_sc[:], w2s_raw[:].bitcast(U8).rearrange("p (m t) -> p t m", t=PACK)
-        )
         for t, s in groups[:8]:
             h_pass(t, s, 0)
         cast_w1(1, 0, 4, 0, P // 2)
@@ -162,6 +171,9 @@ def tile_list_pairwise_state_correction_kernel(
         gather_words(1, 2 * BANK, S)
         quant_w1(1, 0, 2)
         quant_w1(1, 2, 4)
+        nc.vector.tensor_copy(
+            w2_sc[:], w2s_raw[:].bitcast(U8).rearrange("p (m t) -> p t m", t=PACK)
+        )
         for t, s in groups[:8]:
             h_pass(t, s, 1)
             h_copy(t, s)
@@ -172,10 +184,16 @@ def tile_list_pairwise_state_correction_kernel(
 
         WIDE = 2 * CHUNK
         a_wide = keep.tile([P, PACK, WIDE], F32, name="a_wide")
-        work = keep.tile([P, PACK, WIDE], F32, name="work")
-        th_sb = keep.tile([P, PACK, NP], F32, name="th_sb")
+        b_wide = keep.tile([P, PACK, WIDE], F32, name="b_wide")
+        ring = keep.tile([P, PACK + 1, WIDE], F32, name="ring")
+        th_last = keep.tile([P, PACK, CHUNK], F32, name="th_last")
         z_planes = keep.tile([P, PACK, NP], BF16, name="z_planes")
-        z_bf = keep.tile([P, NP, PACK], BF16, name="z_bf", align_bytes=64)
+        z_bf = [
+            reuse.tile([P, CHUNK, PACK], BF16, name="z_bf0", align_bytes=64, offset=12288),
+            keep.tile([P, CHUNK, PACK], BF16, name="z_bf1", align_bytes=64),
+            keep.tile([P, CHUNK, PACK], BF16, name="z_bf2", align_bytes=64),
+        ]
+        b_end = reuse.tile([P, 1, CHUNK], F32, name="b_end", align_bytes=64, offset=12288)
         z_codes = keep.tile([P, NP], U32, name="z_codes", align_bytes=64)
         z_scales = keep.tile([P, NP], U8, name="z_scales", align_bytes=64)
         o_sb = keep.tile([P, PACK, NP], F32, name="o_sb")
@@ -184,35 +202,64 @@ def tile_list_pairwise_state_correction_kernel(
         def a_of(t0, t1, j0, j1):
             if j0 < WIDE:
                 return a_wide[:, t0:t1, j0:j1]
-            return work[:, t0:t1, j0 - WIDE : j1 - WIDE]
+            return ring[:, t0 + 1 : t1 + 1, j0 - WIDE : j1 - WIDE]
 
         def b_of(t0, t1, j0, j1):
             if j0 < WIDE:
-                return work[:, t0:t1, j0:j1]
-            return work[:, t0:t1, j0 - CHUNK : j1 - CHUNK]
+                return b_wide[:, t0:t1, j0:j1]
+            if t0 == PACK - 1:
+                return b_end[:]
+            return ring[:, t0 + 1 : t1 + 1, j0 - CHUNK : j1 - CHUNK]
+
+        def th_of(t, j0, j1):
+            if j0 < WIDE:
+                return ring[:, t, j0:j1]
+            return th_last[:, t, j0 - WIDE : j1 - WIDE]
+
+        def z_of(j0, j1):
+            base = j0 // CHUNK * CHUNK
+            return z_bf[j0 // CHUNK][:, j0 - base : j1 - base, :]
 
         def flat(ap):
             return ap.rearrange("p t n -> p (t n)")
 
-        def pick(t, j0, j1):
+        def pick(t, j0, j1, negate):
             nc.vector.tensor_copy(flat(a_of(t, t + 1, j0, j1)), h[t][:].indirect(pos1_sb[:, j0 // 16 : j1 // 16]))
-            nc.vector.tensor_copy(flat(b_of(t, t + 1, j0, j1)), h[t][:].indirect(pos2_sb[:, j0 // 16 : j1 // 16]))
-
-        def error(t, j0, j1, sub_eng, gain_on_scalar):
-            d = flat(b_of(t, t + 1, j0, j1))
-            sub_eng.tensor_tensor(d, flat(a_of(t, t + 1, j0, j1)), d, ALU.subtract)
-            nc.scalar.activation(th_sb[:, t, j0:j1], d, ACT.Tanh)
-            if gain_on_scalar:
-                nc.scalar.activation(
-                    z_planes[:, t, j0:j1], th_sb[:, t, j0:j1], ACT.Copy, scale=gain_sb[:, t : t + 1]
-                )
+            window = h[t][:].indirect(pos2_sb[:, j0 // 16 : j1 // 16])
+            if negate:
+                nc.vector.tensor_tensor(flat(b_of(t, t + 1, j0, j1)), window, minus[:, 0 : j1 - j0], ALU.mult)
             else:
-                nc.gpsimd.tensor_scalar(
-                    z_planes[:, t, j0:j1], th_sb[:, t, j0:j1], gain_sb[:, t : t + 1], 0.0, ALU.mult, ALU.add
-                )
+                nc.vector.tensor_copy(flat(b_of(t, t + 1, j0, j1)), window)
+
+        def error_v(t, j0, j1):
+            d = flat(b_of(t, t + 1, j0, j1))
+            nc.vector.tensor_tensor(d, flat(a_of(t, t + 1, j0, j1)), d, ALU.subtract)
+            nc.scalar.activation(th_of(t, j0, j1), d, ACT.Tanh)
+            nc.scalar.activation(
+                z_planes[:, t, j0:j1], th_of(t, j0, j1), ACT.Copy, scale=gain_sb[:, t : t + 1]
+            )
+
+        turns = []
+
+        def error_pe(t, j0, j1):
+            n = len(turns)
+            turns.append(t)
+            width = j1 - j0
+            a_t = flat(a_of(t, t + 1, j0, j1))
+            nb_t = flat(b_of(t, t + 1, j0, j1))
+            dT = psum.tile([P, width], F32, name="bank%d" % (4 + n % 2))
+            for c0 in range(0, width, P):
+                blk = slice(c0, c0 + P)
+                nc.tensor.matmul(dT[:, blk], a_t[:, blk], ident[:], start=True, stop=False, is_transpose=True)
+                nc.tensor.matmul(dT[:, blk], nb_t[:, blk], ident[:], start=False, stop=True, is_transpose=True)
+            nc.scalar.activation(th_of(t, j0, j1), dT[:], ACT.Tanh)
+            back = psum.tile([P, width], F32, name="bank%d" % (6 + n % 2))
+            for c0 in range(0, width, P):
+                nc.tensor.transpose(back[:, c0 : c0 + P], th_of(t, j0 + c0, j0 + c0 + P), ident[:])
+            nc.scalar.activation(z_planes[:, t, j0:j1], back[:], ACT.Copy, scale=gain_sb[:, t : t + 1])
 
         def interleave(j0, j1, on_vector):
-            dst = z_bf[:, j0:j1, :].rearrange("p (c i) t -> p c t i", i=4)
+            dst = z_of(j0, j1).rearrange("p (c i) t -> p c t i", i=4)
             src = z_planes[:, :, j0:j1].rearrange("p t (c i) -> p c t i", i=4)
             if on_vector:
                 nc.vector.tensor_copy(dst, src)
@@ -223,61 +270,61 @@ def tile_list_pairwise_state_correction_kernel(
             nc.vector.quantize_mx(
                 out=z_codes[:, j0:j1].bitcast(FP8X4),
                 scales=z_scales[:, j0:j1],
-                in_=z_bf[:, j0:j1, :].rearrange("p n t -> p (n t)"),
+                in_=z_of(j0, j1).rearrange("p n t -> p (n t)"),
             )
 
         ybanks = {}
 
-        def correct(c):
-            cols = slice(c * CHUNK, (c + 1) * CHUNK)
-            for u in range(2):
-                ybanks[(c, u)] = psum.tile([P, 2, CHUNK], F32, name="bank%d" % ((4 + 2 * c + u) % 8))
-                for v in range(2):
-                    t = 2 * u + v
-                    nc.tensor.matmul_mx(
-                        out=ybanks[(c, u)][:, v, :],
-                        lhsT=w2_codes[:, t, :].bitcast(FP4X4),
-                        lhsT_scale=w2_sc[:, t, :],
-                        rhs=z_codes[:, cols].bitcast(FP8X4),
-                        rhs_scale=z_scales[:, cols],
-                        start=True,
-                        stop=True,
-                    )
+        def correct(j0, j1, t0, t1, bank):
+            ybanks[(j0, t0)] = psum.tile([P, t1 - t0, j1 - j0], F32, name="bank%d" % bank)
+            for t in range(t0, t1):
+                nc.tensor.matmul_mx(
+                    out=ybanks[(j0, t0)][:, t - t0, :],
+                    lhsT=w2_codes[:, t, :].bitcast(FP4X4),
+                    lhsT_scale=w2_sc[:, t, :],
+                    rhs=z_codes[:, j0:j1].bitcast(FP8X4),
+                    rhs_scale=z_scales[:, j0:j1],
+                    start=True,
+                    stop=True,
+                )
 
-        def finish(c, u):
-            j0, j1 = c * CHUNK, (c + 1) * CHUNK
-            nc.vector.tensor_tensor(
-                o_sb[:, 2 * u : 2 * u + 2, j0:j1], ybanks[(c, u)][:], a_of(2 * u, 2 * u + 2, j0, j1), ALU.add
-            )
-            nc.sync.dma_start(out=out_v[:, 2 * u : 2 * u + 2, j0:j1], in_=o_sb[:, 2 * u : 2 * u + 2, j0:j1])
+        def finish(j0, j1, t0, t1):
+            nc.vector.tensor_tensor(o_sb[:, t0:t1, j0:j1], ybanks[(j0, t0)][:], a_of(t0, t1, j0, j1), ALU.add)
+            nc.sync.dma_start(out=out_v[:, t0:t1, j0:j1], in_=o_sb[:, t0:t1, j0:j1])
 
         for t in range(PACK - 1):
-            pick(t, 0, WIDE)
-            error(t, 0, WIDE, nc.gpsimd, True)
-        pick(3, 0, CHUNK)
-        error(3, 0, CHUNK, nc.gpsimd, False)
-        pick(3, CHUNK, WIDE)
-        error(3, CHUNK, WIDE, nc.gpsimd, False)
+            pick(t, 0, WIDE, True)
+            error_pe(t, 0, WIDE)
+        pick(3, 0, CHUNK, True)
+        error_pe(3, 0, CHUNK)
+        pick(3, CHUNK, WIDE, True)
+        error_pe(3, CHUNK, WIDE)
         interleave(0, CHUNK, False)
-        pick(0, WIDE, NP)
-        error(0, WIDE, NP, nc.gpsimd, False)
+        pick(0, WIDE, NP, True)
+        error_pe(0, WIDE, NP)
         interleave(CHUNK, WIDE, False)
-        pick(1, WIDE, NP)
-        error(1, WIDE, NP, nc.gpsimd, False)
+        pick(1, WIDE, NP, True)
+        error_pe(1, WIDE, NP)
         quant_z(0, CHUNK)
-        correct(0)
-        pick(2, WIDE, NP)
-        error(2, WIDE, NP, nc.gpsimd, False)
-        pick(3, WIDE, NP)
-        error(3, WIDE, NP, nc.vector, True)
+        correct(0, CHUNK, 0, 2, 0)
+        correct(0, CHUNK, 2, 4, 1)
+        pick(2, WIDE, NP, True)
+        error_pe(2, WIDE, NP)
+        pick(3, WIDE, NP, False)
+        error_v(3, WIDE, NP)
+        finish(0, CHUNK, 0, 2)
+        finish(0, CHUNK, 2, 4)
         quant_z(CHUNK, WIDE)
-        correct(1)
-        finish(0, 0)
-        finish(0, 1)
-        interleave(WIDE, NP, True)
-        finish(1, 0)
-        quant_z(WIDE, NP)
-        correct(2)
-        finish(1, 1)
-        finish(2, 0)
-        finish(2, 1)
+        correct(CHUNK, WIDE, 0, 2, 2)
+        correct(CHUNK, WIDE, 2, 4, 3)
+        finish(CHUNK, WIDE, 0, 2)
+        HALF = WIDE + P
+        interleave(WIDE, HALF, True)
+        interleave(HALF, NP, True)
+        quant_z(WIDE, HALF)
+        correct(WIDE, HALF, 0, 4, 0)
+        quant_z(HALF, NP)
+        correct(HALF, NP, 0, 4, 1)
+        finish(CHUNK, WIDE, 2, 4)
+        finish(WIDE, HALF, 0, 4)
+        finish(HALF, NP, 0, 4)

@@ -1,7 +1,6 @@
 from contextlib import ExitStack
 
 import concourse.mybir as mybir
-from concourse.masks import make_identity
 
 K, T, S, NP, H = 1024, 4096, 1536, 768, 512
 FLOPS = 2 * K * H * S + 2 * H * H * NP
@@ -33,25 +32,30 @@ def tile_list_pairwise_state_correction_kernel(
         lists = ctx.enter_context(tc.tile_pool(name="lists", bufs=1))
         keep = ctx.enter_context(tc.tile_pool(name="keep", bufs=1))
         reuse = ctx.enter_context(tc.tile_pool(name="reuse", bufs=1))
+        late = ctx.enter_context(tc.tile_pool(name="late", bufs=1))
         psum = ctx.enter_context(tc.psum_pool(name="psum", bufs=1))
 
         offs_sb = lists.tile([P, S // 16], U16, name="offs_sb")
         pos1_sb = lists.tile([P, NP // 16], U16, name="pos1_sb")
         pos2_sb = lists.tile([P, NP // 16], U16, name="pos2_sb")
 
-        words = [keep.tile([P, T], I32, name="words%d" % a, align_bytes=64) for a in range(PASSES)]
+        warm = late.tile([P, 48], F32, name="warm", offset=960)
+        warm_out = late.tile([P, 48], F32, name="warm_out", offset=17888)
         tscale = reuse.tile([P, T // 4], I32, name="tscale", align_bytes=64, offset=0)
-        w1_raw = [keep.tile([P, PACK, H], F32, name="w1_raw%d" % a) for a in range(PASSES)]
-        gain_sb = keep.tile([P, PACK], F32, name="gain_sb")
-        w2_raw = keep.tile([P, 2 * H // 4], I32, name="w2_raw")
-        w2s_raw = keep.tile([P, H // 4], I32, name="w2s_raw")
-        warm = keep.tile([P, 8], F32, name="warm")
-        warm_out = keep.tile([P, 8], F32, name="warm_out")
-
         nc.vector.memset(tscale[:], 0)
-        nc.vector.memset(w2s_raw[:], 0)
         nc.vector.memset(warm[:], 0.0)
         nc.scalar.activation(warm_out[:], warm[:], ACT.Tanh)
+
+        words = [
+            keep.tile([P, T], I32, name="words0", align_bytes=64),
+            late.tile([P, T], I32, name="words1", offset=17984),
+        ]
+        w1_all = late.tile([P, PASSES, PACK, H], F32, name="w1_all", offset=1088)
+        w1_raw = [w1_all[:, a, :, :] for a in range(PASSES)]
+        gain_sb = late.tile([P, PACK], F32, name="gain_sb", offset=1024)
+        w2_raw = late.tile([P, 2 * H // 4], I32, name="w2_raw", offset=0)
+        w2s_raw = late.tile([P, H // 4], I32, name="w2s_raw", offset=17472)
+        nc.vector.memset(w2s_raw[:], 0)
 
         def load_words(a):
             nc.sync.dma_start(
@@ -64,13 +68,18 @@ def tile_list_pairwise_state_correction_kernel(
                 out=w1_raw[a][:, :, c0:c1], in_=rows.rearrange("(p j) c -> p j c", j=PACK)
             )
 
-        ident = keep.tile([P, P], F32, name="ident")
-        minus = keep.tile([P, 2 * CHUNK], F32, name="minus")
         nc.sync.dma_start(offs_sb[:], offs)
-        nc.sync.dma_start(out=w2_raw[:], in_=w2_words[0].bitcast(I32))
+        nc.sync.dma_start(pos1_sb[:], pos1)
+        nc.sync.dma_start(pos2_sb[:], pos2)
         load_words(0)
-        for q in range(4):
-            nc.gpsimd.dma_start(
+        for q in range(2):
+            for a in range(PASSES):
+                nc.sync.dma_start(
+                    out=tscale[32 * q + 4 * a : 32 * q + 4 * a + 4, :],
+                    in_=tab_scales[a, 4 * q : 4 * q + 4, :].bitcast(I32),
+                )
+        for q in range(2, 4):
+            nc.sync.dma_start(
                 out=tscale[32 * q : 32 * q + 4 * PASSES, :],
                 in_=tab_scales[:, 4 * q : 4 * q + 4, :].bitcast(I32),
             )
@@ -78,8 +87,7 @@ def tile_list_pairwise_state_correction_kernel(
         load_words(1)
         load_w1(1, 0, H // 2)
         load_w1(1, H // 2, H)
-        nc.sync.dma_start(pos1_sb[:], pos1)
-        nc.sync.dma_start(pos2_sb[:], pos2)
+        nc.sync.dma_start(out=w2_raw[:], in_=w2_words[0].bitcast(I32))
         nc.sync.dma_start(out=gain_sb[:], in_=gain.rearrange("(p t) -> p t", t=PACK))
         for q in range(4):
             nc.sync.dma_start(
@@ -87,41 +95,51 @@ def tile_list_pairwise_state_correction_kernel(
                 in_=w2_scales[0, 4 * q : 4 * q + 4, :].bitcast(I32),
             )
 
-        nc.vector.memset(ident[:], 0.0)
-        make_identity(nc, ident[:], nomemset=True)
-        nc.vector.memset(minus[:], -1.0)
-        g_words = [
-            keep.tile([P, S], U32, name="g_words0", align_bytes=64),
-            reuse.tile([P, S], U32, name="g_words1", align_bytes=64, offset=4 * H),
+        g_first = keep.tile([P, S], U32, name="g_first", align_bytes=64)
+        g_second = reuse.tile([P, 2 * BANK], U32, name="g_second", align_bytes=64, offset=4 * H)
+        w1_bf0 = keep.tile([P, PACK, P, PACK], BF16, name="w1_bf0", align_bytes=64)
+        w1_bf1 = [
+            reuse.tile([P, 2, P, PACK], BF16, name="w1_bf1_%d" % u, align_bytes=64, offset=8192 + 2048 * u)
+            for u in range(2)
         ]
+        g_tail = reuse.tile([P, BANK], U32, name="g_tail", align_bytes=64, offset=0)
         g_scale = keep.tile([P, S], U8, name="g_scale", align_bytes=64)
-        w1_bf = [
-            keep.tile([P, PACK, P, PACK], BF16, name="w1_bf0", align_bytes=64),
-            reuse.tile([P, PACK, P, PACK], BF16, name="w1_bf1", align_bytes=64, offset=8192),
-        ]
+
+        def g_words(a, s0, s1):
+            if a == 0:
+                return g_first[:, s0:s1]
+            if s0 < 2 * BANK:
+                return g_second[:, s0:s1]
+            return g_tail[:]
+
+        def w1_bf(a, t0, t1):
+            if a == 0:
+                return w1_bf0[:, t0:t1, :, :]
+            return w1_bf1[t0 // 2][:]
+
         w1_codes = [
             keep.tile([P, H], U32, name="w1_codes0", align_bytes=64),
-            reuse.tile([P, H], U32, name="w1_codes1", align_bytes=64, offset=0),
+            reuse.tile([P, H], U32, name="w1_codes1", align_bytes=64, offset=16384),
         ]
         w1_scales = keep.tile([P, PASSES, H], U8, name="w1_scales", align_bytes=64)
 
         def gather_words(a, s0, s1):
             nc.vector.tensor_copy(
-                g_words[a][:, s0:s1],
+                g_words(a, s0, s1),
                 words[a][:].bitcast(U32).indirect(offs_sb[:, s0 // 16 : s1 // 16]),
             )
 
-        def cast_w1(a, t0, t1, m0, m1):
-            nc.scalar.copy(
-                w1_bf[a][:, t0:t1, m0:m1, :].rearrange("p t m j -> p m t j"),
-                w1_raw[a][:].rearrange("p j (m t) -> p m t j", t=PACK)[:, m0:m1, t0:t1, :],
+        def cast_w1(a, t0, t1, m0, m1, on_vector=False):
+            (nc.vector.tensor_copy if on_vector else nc.scalar.copy)(
+                w1_bf(a, t0, t1)[:, :, m0:m1, :].rearrange("p t m j -> p m t j"),
+                w1_raw[a].rearrange("p j (m t) -> p m t j", t=PACK)[:, m0:m1, t0:t1, :],
             )
 
         def quant_w1(a, t0, t1):
             nc.vector.quantize_mx(
                 out=w1_codes[a][:, t0 * P : t1 * P].bitcast(FP8X4),
                 scales=w1_scales[:, a, t0 * P : t1 * P],
-                in_=w1_bf[a][:, t0:t1, :, :].rearrange("p t m j -> p (t m j)"),
+                in_=w1_bf(a, t0, t1).rearrange("p t m j -> p (t m j)"),
             )
 
         groups = [(t, s) for t in range(PACK) for s in range(SLICES)]
@@ -136,7 +154,7 @@ def tile_list_pairwise_state_correction_kernel(
                 out=banks[(t, s)][:],
                 lhsT=w1_codes[a][:, t * P : (t + 1) * P].bitcast(FP8X4),
                 lhsT_scale=w1_scales[:, a, t * P : (t + 1) * P],
-                rhs=g_words[a][:, cols].bitcast(FP8X4),
+                rhs=g_words(a, s * BANK, (s + 1) * BANK).bitcast(FP8X4),
                 rhs_scale=g_scale[4 * a :, cols],
                 start=(a == 0),
                 stop=(a == PASSES - 1),
@@ -145,31 +163,32 @@ def tile_list_pairwise_state_correction_kernel(
         h = [keep.tile([P, S], F32, name="h%d" % t) for t in range(PACK)]
 
         def h_copy(t, s):
-            if (t, s) == (0, 1):
+            if (t, s) in [(0, 1)]:
                 nc.vector.tensor_copy(h[t][:, s * BANK : (s + 1) * BANK], banks[(t, s)][:])
             else:
                 nc.scalar.copy(h[t][:, s * BANK : (s + 1) * BANK], banks[(t, s)][:])
 
-        w2_codes = keep.tile([P, PACK, 2 * P], U8, name="w2_codes", align_bytes=64)
-        w2_sc = reuse.tile([P, PACK, P], U8, name="w2_sc", align_bytes=64, offset=8192 + 3584)
-        nc.vector.tensor_copy(
-            w2_codes[:].rearrange("p t (m b) -> p t m b", b=2),
-            w2_raw[:].bitcast(U8).rearrange("p (m t b) -> p t m b", t=PACK, b=2),
-        )
-        nc.vector.tensor_copy(g_scale[:], tscale[:].bitcast(U8).indirect(offs_sb[:]))
+        w2_codes = reuse.tile([P, PACK, 2 * P], U8, name="w2_codes", align_bytes=64, offset=8192)
+        w2_sc = reuse.tile([P, PACK, P], U8, name="w2_sc", align_bytes=64, offset=8192 + 1024)
         gather_words(0, 0, S)
+        nc.vector.tensor_copy(g_scale[:], tscale[:].bitcast(U8).indirect(offs_sb[:]))
         cast_w1(0, 0, 2, 0, P)
         cast_w1(0, 2, 4, 0, P)
         quant_w1(0, 0, 4)
         for t, s in groups[:8]:
             h_pass(t, s, 0)
-        cast_w1(1, 0, 4, 0, P // 2)
+        cast_w1(1, 0, 2, 0, P // 2)
+        cast_w1(1, 2, 4, 0, P // 2)
         cast_w1(1, 0, 2, P // 2, P)
         cast_w1(1, 2, 4, P // 2, P)
         gather_words(1, 0, BANK)
         gather_words(1, BANK, 2 * BANK)
         gather_words(1, 2 * BANK, S)
         quant_w1(1, 0, 2)
+        nc.vector.tensor_copy(
+            w2_codes[:].rearrange("p t (m b) -> p t m b", b=2),
+            w2_raw[:].bitcast(U8).rearrange("p (m t b) -> p t m b", t=PACK, b=2),
+        )
         quant_w1(1, 2, 4)
         nc.vector.tensor_copy(
             w2_sc[:], w2s_raw[:].bitcast(U8).rearrange("p (m t) -> p t m", t=PACK)
@@ -190,13 +209,15 @@ def tile_list_pairwise_state_correction_kernel(
         z_planes = keep.tile([P, PACK, NP], BF16, name="z_planes")
         z_bf = [
             reuse.tile([P, CHUNK, PACK], BF16, name="z_bf0", align_bytes=64, offset=12288),
-            keep.tile([P, CHUNK, PACK], BF16, name="z_bf1", align_bytes=64),
-            keep.tile([P, CHUNK, PACK], BF16, name="z_bf2", align_bytes=64),
+            reuse.tile([P, CHUNK, PACK], BF16, name="z_bf1", align_bytes=64, offset=18432),
+            reuse.tile([P, CHUNK, PACK], BF16, name="z_bf2", align_bytes=64, offset=14336),
         ]
         b_end = reuse.tile([P, 1, CHUNK], F32, name="b_end", align_bytes=64, offset=12288)
         z_codes = keep.tile([P, NP], U32, name="z_codes", align_bytes=64)
         z_scales = keep.tile([P, NP], U8, name="z_scales", align_bytes=64)
         o_sb = keep.tile([P, PACK, NP], F32, name="o_sb")
+        o_late = reuse.tile([P, 2, CHUNK], F32, name="o_late", align_bytes=64, offset=14336)
+        o_mid = reuse.tile([P, 2, CHUNK], F32, name="o_mid", align_bytes=64, offset=18432)
         out_v = out.rearrange("(p t) j -> p t j", t=PACK)
 
         def a_of(t0, t1, j0, j1):
@@ -209,11 +230,15 @@ def tile_list_pairwise_state_correction_kernel(
                 return b_wide[:, t0:t1, j0:j1]
             if t0 == PACK - 1:
                 return b_end[:]
+            if t0 == PACK - 2:
+                return b_wide[:, PACK - 1 : PACK, 0:CHUNK]
             return ring[:, t0 + 1 : t1 + 1, j0 - CHUNK : j1 - CHUNK]
 
         def th_of(t, j0, j1):
             if j0 < WIDE:
                 return ring[:, t, j0:j1]
+            if t == PACK - 1:
+                return b_wide[:, t, 0:CHUNK]
             return th_last[:, t, j0 - WIDE : j1 - WIDE]
 
         def z_of(j0, j1):
@@ -223,40 +248,27 @@ def tile_list_pairwise_state_correction_kernel(
         def flat(ap):
             return ap.rearrange("p t n -> p (t n)")
 
-        def pick(t, j0, j1, negate):
+        def pick(t, j0, j1):
             nc.vector.tensor_copy(flat(a_of(t, t + 1, j0, j1)), h[t][:].indirect(pos1_sb[:, j0 // 16 : j1 // 16]))
-            window = h[t][:].indirect(pos2_sb[:, j0 // 16 : j1 // 16])
-            if negate:
-                nc.vector.tensor_tensor(flat(b_of(t, t + 1, j0, j1)), window, minus[:, 0 : j1 - j0], ALU.mult)
-            else:
-                nc.vector.tensor_copy(flat(b_of(t, t + 1, j0, j1)), window)
+            nc.vector.tensor_copy(flat(b_of(t, t + 1, j0, j1)), h[t][:].indirect(pos2_sb[:, j0 // 16 : j1 // 16]))
 
-        def error_v(t, j0, j1):
-            d = flat(b_of(t, t + 1, j0, j1))
-            nc.vector.tensor_tensor(d, flat(a_of(t, t + 1, j0, j1)), d, ALU.subtract)
+        def d_of(t, j0, j1):
+            return flat(b_of(t, t + 1, j0, j1))
+
+        def squash(t, j0, j1, sub_engine):
+            d = d_of(t, j0, j1)
+            sub_engine.tensor_tensor(d, flat(a_of(t, t + 1, j0, j1)), flat(b_of(t, t + 1, j0, j1)), ALU.subtract)
             nc.scalar.activation(th_of(t, j0, j1), d, ACT.Tanh)
-            nc.scalar.activation(
-                z_planes[:, t, j0:j1], th_of(t, j0, j1), ACT.Copy, scale=gain_sb[:, t : t + 1]
-            )
 
-        turns = []
-
-        def error_pe(t, j0, j1):
-            n = len(turns)
-            turns.append(t)
-            width = j1 - j0
-            a_t = flat(a_of(t, t + 1, j0, j1))
-            nb_t = flat(b_of(t, t + 1, j0, j1))
-            dT = psum.tile([P, width], F32, name="bank%d" % (4 + n % 2))
-            for c0 in range(0, width, P):
-                blk = slice(c0, c0 + P)
-                nc.tensor.matmul(dT[:, blk], a_t[:, blk], ident[:], start=True, stop=False, is_transpose=True)
-                nc.tensor.matmul(dT[:, blk], nb_t[:, blk], ident[:], start=False, stop=True, is_transpose=True)
-            nc.scalar.activation(th_of(t, j0, j1), dT[:], ACT.Tanh)
-            back = psum.tile([P, width], F32, name="bank%d" % (6 + n % 2))
-            for c0 in range(0, width, P):
-                nc.tensor.transpose(back[:, c0 : c0 + P], th_of(t, j0 + c0, j0 + c0 + P), ident[:])
-            nc.scalar.activation(z_planes[:, t, j0:j1], back[:], ACT.Copy, scale=gain_sb[:, t : t + 1])
+        def apply_gain(t, j0, j1, on_scalar):
+            if on_scalar:
+                nc.scalar.activation(
+                    z_planes[:, t, j0:j1], th_of(t, j0, j1), ACT.Copy, scale=gain_sb[:, t : t + 1]
+                )
+            else:
+                nc.gpsimd.tensor_scalar(
+                    z_planes[:, t, j0:j1], th_of(t, j0, j1), gain_sb[:, t : t + 1], 0.0, ALU.mult, ALU.add
+                )
 
         def interleave(j0, j1, on_vector):
             dst = z_of(j0, j1).rearrange("p (c i) t -> p c t i", i=4)
@@ -288,43 +300,57 @@ def tile_list_pairwise_state_correction_kernel(
                     stop=True,
                 )
 
-        def finish(j0, j1, t0, t1):
-            nc.vector.tensor_tensor(o_sb[:, t0:t1, j0:j1], ybanks[(j0, t0)][:], a_of(t0, t1, j0, j1), ALU.add)
-            nc.sync.dma_start(out=out_v[:, t0:t1, j0:j1], in_=o_sb[:, t0:t1, j0:j1])
+        def finish(j0, j1, t0, t1, unused=False):
+            dst = o_late[:] if (j0, t0) == (CHUNK, 2) else o_sb[:, t0:t1, j0:j1]
+            if (j0, t0) == (0, 2):
+                dst = o_mid[:]
+            nc.vector.tensor_tensor(dst, ybanks[(j0, t0)][:], a_of(t0, t1, j0, j1), ALU.add)
+            nc.sync.dma_start(out=out_v[:, t0:t1, j0:j1], in_=dst)
 
-        for t in range(PACK - 1):
-            pick(t, 0, WIDE, True)
-            error_pe(t, 0, WIDE)
-        pick(3, 0, CHUNK, True)
-        error_pe(3, 0, CHUNK)
-        pick(3, CHUNK, WIDE, True)
-        error_pe(3, CHUNK, WIDE)
+        HALF = WIDE + P
+        for t in range(2):
+            pick(t, 0, WIDE)
+            squash(t, 0, WIDE, nc.gpsimd)
+        apply_gain(0, 0, WIDE, True)
+        apply_gain(1, 0, WIDE, True)
+        pick(2, 0, WIDE)
+        squash(2, 0, WIDE, nc.gpsimd)
+        pick(3, 0, CHUNK)
+        squash(3, 0, CHUNK, nc.gpsimd)
+        apply_gain(2, 0, WIDE, True)
+        apply_gain(3, 0, CHUNK, True)
+        pick(3, CHUNK, WIDE)
+        squash(3, CHUNK, WIDE, nc.gpsimd)
         interleave(0, CHUNK, False)
-        pick(0, WIDE, NP, True)
-        error_pe(0, WIDE, NP)
+        apply_gain(3, CHUNK, WIDE, True)
+        pick(0, WIDE, NP)
+        squash(0, WIDE, NP, nc.gpsimd)
         interleave(CHUNK, WIDE, False)
-        pick(1, WIDE, NP, True)
-        error_pe(1, WIDE, NP)
+        apply_gain(0, WIDE, NP, True)
+        pick(1, WIDE, NP)
+        squash(1, WIDE, NP, nc.gpsimd)
         quant_z(0, CHUNK)
         correct(0, CHUNK, 0, 2, 0)
         correct(0, CHUNK, 2, 4, 1)
-        pick(2, WIDE, NP, True)
-        error_pe(2, WIDE, NP)
-        pick(3, WIDE, NP, False)
-        error_v(3, WIDE, NP)
-        finish(0, CHUNK, 0, 2)
-        finish(0, CHUNK, 2, 4)
+        apply_gain(1, WIDE, NP, True)
+        pick(2, WIDE, NP)
+        squash(2, WIDE, NP, nc.gpsimd)
+        pick(3, WIDE, NP)
+        squash(3, WIDE, NP, nc.vector)
+        apply_gain(2, WIDE, NP, True)
+        apply_gain(3, WIDE, NP, True)
         quant_z(CHUNK, WIDE)
         correct(CHUNK, WIDE, 0, 2, 2)
         correct(CHUNK, WIDE, 2, 4, 3)
-        finish(CHUNK, WIDE, 0, 2)
-        HALF = WIDE + P
+        finish(0, CHUNK, 0, 2, False)
+        finish(0, CHUNK, 2, 4, False)
+        finish(CHUNK, WIDE, 0, 2, False)
         interleave(WIDE, HALF, True)
         interleave(HALF, NP, True)
         quant_z(WIDE, HALF)
         correct(WIDE, HALF, 0, 4, 0)
         quant_z(HALF, NP)
         correct(HALF, NP, 0, 4, 1)
-        finish(CHUNK, WIDE, 2, 4)
+        finish(CHUNK, WIDE, 2, 4, False)
         finish(WIDE, HALF, 0, 4)
         finish(HALF, NP, 0, 4)

@@ -39,101 +39,63 @@ def tile_list_pairwise_state_correction_kernel(
         pos1_sb = lists.tile([P, NP // 16], U16, name="pos1_sb")
         pos2_sb = lists.tile([P, NP // 16], U16, name="pos2_sb")
 
-        warm = late.tile([P, 48], F32, name="warm", offset=960)
-        warm_out = late.tile([P, 48], F32, name="warm_out", offset=17888)
-        tscale = reuse.tile([P, T // 4], I32, name="tscale", align_bytes=64, offset=0)
-        nc.vector.memset(tscale[:], 0)
+        warm = keep.tile([P, 8], F32, name="warm")
+        warm_out = keep.tile([P, 8], F32, name="warm_out")
+        tscale = late.tile([P, T // 4], I32, name="tscale", align_bytes=64, offset=4 * T)
+        planes = [keep.tile([P, S // 4], I32, name="plane%d" % a, align_bytes=64) for a in range(PASSES)]
+        w2s_raw = late.tile([P, H // 4], I32, name="w2s_raw", align_bytes=64, offset=8192)
         nc.vector.memset(warm[:], 0.0)
         nc.scalar.activation(warm_out[:], warm[:], ACT.Tanh)
+        nc.vector.memset(tscale[32:64, :], 0)
+        nc.vector.memset(tscale[64:128, :], 0)
+        for a in range(PASSES):
+            nc.vector.memset(planes[a][:], 0)
 
         words = [
-            keep.tile([P, T], I32, name="words0", align_bytes=64),
-            late.tile([P, T], I32, name="words1", offset=17984),
+            late.tile([P, T], I32, name="words0", align_bytes=64, offset=0),
+            late.tile([P, T], I32, name="words1", align_bytes=64, offset=4 * T),
         ]
-        w1_all = late.tile([P, PASSES, PACK, H], F32, name="w1_all", offset=1088)
-        w1_raw = [w1_all[:, a, :, :] for a in range(PASSES)]
-        gain_sb = late.tile([P, PACK], F32, name="gain_sb", offset=1024)
-        w2_raw = late.tile([P, 2 * H // 4], I32, name="w2_raw", offset=0)
-        w2s_raw = late.tile([P, H // 4], I32, name="w2s_raw", offset=17472)
-        nc.vector.memset(w2s_raw[:], 0)
+        w1_raw = [
+            keep.tile([P, PACK, H], F32, name="w1_raw0"),
+            [late.tile([P, PACK, H // 2], F32, name="w1_raw1_%d" % u, align_bytes=64, offset=4096 * u) for u in range(2)],
+        ]
+        gain_sb = keep.tile([P, PACK], F32, name="gain_sb")
+        w2_raw = keep.tile([P, 2 * H // 4], I32, name="w2_raw")
 
         def load_words(a):
             nc.sync.dma_start(
                 out=words[a][:], in_=tab_words[a].rearrange("p n t -> p (n t)").bitcast(I32)
             )
 
-        def load_w1(a, c0, c1):
-            rows = w1[a * P * PACK : (a + 1) * P * PACK, c0:c1]
-            nc.sync.dma_start(
-                out=w1_raw[a][:, :, c0:c1], in_=rows.rearrange("(p j) c -> p j c", j=PACK)
-            )
+        def w1_rows(a, c0, c1):
+            return w1[a * P * PACK : (a + 1) * P * PACK, c0:c1].rearrange("(p j) c -> p j c", j=PACK)
 
+        nc.sync.dma_start(out=tscale[0:32, :], in_=tab_scales.rearrange("a q n -> (a q) n").bitcast(I32))
         nc.sync.dma_start(offs_sb[:], offs)
         nc.sync.dma_start(pos1_sb[:], pos1)
         nc.sync.dma_start(pos2_sb[:], pos2)
-        load_words(0)
-        for q in range(2):
-            for a in range(PASSES):
-                nc.sync.dma_start(
-                    out=tscale[32 * q + 4 * a : 32 * q + 4 * a + 4, :],
-                    in_=tab_scales[a, 4 * q : 4 * q + 4, :].bitcast(I32),
-                )
-        for q in range(2, 4):
-            nc.sync.dma_start(
-                out=tscale[32 * q : 32 * q + 4 * PASSES, :],
-                in_=tab_scales[:, 4 * q : 4 * q + 4, :].bitcast(I32),
-            )
-        load_w1(0, 0, H)
-        load_words(1)
-        load_w1(1, 0, H // 2)
-        load_w1(1, H // 2, H)
-        nc.sync.dma_start(out=w2_raw[:], in_=w2_words[0].bitcast(I32))
         nc.sync.dma_start(out=gain_sb[:], in_=gain.rearrange("(p t) -> p t", t=PACK))
-        for q in range(4):
-            nc.sync.dma_start(
-                out=w2s_raw[32 * q : 32 * q + 4, :],
-                in_=w2_scales[0, 4 * q : 4 * q + 4, :].bitcast(I32),
-            )
+        nc.sync.dma_start(out=w2_raw[:], in_=w2_words[0].bitcast(I32))
+        load_words(0)
+        nc.sync.dma_start(out=w1_raw[0][:], in_=w1_rows(0, 0, H))
 
-        g_first = keep.tile([P, S], U32, name="g_first", align_bytes=64)
-        g_second = reuse.tile([P, 2 * BANK], U32, name="g_second", align_bytes=64, offset=4 * H)
+        g_words = [keep.tile([P, S], U32, name="g_words%d" % a, align_bytes=64) for a in range(PASSES)]
+        g_scale = keep.tile([P, S // 4], I32, name="g_scale", align_bytes=64)
         w1_bf0 = keep.tile([P, PACK, P, PACK], BF16, name="w1_bf0", align_bytes=64)
         w1_bf1 = [
-            reuse.tile([P, 2, P, PACK], BF16, name="w1_bf1_%d" % u, align_bytes=64, offset=8192 + 2048 * u)
-            for u in range(2)
+            keep.tile([P, 2, P, PACK], BF16, name="w1_bf1_%d" % u, align_bytes=64) for u in range(2)
         ]
-        g_tail = reuse.tile([P, BANK], U32, name="g_tail", align_bytes=64, offset=0)
-        g_scale = keep.tile([P, S], U8, name="g_scale", align_bytes=64)
-
-        def g_words(a, s0, s1):
-            if a == 0:
-                return g_first[:, s0:s1]
-            if s0 < 2 * BANK:
-                return g_second[:, s0:s1]
-            return g_tail[:]
 
         def w1_bf(a, t0, t1):
             if a == 0:
                 return w1_bf0[:, t0:t1, :, :]
             return w1_bf1[t0 // 2][:]
 
-        w1_codes = [
-            keep.tile([P, H], U32, name="w1_codes0", align_bytes=64),
-            reuse.tile([P, H], U32, name="w1_codes1", align_bytes=64, offset=16384),
-        ]
+        w1_codes = [keep.tile([P, H], U32, name="w1_codes%d" % a, align_bytes=64) for a in range(PASSES)]
         w1_scales = keep.tile([P, PASSES, H], U8, name="w1_scales", align_bytes=64)
 
-        def gather_words(a, s0, s1):
-            nc.vector.tensor_copy(
-                g_words(a, s0, s1),
-                words[a][:].bitcast(U32).indirect(offs_sb[:, s0 // 16 : s1 // 16]),
-            )
-
-        def cast_w1(a, t0, t1, m0, m1, on_vector=False):
-            (nc.vector.tensor_copy if on_vector else nc.scalar.copy)(
-                w1_bf(a, t0, t1)[:, :, m0:m1, :].rearrange("p t m j -> p m t j"),
-                w1_raw[a].rearrange("p j (m t) -> p m t j", t=PACK)[:, m0:m1, t0:t1, :],
-            )
+        def gather_words(a):
+            nc.vector.tensor_copy(g_words[a][:], words[a][:].bitcast(U32).indirect(offs_sb[:]))
 
         def quant_w1(a, t0, t1):
             nc.vector.quantize_mx(
@@ -154,8 +116,8 @@ def tile_list_pairwise_state_correction_kernel(
                 out=banks[(t, s)][:],
                 lhsT=w1_codes[a][:, t * P : (t + 1) * P].bitcast(FP8X4),
                 lhsT_scale=w1_scales[:, a, t * P : (t + 1) * P],
-                rhs=g_words(a, s * BANK, (s + 1) * BANK).bitcast(FP8X4),
-                rhs_scale=g_scale[4 * a :, cols],
+                rhs=g_words[a][:, cols].bitcast(FP8X4),
+                rhs_scale=planes[a][:].bitcast(U8)[4 * a :, cols],
                 start=(a == 0),
                 stop=(a == PASSES - 1),
             )
@@ -168,27 +130,47 @@ def tile_list_pairwise_state_correction_kernel(
             else:
                 nc.scalar.copy(h[t][:, s * BANK : (s + 1) * BANK], banks[(t, s)][:])
 
-        w2_codes = reuse.tile([P, PACK, 2 * P], U8, name="w2_codes", align_bytes=64, offset=8192)
-        w2_sc = reuse.tile([P, PACK, P], U8, name="w2_sc", align_bytes=64, offset=8192 + 1024)
-        gather_words(0, 0, S)
-        nc.vector.tensor_copy(g_scale[:], tscale[:].bitcast(U8).indirect(offs_sb[:]))
-        cast_w1(0, 0, 2, 0, P)
-        cast_w1(0, 2, 4, 0, P)
-        quant_w1(0, 0, 4)
-        for t, s in groups[:8]:
-            h_pass(t, s, 0)
-        cast_w1(1, 0, 2, 0, P // 2)
-        cast_w1(1, 2, 4, 0, P // 2)
-        cast_w1(1, 0, 2, P // 2, P)
-        cast_w1(1, 2, 4, P // 2, P)
-        gather_words(1, 0, BANK)
-        gather_words(1, BANK, 2 * BANK)
-        gather_words(1, 2 * BANK, S)
-        quant_w1(1, 0, 2)
+        w2_codes = keep.tile([P, PACK, 2 * P], U8, name="w2_codes", align_bytes=64)
+        w2_sc = keep.tile([P, PACK, P], U8, name="w2_sc", align_bytes=64)
+        nc.vector.tensor_copy(g_scale[:].bitcast(U8), tscale[:].bitcast(U8).indirect(offs_sb[:]))
+
+        def carry_scales(a):
+            for r in range(4):
+                nc.sync.dma_start(
+                    out=planes[a][4 * a + r : P : 32, :], in_=g_scale[16 * a + r : 16 * a + 16 : 4, :]
+                )
+
+        carry_scales(0)
+        load_words(1)
+        carry_scales(1)
+        gather_words(0)
+        for u in range(2):
+            nc.sync.dma_start(out=w1_raw[1][u][:], in_=w1_rows(1, u * H // 2, (u + 1) * H // 2))
+        nc.vector.memset(w2s_raw[:], 0)
+        for q in range(4):
+            nc.sync.dma_start(
+                out=w2s_raw[32 * q : 32 * q + 4, :],
+                in_=w2_scales[0, 4 * q : 4 * q + 4, :].bitcast(I32),
+            )
+        nc.scalar.copy(
+            w1_bf0[:].rearrange("p t m j -> p m j t"),
+            w1_raw[0][:].rearrange("p j (m t) -> p m j t", t=PACK),
+        )
         nc.vector.tensor_copy(
             w2_codes[:].rearrange("p t (m b) -> p t m b", b=2),
             w2_raw[:].bitcast(U8).rearrange("p (m t b) -> p t m b", t=PACK, b=2),
         )
+        quant_w1(0, 0, 4)
+        for t, s in groups[:8]:
+            h_pass(t, s, 0)
+        gather_words(1)
+        for u in range(2):
+            for v in range(2):
+                nc.scalar.copy(
+                    w1_bf1[v][:, :, u * P // 2 : (u + 1) * P // 2, :].rearrange("p t m j -> p m j t"),
+                    w1_raw[1][u][:].rearrange("p j (m t) -> p m j t", t=PACK)[:, :, :, 2 * v : 2 * v + 2],
+                )
+        quant_w1(1, 0, 2)
         quant_w1(1, 2, 4)
         nc.vector.tensor_copy(
             w2_sc[:], w2s_raw[:].bitcast(U8).rearrange("p (m t) -> p t m", t=PACK)

@@ -232,15 +232,19 @@ def tile_list_pairwise_state_correction_kernel(
 
         def pick(t, j0, j1):
             nc.vector.tensor_copy(flat(a_of(t, t + 1, j0, j1)), h[t][:].indirect(pos1_sb[:, j0 // 16 : j1 // 16]))
-            nc.vector.tensor_copy(flat(b_of(t, t + 1, j0, j1)), h[t][:].indirect(pos2_sb[:, j0 // 16 : j1 // 16]))
+            nc.vector.tensor_tensor(
+                flat(b_of(t, t + 1, j0, j1)),
+                h[t][:].indirect(pos2_sb[:, j0 // 16 : j1 // 16]),
+                flat(a_of(t, t + 1, j0, j1)),
+                ALU.subtract,
+            )
 
         def d_of(t, j0, j1):
             return flat(b_of(t, t + 1, j0, j1))
 
         def squash(t, j0, j1, sub_engine):
             d = d_of(t, j0, j1)
-            sub_engine.tensor_tensor(d, flat(a_of(t, t + 1, j0, j1)), flat(b_of(t, t + 1, j0, j1)), ALU.subtract)
-            nc.scalar.activation(th_of(t, j0, j1), d, ACT.Tanh)
+            nc.scalar.activation(th_of(t, j0, j1), d, ACT.Tanh, scale=-1.0)
 
         def apply_gain(t, j0, j1, on_scalar):
             if on_scalar:

@@ -43,8 +43,9 @@ def tile_list_pairwise_state_correction_kernel(
         warm_out = keep.tile([P, 8], F32, name="warm_out")
         tscale = late.tile([P, T // 4], I32, name="tscale", align_bytes=64, offset=4 * T)
         planes = [keep.tile([P, S // 4], I32, name="plane%d" % a, align_bytes=64) for a in range(PASSES)]
-        w2s_raw = late.tile([P, H // 4], I32, name="w2s_raw", align_bytes=64, offset=8192)
+        w2s_raw = keep.tile([P, H // 4], I32, name="w2s_raw", align_bytes=64)
         nc.vector.memset(warm[:], 0.0)
+        nc.vector.memset(w2s_raw[:], 0)
         nc.scalar.activation(warm_out[:], warm[:], ACT.Tanh)
         nc.vector.memset(tscale[32:64, :], 0)
         nc.vector.memset(tscale[64:128, :], 0)
@@ -53,12 +54,9 @@ def tile_list_pairwise_state_correction_kernel(
 
         words = [
             late.tile([P, T], I32, name="words0", align_bytes=64, offset=0),
-            late.tile([P, T], I32, name="words1", align_bytes=64, offset=4 * T),
+            late.tile([P, T], I32, name="words1", align_bytes=64, offset=8 * T),
         ]
-        w1_raw = [
-            keep.tile([P, PACK, H], F32, name="w1_raw0"),
-            [late.tile([P, PACK, H // 2], F32, name="w1_raw1_%d" % u, align_bytes=64, offset=4096 * u) for u in range(2)],
-        ]
+        w1_raw = late.tile([P, PASSES, 2, PACK, H // 2], F32, name="w1_raw", align_bytes=64, offset=4 * T)
         gain_sb = keep.tile([P, PACK], F32, name="gain_sb")
         w2_raw = keep.tile([P, 2 * H // 4], I32, name="w2_raw")
 
@@ -67,9 +65,6 @@ def tile_list_pairwise_state_correction_kernel(
                 out=words[a][:], in_=tab_words[a].rearrange("p n t -> p (n t)").bitcast(I32)
             )
 
-        def w1_rows(a, c0, c1):
-            return w1[a * P * PACK : (a + 1) * P * PACK, c0:c1].rearrange("(p j) c -> p j c", j=PACK)
-
         nc.sync.dma_start(out=tscale[0:32, :], in_=tab_scales.rearrange("a q n -> (a q) n").bitcast(I32))
         nc.sync.dma_start(offs_sb[:], offs)
         nc.sync.dma_start(pos1_sb[:], pos1)
@@ -77,29 +72,53 @@ def tile_list_pairwise_state_correction_kernel(
         nc.sync.dma_start(out=gain_sb[:], in_=gain.rearrange("(p t) -> p t", t=PACK))
         nc.sync.dma_start(out=w2_raw[:], in_=w2_words[0].bitcast(I32))
         load_words(0)
-        nc.sync.dma_start(out=w1_raw[0][:], in_=w1_rows(0, 0, H))
+        for q in range(4):
+            nc.sync.dma_start(
+                out=w2s_raw[32 * q : 32 * q + 4, :],
+                in_=w2_scales[0, 4 * q : 4 * q + 4, :].bitcast(I32),
+            )
+        load_words(1)
 
-        g_words = [keep.tile([P, S], U32, name="g_words%d" % a, align_bytes=64) for a in range(PASSES)]
+        g_first = keep.tile([P, S], U32, name="g_first", align_bytes=64)
+        g_second = keep.tile([P, 2 * BANK], U32, name="g_second", align_bytes=64)
+        g_tail = reuse.tile([P, BANK], U32, name="g_tail", align_bytes=64, offset=24576)
         g_scale = keep.tile([P, S // 4], I32, name="g_scale", align_bytes=64)
-        w1_bf0 = keep.tile([P, PACK, P, PACK], BF16, name="w1_bf0", align_bytes=64)
-        w1_bf1 = [
-            keep.tile([P, 2, P, PACK], BF16, name="w1_bf1_%d" % u, align_bytes=64) for u in range(2)
-        ]
-
-        def w1_bf(a, t0, t1):
-            if a == 0:
-                return w1_bf0[:, t0:t1, :, :]
-            return w1_bf1[t0 // 2][:]
-
-        w1_codes = [keep.tile([P, H], U32, name="w1_codes%d" % a, align_bytes=64) for a in range(PASSES)]
+        bf0_head = reuse.tile([P, 1, P, PACK], BF16, name="bf0_head", align_bytes=64, offset=24576)
+        bf0_rest = keep.tile([P, 3, P, PACK], BF16, name="bf0_rest", align_bytes=64)
+        bf1_head = reuse.tile([P, 1, P, PACK], BF16, name="bf1_head", align_bytes=64, offset=26624)
+        bf1_rest = keep.tile([P, 3, P, PACK], BF16, name="bf1_rest", align_bytes=64)
+        codes0_head = keep.tile([P, P], U32, name="codes0_head", align_bytes=64)
+        codes0_rest = reuse.tile([P, 3 * P], U32, name="codes0_rest", align_bytes=64, offset=26624)
+        codes1 = keep.tile([P, H], U32, name="codes1", align_bytes=64)
         w1_scales = keep.tile([P, PASSES, H], U8, name="w1_scales", align_bytes=64)
 
-        def gather_words(a):
-            nc.vector.tensor_copy(g_words[a][:], words[a][:].bitcast(U32).indirect(offs_sb[:]))
+        def g_words(a, s):
+            if a == 0:
+                return g_first[:, s * BANK : (s + 1) * BANK]
+            return g_second[:, s * BANK : (s + 1) * BANK] if s < 2 else g_tail[:]
+
+        def w1_bf(a, t0, t1):
+            if t0 == 0:
+                return (bf0_head, bf1_head)[a][:]
+            return (bf0_rest, bf1_rest)[a][:, t0 - 1 : t1 - 1, :, :]
+
+        def w1_codes(a, t0, t1):
+            if a == 0:
+                return codes0_head[:] if t0 == 0 else codes0_rest[:, (t0 - 1) * P : (t1 - 1) * P]
+            return codes1[:, t0 * P : t1 * P]
+
+        def gather_words(dst, a, s0, s1):
+            nc.vector.tensor_copy(dst, words[a][:].bitcast(U32).indirect(offs_sb[:, s0 // 16 : s1 // 16]))
+
+        def cast_w1(copy, a, u, t0, t1):
+            copy(
+                w1_bf(a, t0, t1)[:, :, u * P // 2 : (u + 1) * P // 2, :].rearrange("p t m j -> p m j t"),
+                w1_raw[:, a, u, :, :].rearrange("p j (m t) -> p m j t", t=PACK)[:, :, :, t0:t1],
+            )
 
         def quant_w1(a, t0, t1):
             nc.vector.quantize_mx(
-                out=w1_codes[a][:, t0 * P : t1 * P].bitcast(FP8X4),
+                out=w1_codes(a, t0, t1).bitcast(FP8X4),
                 scales=w1_scales[:, a, t0 * P : t1 * P],
                 in_=w1_bf(a, t0, t1).rearrange("p t m j -> p (t m j)"),
             )
@@ -114,15 +133,16 @@ def tile_list_pairwise_state_correction_kernel(
             cols = slice(s * BANK, (s + 1) * BANK)
             nc.tensor.matmul_mx(
                 out=banks[(t, s)][:],
-                lhsT=w1_codes[a][:, t * P : (t + 1) * P].bitcast(FP8X4),
+                lhsT=w1_codes(a, t, t + 1).bitcast(FP8X4),
                 lhsT_scale=w1_scales[:, a, t * P : (t + 1) * P],
-                rhs=g_words[a][:, cols].bitcast(FP8X4),
+                rhs=g_words(a, s).bitcast(FP8X4),
                 rhs_scale=planes[a][:].bitcast(U8)[4 * a :, cols],
                 start=(a == 0),
                 stop=(a == PASSES - 1),
             )
 
-        h = [keep.tile([P, S], F32, name="h%d" % t) for t in range(PACK)]
+        h = [keep.tile([P, S], F32, name="h%d" % t) for t in range(PACK - 1)]
+        h.append(reuse.tile([P, S], F32, name="h3", align_bytes=64, offset=4096))
 
         def h_copy(t, s):
             if (t, s) in [(0, 1)]:
@@ -134,135 +154,133 @@ def tile_list_pairwise_state_correction_kernel(
         w2_sc = keep.tile([P, PACK, P], U8, name="w2_sc", align_bytes=64)
         nc.vector.tensor_copy(g_scale[:].bitcast(U8), tscale[:].bitcast(U8).indirect(offs_sb[:]))
 
-        def carry_scales(a):
-            for r in range(4):
+        def carry_scales(a, r0, r1):
+            for r in range(r0, r1):
                 nc.sync.dma_start(
                     out=planes[a][4 * a + r : P : 32, :], in_=g_scale[16 * a + r : 16 * a + 16 : 4, :]
                 )
 
-        carry_scales(0)
-        load_words(1)
-        carry_scales(1)
-        gather_words(0)
-        for u in range(2):
-            nc.sync.dma_start(out=w1_raw[1][u][:], in_=w1_rows(1, u * H // 2, (u + 1) * H // 2))
-        nc.vector.memset(w2s_raw[:], 0)
-        for q in range(4):
-            nc.sync.dma_start(
-                out=w2s_raw[32 * q : 32 * q + 4, :],
-                in_=w2_scales[0, 4 * q : 4 * q + 4, :].bitcast(I32),
-            )
-        nc.scalar.copy(
-            w1_bf0[:].rearrange("p t m j -> p m j t"),
-            w1_raw[0][:].rearrange("p j (m t) -> p m j t", t=PACK),
-        )
+        for a in range(PASSES):
+            carry_scales(a, 0, 4)
+            for u in range(2):
+                rows = w1[a * P * PACK : (a + 1) * P * PACK, u * H // 2 : (u + 1) * H // 2]
+                nc.sync.dma_start(out=w1_raw[:, a, u, :, :], in_=rows.rearrange("(p j) c -> p j c", j=PACK))
+        gather_words(g_first[:], 0, 0, S)
         nc.vector.tensor_copy(
             w2_codes[:].rearrange("p t (m b) -> p t m b", b=2),
             w2_raw[:].bitcast(U8).rearrange("p (m t b) -> p t m b", t=PACK, b=2),
         )
-        quant_w1(0, 0, 4)
-        for t, s in groups[:8]:
-            h_pass(t, s, 0)
-        gather_words(1)
-        for u in range(2):
-            for v in range(2):
-                nc.scalar.copy(
-                    w1_bf1[v][:, :, u * P // 2 : (u + 1) * P // 2, :].rearrange("p t m j -> p m j t"),
-                    w1_raw[1][u][:].rearrange("p j (m t) -> p m j t", t=PACK)[:, :, :, 2 * v : 2 * v + 2],
-                )
-        quant_w1(1, 0, 2)
-        quant_w1(1, 2, 4)
         nc.vector.tensor_copy(
             w2_sc[:], w2s_raw[:].bitcast(U8).rearrange("p (m t) -> p t m", t=PACK)
         )
-        for t, s in groups[:8]:
-            h_pass(t, s, 1)
-            h_copy(t, s)
-        for t, s in groups[8:]:
+        gather_words(g_second[:], 1, 0, 2 * BANK)
+        cast_w1(nc.scalar.copy, 0, 0, 0, 1)
+        cast_w1(nc.scalar.copy, 0, 0, 1, 4)
+        cast_w1(nc.vector.tensor_copy, 0, 1, 0, 1)
+        cast_w1(nc.scalar.copy, 0, 1, 1, 4)
+        quant_w1(0, 0, 1)
+        for s in range(SLICES):
+            h_pass(0, s, 0)
+        gather_words(g_tail[:], 1, 2 * BANK, S)
+        cast_w1(nc.scalar.copy, 1, 0, 0, 1)
+        cast_w1(nc.scalar.copy, 1, 0, 1, 4)
+        cast_w1(nc.vector.tensor_copy, 1, 1, 0, 1)
+        quant_w1(1, 0, 1)
+        cast_w1(nc.scalar.copy, 1, 1, 1, 2)
+        cast_w1(nc.scalar.copy, 1, 1, 2, 4)
+        for s in range(SLICES):
+            h_pass(0, s, 1)
+            h_copy(0, s)
+        quant_w1(0, 1, 2)
+        quant_w1(1, 1, 2)
+        quant_w1(0, 2, 4)
+        quant_w1(1, 2, 4)
+        for t, s in groups[SLICES:]:
             h_pass(t, s, 0)
             h_pass(t, s, 1)
             h_copy(t, s)
 
         WIDE = 2 * CHUNK
         a_wide = keep.tile([P, PACK, WIDE], F32, name="a_wide")
-        b_wide = keep.tile([P, PACK, WIDE], F32, name="b_wide")
-        ring = keep.tile([P, PACK + 1, WIDE], F32, name="ring")
-        th_last = keep.tile([P, PACK, CHUNK], F32, name="th_last")
-        z_planes = keep.tile([P, PACK, NP], BF16, name="z_planes")
-        z_bf = [
-            reuse.tile([P, CHUNK, PACK], BF16, name="z_bf0", align_bytes=64, offset=12288),
-            reuse.tile([P, CHUNK, PACK], BF16, name="z_bf1", align_bytes=64, offset=18432),
-            reuse.tile([P, CHUNK, PACK], BF16, name="z_bf2", align_bytes=64, offset=14336),
+        d_wide = keep.tile([P, PACK, WIDE], F32, name="d_wide")
+        th_first = keep.tile([P, WIDE], F32, name="th_first")
+        ring = keep.tile([P, PACK, CHUNK], F32, name="ring")
+        d_last = [
+            keep.tile([P, CHUNK], F32, name="d_last0"),
+            keep.tile([P, CHUNK], F32, name="d_last1"),
+            keep.tile([P, CHUNK], F32, name="d_last2"),
+            reuse.tile([P, CHUNK], F32, name="d_last3", align_bytes=64, offset=0),
         ]
-        b_end = reuse.tile([P, 1, CHUNK], F32, name="b_end", align_bytes=64, offset=12288)
+        th_last = [
+            reuse.tile([P, CHUNK], F32, name="th_last%d" % t, align_bytes=64, offset=14336 + 1024 * t)
+            for t in range(PACK)
+        ]
+        z_wide = reuse.tile([P, PACK, WIDE], BF16, name="z_wide", align_bytes=64, offset=14336)
+        z_last = keep.tile([P, PACK, CHUNK], BF16, name="z_last")
+        z_bf = [
+            reuse.tile([P, CHUNK, PACK], BF16, name="z_bf0", align_bytes=64, offset=0),
+            reuse.tile([P, CHUNK, PACK], BF16, name="z_bf1", align_bytes=64, offset=2048),
+            reuse.tile([P, P, PACK], BF16, name="z_bf2", align_bytes=64, offset=10240),
+            keep.tile([P, P, PACK], BF16, name="z_bf3", align_bytes=64),
+        ]
         z_codes = keep.tile([P, NP], U32, name="z_codes", align_bytes=64)
         z_scales = keep.tile([P, NP], U8, name="z_scales", align_bytes=64)
         o_sb = keep.tile([P, PACK, NP], F32, name="o_sb")
-        o_late = reuse.tile([P, 2, CHUNK], F32, name="o_late", align_bytes=64, offset=14336)
-        o_mid = reuse.tile([P, 2, CHUNK], F32, name="o_mid", align_bytes=64, offset=18432)
+        o_first = reuse.tile([P, PACK, CHUNK], F32, name="o_first", align_bytes=64, offset=4096)
+        o_late = reuse.tile([P, 2, CHUNK], F32, name="o_late", align_bytes=64, offset=10240)
         out_v = out.rearrange("(p t) j -> p t j", t=PACK)
 
         def a_of(t0, t1, j0, j1):
             if j0 < WIDE:
                 return a_wide[:, t0:t1, j0:j1]
-            return ring[:, t0 + 1 : t1 + 1, j0 - WIDE : j1 - WIDE]
+            return ring[:, t0:t1, j0 - WIDE : j1 - WIDE]
 
-        def b_of(t0, t1, j0, j1):
+        def d_of(t, j0, j1):
             if j0 < WIDE:
-                return b_wide[:, t0:t1, j0:j1]
-            if t0 == PACK - 1:
-                return b_end[:]
-            if t0 == PACK - 2:
-                return b_wide[:, PACK - 1 : PACK, 0:CHUNK]
-            return ring[:, t0 + 1 : t1 + 1, j0 - CHUNK : j1 - CHUNK]
-
-        def th_of(t, j0, j1):
-            if j0 < WIDE:
-                return ring[:, t, j0:j1]
-            if t == PACK - 1:
-                return b_wide[:, t, 0:CHUNK]
-            return th_last[:, t, j0 - WIDE : j1 - WIDE]
-
-        def z_of(j0, j1):
-            base = j0 // CHUNK * CHUNK
-            return z_bf[j0 // CHUNK][:, j0 - base : j1 - base, :]
+                return d_wide[:, t, j0:j1]
+            return d_last[t][:, j0 - WIDE : j1 - WIDE]
 
         def flat(ap):
             return ap.rearrange("p t n -> p (t n)")
 
-        def pick(t, j0, j1):
+        def th_of(t, j0, j1):
+            if j0 >= WIDE:
+                return th_last[t][:, j0 - WIDE : j1 - WIDE]
+            if t == 0:
+                return th_first[:, j0:j1]
+            row = 2 * min(t - 1, 1)
+            return flat(ring[:, row : row + 2, :])[:, j0:j1]
+
+        def planes_of(t0, t1, j0, j1):
+            if j0 < WIDE:
+                return z_wide[:, t0:t1, j0:j1]
+            return z_last[:, t0:t1, j0 - WIDE : j1 - WIDE]
+
+        def z_of(j0, j1):
+            return z_bf[j0 // CHUNK if j0 < WIDE else j0 // P - 2][:]
+
+        def pick_a(t, j0, j1):
             nc.vector.tensor_copy(flat(a_of(t, t + 1, j0, j1)), h[t][:].indirect(pos1_sb[:, j0 // 16 : j1 // 16]))
+
+        def pick_d(t, j0, j1):
             nc.vector.tensor_tensor(
-                flat(b_of(t, t + 1, j0, j1)),
+                d_of(t, j0, j1),
                 h[t][:].indirect(pos2_sb[:, j0 // 16 : j1 // 16]),
                 flat(a_of(t, t + 1, j0, j1)),
                 ALU.subtract,
             )
 
-        def d_of(t, j0, j1):
-            return flat(b_of(t, t + 1, j0, j1))
+        def squash(t, j0, j1):
+            nc.scalar.activation(th_of(t, j0, j1), d_of(t, j0, j1), ACT.Tanh, scale=-1.0)
+            nc.scalar.activation(
+                flat(planes_of(t, t + 1, j0, j1)), th_of(t, j0, j1), ACT.Copy, scale=gain_sb[:, t : t + 1]
+            )
 
-        def squash(t, j0, j1, sub_engine):
-            d = d_of(t, j0, j1)
-            nc.scalar.activation(th_of(t, j0, j1), d, ACT.Tanh, scale=-1.0)
-
-        def apply_gain(t, j0, j1, on_scalar):
-            if on_scalar:
-                nc.scalar.activation(
-                    z_planes[:, t, j0:j1], th_of(t, j0, j1), ACT.Copy, scale=gain_sb[:, t : t + 1]
-                )
-            else:
-                nc.gpsimd.tensor_scalar(
-                    z_planes[:, t, j0:j1], th_of(t, j0, j1), gain_sb[:, t : t + 1], 0.0, ALU.mult, ALU.add
-                )
-
-        def interleave(j0, j1, on_vector):
-            dst = z_of(j0, j1).rearrange("p (c i) t -> p c t i", i=4)
-            src = z_planes[:, :, j0:j1].rearrange("p t (c i) -> p c t i", i=4)
-            if on_vector:
-                nc.vector.tensor_copy(dst, src)
-            else:
-                nc.scalar.copy(dst, src)
+        def interleave(j0, j1):
+            nc.scalar.copy(
+                z_of(j0, j1).rearrange("p (c i) t -> p c t i", i=4),
+                planes_of(0, PACK, j0, j1).rearrange("p t (c i) -> p c t i", i=4),
+            )
 
         def quant_z(j0, j1):
             nc.vector.quantize_mx(
@@ -286,57 +304,51 @@ def tile_list_pairwise_state_correction_kernel(
                     stop=True,
                 )
 
-        def finish(j0, j1, t0, t1, unused=False):
-            dst = o_late[:] if (j0, t0) == (CHUNK, 2) else o_sb[:, t0:t1, j0:j1]
-            if (j0, t0) == (0, 2):
-                dst = o_mid[:]
+        def finish(j0, j1, t0, t1):
+            dst = o_sb[:, t0:t1, j0:j1]
+            if j0 == 0:
+                dst = o_first[:, t0:t1, :]
+            if (j0, t0) == (CHUNK, 2):
+                dst = o_late[:]
             nc.vector.tensor_tensor(dst, ybanks[(j0, t0)][:], a_of(t0, t1, j0, j1), ALU.add)
             nc.sync.dma_start(out=out_v[:, t0:t1, j0:j1], in_=dst)
 
         HALF = WIDE + P
+        for t in range(PACK):
+            pick_a(t, 0, CHUNK)
+            pick_a(t, CHUNK, WIDE)
+            pick_d(t, 0, CHUNK)
+            pick_d(t, CHUNK, WIDE)
+        for t in range(PACK - 1):
+            squash(t, 0, WIDE)
+        for j0 in (0, CHUNK):
+            squash(PACK - 1, j0, j0 + CHUNK)
+            interleave(j0, j0 + CHUNK)
         for t in range(2):
-            pick(t, 0, WIDE)
-            squash(t, 0, WIDE, nc.gpsimd)
-        apply_gain(0, 0, WIDE, True)
-        apply_gain(1, 0, WIDE, True)
-        pick(2, 0, WIDE)
-        squash(2, 0, WIDE, nc.gpsimd)
-        pick(3, 0, CHUNK)
-        squash(3, 0, CHUNK, nc.gpsimd)
-        apply_gain(2, 0, WIDE, True)
-        apply_gain(3, 0, CHUNK, True)
-        pick(3, CHUNK, WIDE)
-        squash(3, CHUNK, WIDE, nc.gpsimd)
-        interleave(0, CHUNK, False)
-        apply_gain(3, CHUNK, WIDE, True)
-        pick(0, WIDE, NP)
-        squash(0, WIDE, NP, nc.gpsimd)
-        interleave(CHUNK, WIDE, False)
-        apply_gain(0, WIDE, NP, True)
-        pick(1, WIDE, NP)
-        squash(1, WIDE, NP, nc.gpsimd)
+            pick_a(t, WIDE, NP)
+        for t in range(2):
+            pick_d(t, WIDE, NP)
+        for t in range(2, PACK):
+            pick_a(t, WIDE, NP)
+        pick_d(2, WIDE, NP)
         quant_z(0, CHUNK)
-        correct(0, CHUNK, 0, 2, 0)
-        correct(0, CHUNK, 2, 4, 1)
-        apply_gain(1, WIDE, NP, True)
-        pick(2, WIDE, NP)
-        squash(2, WIDE, NP, nc.gpsimd)
-        pick(3, WIDE, NP)
-        squash(3, WIDE, NP, nc.vector)
-        apply_gain(2, WIDE, NP, True)
-        apply_gain(3, WIDE, NP, True)
+        correct(0, CHUNK, 0, 2, 4)
+        correct(0, CHUNK, 2, 4, 5)
+        pick_d(3, WIDE, NP)
         quant_z(CHUNK, WIDE)
-        correct(CHUNK, WIDE, 0, 2, 2)
-        correct(CHUNK, WIDE, 2, 4, 3)
-        finish(0, CHUNK, 0, 2, False)
-        finish(0, CHUNK, 2, 4, False)
-        finish(CHUNK, WIDE, 0, 2, False)
-        interleave(WIDE, HALF, True)
-        interleave(HALF, NP, True)
+        correct(CHUNK, WIDE, 0, 2, 6)
+        correct(CHUNK, WIDE, 2, 4, 7)
+        for t in range(PACK):
+            squash(t, WIDE, NP)
+        interleave(WIDE, HALF)
+        interleave(HALF, NP)
+        finish(0, CHUNK, 0, 2)
+        finish(0, CHUNK, 2, 4)
         quant_z(WIDE, HALF)
         correct(WIDE, HALF, 0, 4, 0)
         quant_z(HALF, NP)
         correct(HALF, NP, 0, 4, 1)
-        finish(CHUNK, WIDE, 2, 4, False)
+        finish(CHUNK, WIDE, 0, 2)
+        finish(CHUNK, WIDE, 2, 4)
         finish(WIDE, HALF, 0, 4)
         finish(HALF, NP, 0, 4)

@@ -41,7 +41,7 @@ def tile_list_pairwise_state_correction_kernel(
 
         warm = keep.tile([P, 8], F32, name="warm")
         warm_out = keep.tile([P, 8], F32, name="warm_out")
-        tscale = late.tile([P, T // 4], I32, name="tscale", align_bytes=64, offset=4 * T)
+        tscale = late.tile([P, T // 4], I32, name="tscale", align_bytes=64, offset=4 * T + 2048)
         planes = [keep.tile([P, S // 4], I32, name="plane%d" % a, align_bytes=64) for a in range(PASSES)]
         w2s_raw = keep.tile([P, H // 4], I32, name="w2s_raw", align_bytes=64)
         nc.vector.memset(warm[:], 0.0)
@@ -54,9 +54,12 @@ def tile_list_pairwise_state_correction_kernel(
 
         words = [
             late.tile([P, T], I32, name="words0", align_bytes=64, offset=0),
-            late.tile([P, T], I32, name="words1", align_bytes=64, offset=8 * T),
+            keep.tile([P, T], I32, name="words1", align_bytes=64),
         ]
-        w1_raw = late.tile([P, PASSES, 2, PACK, H // 2], F32, name="w1_raw", align_bytes=64, offset=4 * T)
+        w1_raw = [
+            keep.tile([P, PACK, H], F32, name="w1_raw0"),
+            late.tile([P, PACK, H], F32, name="w1_raw1", align_bytes=64, offset=4 * T),
+        ]
         gain_sb = keep.tile([P, PACK], F32, name="gain_sb")
         w2_raw = keep.tile([P, 2 * H // 4], I32, name="w2_raw")
 
@@ -64,6 +67,9 @@ def tile_list_pairwise_state_correction_kernel(
             nc.sync.dma_start(
                 out=words[a][:], in_=tab_words[a].rearrange("p n t -> p (n t)").bitcast(I32)
             )
+
+        def w1_rows(a, c0, c1):
+            return w1[a * P * PACK : (a + 1) * P * PACK, c0:c1].rearrange("(p j) c -> p j c", j=PACK)
 
         nc.sync.dma_start(out=tscale[0:32, :], in_=tab_scales.rearrange("a q n -> (a q) n").bitcast(I32))
         nc.sync.dma_start(offs_sb[:], offs)
@@ -77,48 +83,32 @@ def tile_list_pairwise_state_correction_kernel(
                 out=w2s_raw[32 * q : 32 * q + 4, :],
                 in_=w2_scales[0, 4 * q : 4 * q + 4, :].bitcast(I32),
             )
+        nc.sync.dma_start(out=w1_raw[0][:], in_=w1_rows(0, 0, H))
         load_words(1)
 
-        g_first = keep.tile([P, S], U32, name="g_first", align_bytes=64)
-        g_second = keep.tile([P, 2 * BANK], U32, name="g_second", align_bytes=64)
-        g_tail = reuse.tile([P, BANK], U32, name="g_tail", align_bytes=64, offset=24576)
+        g_words = [keep.tile([P, S], U32, name="g_words%d" % a, align_bytes=64) for a in range(PASSES)]
         g_scale = keep.tile([P, S // 4], I32, name="g_scale", align_bytes=64)
-        bf0_head = reuse.tile([P, 1, P, PACK], BF16, name="bf0_head", align_bytes=64, offset=24576)
-        bf0_rest = keep.tile([P, 3, P, PACK], BF16, name="bf0_rest", align_bytes=64)
-        bf1_head = reuse.tile([P, 1, P, PACK], BF16, name="bf1_head", align_bytes=64, offset=26624)
-        bf1_rest = keep.tile([P, 3, P, PACK], BF16, name="bf1_rest", align_bytes=64)
-        codes0_head = keep.tile([P, P], U32, name="codes0_head", align_bytes=64)
-        codes0_rest = reuse.tile([P, 3 * P], U32, name="codes0_rest", align_bytes=64, offset=26624)
-        codes1 = keep.tile([P, H], U32, name="codes1", align_bytes=64)
-        w1_scales = keep.tile([P, PASSES, H], U8, name="w1_scales", align_bytes=64)
-
-        def g_words(a, s):
-            if a == 0:
-                return g_first[:, s * BANK : (s + 1) * BANK]
-            return g_second[:, s * BANK : (s + 1) * BANK] if s < 2 else g_tail[:]
+        w1_bf0 = keep.tile([P, PACK, P, PACK], BF16, name="w1_bf0", align_bytes=64)
+        w1_bf1 = {
+            0: reuse.tile([P, 1, P, PACK], BF16, name="w1_bf1_0", align_bytes=64, offset=20480),
+            1: keep.tile([P, 1, P, PACK], BF16, name="w1_bf1_1", align_bytes=64),
+            2: reuse.tile([P, 2, P, PACK], BF16, name="w1_bf1_2", align_bytes=64, offset=20480),
+        }
 
         def w1_bf(a, t0, t1):
-            if t0 == 0:
-                return (bf0_head, bf1_head)[a][:]
-            return (bf0_rest, bf1_rest)[a][:, t0 - 1 : t1 - 1, :, :]
-
-        def w1_codes(a, t0, t1):
             if a == 0:
-                return codes0_head[:] if t0 == 0 else codes0_rest[:, (t0 - 1) * P : (t1 - 1) * P]
-            return codes1[:, t0 * P : t1 * P]
+                return w1_bf0[:, t0:t1, :, :]
+            return w1_bf1[t0][:]
 
-        def gather_words(dst, a, s0, s1):
-            nc.vector.tensor_copy(dst, words[a][:].bitcast(U32).indirect(offs_sb[:, s0 // 16 : s1 // 16]))
+        w1_codes = [keep.tile([P, H], U32, name="w1_codes%d" % a, align_bytes=64) for a in range(PASSES)]
+        w1_scales = keep.tile([P, PASSES, H], U8, name="w1_scales", align_bytes=64)
 
-        def cast_w1(copy, a, u, t0, t1):
-            copy(
-                w1_bf(a, t0, t1)[:, :, u * P // 2 : (u + 1) * P // 2, :].rearrange("p t m j -> p m j t"),
-                w1_raw[:, a, u, :, :].rearrange("p j (m t) -> p m j t", t=PACK)[:, :, :, t0:t1],
-            )
+        def gather_words(a):
+            nc.vector.tensor_copy(g_words[a][:], words[a][:].bitcast(U32).indirect(offs_sb[:]))
 
         def quant_w1(a, t0, t1):
             nc.vector.quantize_mx(
-                out=w1_codes(a, t0, t1).bitcast(FP8X4),
+                out=w1_codes[a][:, t0 * P : t1 * P].bitcast(FP8X4),
                 scales=w1_scales[:, a, t0 * P : t1 * P],
                 in_=w1_bf(a, t0, t1).rearrange("p t m j -> p (t m j)"),
             )
@@ -133,16 +123,16 @@ def tile_list_pairwise_state_correction_kernel(
             cols = slice(s * BANK, (s + 1) * BANK)
             nc.tensor.matmul_mx(
                 out=banks[(t, s)][:],
-                lhsT=w1_codes(a, t, t + 1).bitcast(FP8X4),
+                lhsT=w1_codes[a][:, t * P : (t + 1) * P].bitcast(FP8X4),
                 lhsT_scale=w1_scales[:, a, t * P : (t + 1) * P],
-                rhs=g_words(a, s).bitcast(FP8X4),
+                rhs=g_words[a][:, cols].bitcast(FP8X4),
                 rhs_scale=planes[a][:].bitcast(U8)[4 * a :, cols],
                 start=(a == 0),
                 stop=(a == PASSES - 1),
             )
 
         h = [keep.tile([P, S], F32, name="h%d" % t) for t in range(PACK - 1)]
-        h.append(reuse.tile([P, S], F32, name="h3", align_bytes=64, offset=4096))
+        h.append(keep.tile([P, S], F32, name="h3"))
 
         def h_copy(t, s):
             if (t, s) in [(0, 1)]:
@@ -160,12 +150,14 @@ def tile_list_pairwise_state_correction_kernel(
                     out=planes[a][4 * a + r : P : 32, :], in_=g_scale[16 * a + r : 16 * a + 16 : 4, :]
                 )
 
-        for a in range(PASSES):
-            carry_scales(a, 0, 4)
-            for u in range(2):
-                rows = w1[a * P * PACK : (a + 1) * P * PACK, u * H // 2 : (u + 1) * H // 2]
-                nc.sync.dma_start(out=w1_raw[:, a, u, :, :], in_=rows.rearrange("(p j) c -> p j c", j=PACK))
-        gather_words(g_first[:], 0, 0, S)
+        carry_scales(0, 0, 4)
+        nc.sync.dma_start(out=w1_raw[1][:], in_=w1_rows(1, 0, H))
+        carry_scales(1, 0, 4)
+        gather_words(0)
+        nc.scalar.copy(
+            w1_bf0[:].rearrange("p t m j -> p m j t"),
+            w1_raw[0][:].rearrange("p j (m t) -> p m j t", t=PACK),
+        )
         nc.vector.tensor_copy(
             w2_codes[:].rearrange("p t (m b) -> p t m b", b=2),
             w2_raw[:].bitcast(U8).rearrange("p (m t b) -> p t m b", t=PACK, b=2),
@@ -173,29 +165,20 @@ def tile_list_pairwise_state_correction_kernel(
         nc.vector.tensor_copy(
             w2_sc[:], w2s_raw[:].bitcast(U8).rearrange("p (m t) -> p t m", t=PACK)
         )
-        gather_words(g_second[:], 1, 0, 2 * BANK)
-        cast_w1(nc.scalar.copy, 0, 0, 0, 1)
-        cast_w1(nc.scalar.copy, 0, 0, 1, 4)
-        cast_w1(nc.vector.tensor_copy, 0, 1, 0, 1)
-        cast_w1(nc.scalar.copy, 0, 1, 1, 4)
-        quant_w1(0, 0, 1)
-        for s in range(SLICES):
-            h_pass(0, s, 0)
-        gather_words(g_tail[:], 1, 2 * BANK, S)
-        cast_w1(nc.scalar.copy, 1, 0, 0, 1)
-        cast_w1(nc.scalar.copy, 1, 0, 1, 4)
-        cast_w1(nc.vector.tensor_copy, 1, 1, 0, 1)
-        quant_w1(1, 0, 1)
-        cast_w1(nc.scalar.copy, 1, 1, 1, 2)
-        cast_w1(nc.scalar.copy, 1, 1, 2, 4)
-        for s in range(SLICES):
-            h_pass(0, s, 1)
-            h_copy(0, s)
-        quant_w1(0, 1, 2)
-        quant_w1(1, 1, 2)
-        quant_w1(0, 2, 4)
-        quant_w1(1, 2, 4)
-        for t, s in groups[SLICES:]:
+        quant_w1(0, 0, 4)
+        for t, s in groups[:8]:
+            h_pass(t, s, 0)
+        gather_words(1)
+        for t0, t1, copy in ((0, 1, nc.scalar.copy), (1, 2, nc.scalar.copy), (2, 4, nc.vector.tensor_copy)):
+            copy(
+                w1_bf1[t0][:].rearrange("p t m j -> p m j t"),
+                w1_raw[1][:].rearrange("p j (m t) -> p m j t", t=PACK)[:, :, :, t0:t1],
+            )
+            quant_w1(1, t0, t1)
+        for t, s in groups[:8]:
+            h_pass(t, s, 1)
+            h_copy(t, s)
+        for t, s in groups[8:]:
             h_pass(t, s, 0)
             h_pass(t, s, 1)
             h_copy(t, s)
@@ -218,16 +201,14 @@ def tile_list_pairwise_state_correction_kernel(
         z_wide = reuse.tile([P, PACK, WIDE], BF16, name="z_wide", align_bytes=64, offset=14336)
         z_last = keep.tile([P, PACK, CHUNK], BF16, name="z_last")
         z_bf = [
-            reuse.tile([P, CHUNK, PACK], BF16, name="z_bf0", align_bytes=64, offset=0),
-            reuse.tile([P, CHUNK, PACK], BF16, name="z_bf1", align_bytes=64, offset=2048),
+            reuse.tile([P, WIDE, PACK], BF16, name="z_bf0", align_bytes=64, offset=0),
             reuse.tile([P, P, PACK], BF16, name="z_bf2", align_bytes=64, offset=10240),
             keep.tile([P, P, PACK], BF16, name="z_bf3", align_bytes=64),
         ]
         z_codes = keep.tile([P, NP], U32, name="z_codes", align_bytes=64)
         z_scales = keep.tile([P, NP], U8, name="z_scales", align_bytes=64)
         o_sb = keep.tile([P, PACK, NP], F32, name="o_sb")
-        o_first = reuse.tile([P, PACK, CHUNK], F32, name="o_first", align_bytes=64, offset=4096)
-        o_late = reuse.tile([P, 2, CHUNK], F32, name="o_late", align_bytes=64, offset=10240)
+        o_late = reuse.tile([P, 1, WIDE], F32, name="o_late", align_bytes=64, offset=10240)
         out_v = out.rearrange("(p t) j -> p t j", t=PACK)
 
         def a_of(t0, t1, j0, j1):
@@ -257,7 +238,9 @@ def tile_list_pairwise_state_correction_kernel(
             return z_last[:, t0:t1, j0 - WIDE : j1 - WIDE]
 
         def z_of(j0, j1):
-            return z_bf[j0 // CHUNK if j0 < WIDE else j0 // P - 2][:]
+            if j0 < WIDE:
+                return z_bf[0][:, j0:j1, :]
+            return z_bf[j0 // P - 3][:]
 
         def pick_a(t, j0, j1):
             nc.vector.tensor_copy(flat(a_of(t, t + 1, j0, j1)), h[t][:].indirect(pos1_sb[:, j0 // 16 : j1 // 16]))
@@ -270,8 +253,14 @@ def tile_list_pairwise_state_correction_kernel(
                 ALU.subtract,
             )
 
-        def squash(t, j0, j1):
+        def saturate(t, j0, j1):
             nc.scalar.activation(th_of(t, j0, j1), d_of(t, j0, j1), ACT.Tanh, scale=-1.0)
+
+        def squash(t, j0, j1):
+            saturate(t, j0, j1)
+            apply_gain(t, j0, j1)
+
+        def apply_gain(t, j0, j1):
             nc.scalar.activation(
                 flat(planes_of(t, t + 1, j0, j1)), th_of(t, j0, j1), ACT.Copy, scale=gain_sb[:, t : t + 1]
             )
@@ -306,9 +295,7 @@ def tile_list_pairwise_state_correction_kernel(
 
         def finish(j0, j1, t0, t1):
             dst = o_sb[:, t0:t1, j0:j1]
-            if j0 == 0:
-                dst = o_first[:, t0:t1, :]
-            if (j0, t0) == (CHUNK, 2):
+            if (j0, t0) == (0, PACK - 1):
                 dst = o_late[:]
             nc.vector.tensor_tensor(dst, ybanks[(j0, t0)][:], a_of(t0, t1, j0, j1), ALU.add)
             nc.sync.dma_start(out=out_v[:, t0:t1, j0:j1], in_=dst)
@@ -323,6 +310,7 @@ def tile_list_pairwise_state_correction_kernel(
             squash(t, 0, WIDE)
         for j0 in (0, CHUNK):
             squash(PACK - 1, j0, j0 + CHUNK)
+        for j0 in (0, CHUNK):
             interleave(j0, j0 + CHUNK)
         for t in range(2):
             pick_a(t, WIDE, NP)
@@ -331,24 +319,25 @@ def tile_list_pairwise_state_correction_kernel(
         for t in range(2, PACK):
             pick_a(t, WIDE, NP)
         pick_d(2, WIDE, NP)
-        quant_z(0, CHUNK)
-        correct(0, CHUNK, 0, 2, 4)
-        correct(0, CHUNK, 2, 4, 5)
-        pick_d(3, WIDE, NP)
-        quant_z(CHUNK, WIDE)
-        correct(CHUNK, WIDE, 0, 2, 6)
-        correct(CHUNK, WIDE, 2, 4, 7)
+        quant_z(0, WIDE)
         for t in range(PACK):
+            correct(0, WIDE, t, t + 1, 4 + t)
+        pick_d(3, WIDE, HALF)
+        pick_d(3, HALF, NP)
+        for t in range(PACK - 1):
             squash(t, WIDE, NP)
+        for step in (saturate, apply_gain):
+            step(PACK - 1, WIDE, HALF)
+            step(PACK - 1, HALF, NP)
         interleave(WIDE, HALF)
         interleave(HALF, NP)
-        finish(0, CHUNK, 0, 2)
-        finish(0, CHUNK, 2, 4)
         quant_z(WIDE, HALF)
         correct(WIDE, HALF, 0, 4, 0)
         quant_z(HALF, NP)
-        correct(HALF, NP, 0, 4, 1)
-        finish(CHUNK, WIDE, 0, 2)
-        finish(CHUNK, WIDE, 2, 4)
+        correct(HALF, NP, 0, 2, 1)
+        correct(HALF, NP, 2, 4, 2)
+        for t in range(PACK):
+            finish(0, WIDE, t, t + 1)
         finish(WIDE, HALF, 0, 4)
-        finish(HALF, NP, 0, 4)
+        finish(HALF, NP, 0, 2)
+        finish(HALF, NP, 2, 4)

@@ -19,9 +19,20 @@ ACT = mybir.ActivationFunctionType
 P = 128
 PACK = 4
 PASSES = K // (P * PACK)
+BLOCKS = 16
+QUAD = 32
 BANK = 512
+BANKS = 8
 SLICES = S // BANK
-CHUNK = 256
+WIDE = 512
+LAST = NP - WIDE
+HALF = WIDE + P
+PIECE = 256
+
+AT_SCALE_WINDOW = 0
+AT_PICKED_SCALES = 8192
+AT_ROUNDED = 10240
+AT_WIDE_PLANES = 12288
 
 
 def tile_list_pairwise_state_correction_kernel(
@@ -31,185 +42,172 @@ def tile_list_pairwise_state_correction_kernel(
     with ExitStack() as ctx:
         lists = ctx.enter_context(tc.tile_pool(name="lists", bufs=1))
         keep = ctx.enter_context(tc.tile_pool(name="keep", bufs=1))
-        reuse = ctx.enter_context(tc.tile_pool(name="reuse", bufs=1))
-        late = ctx.enter_context(tc.tile_pool(name="late", bufs=1))
+        shared = ctx.enter_context(tc.tile_pool(name="shared", bufs=1))
         psum = ctx.enter_context(tc.psum_pool(name="psum", bufs=1))
 
         offs_sb = lists.tile([P, S // 16], U16, name="offs_sb")
         pos1_sb = lists.tile([P, NP // 16], U16, name="pos1_sb")
         pos2_sb = lists.tile([P, NP // 16], U16, name="pos2_sb")
 
-        warm = keep.tile([P, 8], F32, name="warm")
-        warm_out = keep.tile([P, 8], F32, name="warm_out")
-        tscale = late.tile([P, T // 4], I32, name="tscale", align_bytes=64, offset=4 * T + 2048)
-        planes = [keep.tile([P, S // 4], I32, name="plane%d" % a, align_bytes=64) for a in range(PASSES)]
-        w2s_raw = keep.tile([P, H // 4], I32, name="w2s_raw", align_bytes=64)
-        nc.vector.memset(warm[:], 0.0)
-        nc.vector.memset(w2s_raw[:], 0)
-        nc.scalar.activation(warm_out[:], warm[:], ACT.Tanh)
-        nc.vector.memset(tscale[32:64, :], 0)
-        nc.vector.memset(tscale[64:128, :], 0)
-        for a in range(PASSES):
-            nc.vector.memset(planes[a][:], 0)
+        scale_window = shared.tile([P, T // 4], I32, name="scale_window", align_bytes=64, offset=AT_SCALE_WINDOW)
+        v_scales = [keep.tile([P, S // 4], I32, name="v_scales%d" % g, align_bytes=64) for g in range(PASSES)]
+        w2_scales_raw = keep.tile([P, H // 4], I32, name="w2_scales_raw", align_bytes=64)
+        nc.vector.memset(w2_scales_raw[:], 0)
+        nc.vector.memset(scale_window[QUAD : 2 * QUAD, :], 0)
+        nc.vector.memset(scale_window[2 * QUAD : P, :], 0)
+        for g in range(PASSES):
+            nc.vector.memset(v_scales[g][:], 0)
 
-        words = [
-            late.tile([P, T], I32, name="words0", align_bytes=64, offset=0),
-            keep.tile([P, T], I32, name="words1", align_bytes=64),
-        ]
+        words = [keep.tile([P, T], I32, name="words%d" % g, align_bytes=64) for g in range(PASSES)]
         w1_raw = [
             keep.tile([P, PACK, H], F32, name="w1_raw0"),
-            late.tile([P, PACK, H], F32, name="w1_raw1", align_bytes=64, offset=4 * T),
+            shared.tile([P, PACK, H], F32, name="w1_raw1", align_bytes=64, offset=AT_SCALE_WINDOW),
         ]
-        gain_sb = keep.tile([P, PACK], F32, name="gain_sb")
-        w2_raw = keep.tile([P, 2 * H // 4], I32, name="w2_raw")
+        w2_words_raw = keep.tile([P, 2 * H // 4], I32, name="w2_words_raw")
+        gain_sb = shared.tile([P, PACK], F32, name="gain_sb", align_bytes=64, offset=AT_PICKED_SCALES)
 
-        def load_words(a):
-            nc.sync.dma_start(
-                out=words[a][:], in_=tab_words[a].rearrange("p n t -> p (n t)").bitcast(I32)
-            )
+        def load_words(g):
+            nc.sync.dma_start(out=words[g][:], in_=tab_words[g].rearrange("p n i -> p (n i)").bitcast(I32))
 
-        def w1_rows(a, c0, c1):
-            return w1[a * P * PACK : (a + 1) * P * PACK, c0:c1].rearrange("(p j) c -> p j c", j=PACK)
+        def load_w1(g):
+            rows = w1[g * P * PACK : (g + 1) * P * PACK, :]
+            nc.sync.dma_start(out=w1_raw[g][:], in_=rows.rearrange("(p j) c -> p j c", j=PACK))
 
-        nc.sync.dma_start(out=tscale[0:32, :], in_=tab_scales.rearrange("a q n -> (a q) n").bitcast(I32))
+        nc.sync.dma_start(out=scale_window[0:QUAD, :], in_=tab_scales.rearrange("g q n -> (g q) n").bitcast(I32))
         nc.sync.dma_start(offs_sb[:], offs)
         nc.sync.dma_start(pos1_sb[:], pos1)
         nc.sync.dma_start(pos2_sb[:], pos2)
-        nc.sync.dma_start(out=gain_sb[:], in_=gain.rearrange("(p t) -> p t", t=PACK))
-        nc.sync.dma_start(out=w2_raw[:], in_=w2_words[0].bitcast(I32))
+        nc.sync.dma_start(out=w2_words_raw[:], in_=w2_words[0].bitcast(I32))
         load_words(0)
-        for q in range(4):
+        for quad in range(P // QUAD):
             nc.sync.dma_start(
-                out=w2s_raw[32 * q : 32 * q + 4, :],
-                in_=w2_scales[0, 4 * q : 4 * q + 4, :].bitcast(I32),
+                out=w2_scales_raw[QUAD * quad : QUAD * quad + 4, :],
+                in_=w2_scales[0, 4 * quad : 4 * quad + 4, :].bitcast(I32),
             )
-        nc.sync.dma_start(out=w1_raw[0][:], in_=w1_rows(0, 0, H))
+        load_w1(0)
         load_words(1)
 
-        g_words = [keep.tile([P, S], U32, name="g_words%d" % a, align_bytes=64) for a in range(PASSES)]
-        g_scale = keep.tile([P, S // 4], I32, name="g_scale", align_bytes=64)
-        w1_bf0 = keep.tile([P, PACK, P, PACK], BF16, name="w1_bf0", align_bytes=64)
-        w1_bf1 = {
-            0: reuse.tile([P, 1, P, PACK], BF16, name="w1_bf1_0", align_bytes=64, offset=20480),
-            1: keep.tile([P, 1, P, PACK], BF16, name="w1_bf1_1", align_bytes=64),
-            2: reuse.tile([P, 2, P, PACK], BF16, name="w1_bf1_2", align_bytes=64, offset=20480),
-        }
+        picked_scales = shared.tile([P, S // 4], I32, name="picked_scales", align_bytes=64, offset=AT_PICKED_SCALES)
+        v_words = [keep.tile([P, S], U32, name="v_words%d" % g, align_bytes=64) for g in range(PASSES)]
+        nc.vector.tensor_copy(picked_scales[:].bitcast(U8), scale_window[:].bitcast(U8).indirect(offs_sb[:]))
 
-        def w1_bf(a, t0, t1):
-            if a == 0:
-                return w1_bf0[:, t0:t1, :, :]
-            return w1_bf1[t0][:]
-
-        w1_codes = [keep.tile([P, H], U32, name="w1_codes%d" % a, align_bytes=64) for a in range(PASSES)]
-        w1_scales = keep.tile([P, PASSES, H], U8, name="w1_scales", align_bytes=64)
-
-        def gather_words(a):
-            nc.vector.tensor_copy(g_words[a][:], words[a][:].bitcast(U32).indirect(offs_sb[:]))
-
-        def quant_w1(a, t0, t1):
-            nc.vector.quantize_mx(
-                out=w1_codes[a][:, t0 * P : t1 * P].bitcast(FP8X4),
-                scales=w1_scales[:, a, t0 * P : t1 * P],
-                in_=w1_bf(a, t0, t1).rearrange("p t m j -> p (t m j)"),
-            )
-
-        groups = [(t, s) for t in range(PACK) for s in range(SLICES)]
-        banks = {}
-
-        def h_pass(t, s, a):
-            if a == 0:
-                g = groups.index((t, s))
-                banks[(t, s)] = psum.tile([P, BANK], F32, name="bank%d" % (g % 8))
-            cols = slice(s * BANK, (s + 1) * BANK)
-            nc.tensor.matmul_mx(
-                out=banks[(t, s)][:],
-                lhsT=w1_codes[a][:, t * P : (t + 1) * P].bitcast(FP8X4),
-                lhsT_scale=w1_scales[:, a, t * P : (t + 1) * P],
-                rhs=g_words[a][:, cols].bitcast(FP8X4),
-                rhs_scale=planes[a][:].bitcast(U8)[4 * a :, cols],
-                start=(a == 0),
-                stop=(a == PASSES - 1),
-            )
-
-        h = [keep.tile([P, S], F32, name="h%d" % t) for t in range(PACK - 1)]
-        h.append(keep.tile([P, S], F32, name="h3"))
-
-        def h_copy(t, s):
-            if (t, s) in [(0, 1)]:
-                nc.vector.tensor_copy(h[t][:, s * BANK : (s + 1) * BANK], banks[(t, s)][:])
-            else:
-                nc.scalar.copy(h[t][:, s * BANK : (s + 1) * BANK], banks[(t, s)][:])
-
-        w2_codes = keep.tile([P, PACK, 2 * P], U8, name="w2_codes", align_bytes=64)
-        w2_sc = keep.tile([P, PACK, P], U8, name="w2_sc", align_bytes=64)
-        nc.vector.tensor_copy(g_scale[:].bitcast(U8), tscale[:].bitcast(U8).indirect(offs_sb[:]))
-
-        def carry_scales(a, r0, r1):
-            for r in range(r0, r1):
+        def carry_scales(g):
+            for r in range(4):
                 nc.sync.dma_start(
-                    out=planes[a][4 * a + r : P : 32, :], in_=g_scale[16 * a + r : 16 * a + 16 : 4, :]
+                    out=v_scales[g][4 * g + r : P : QUAD, :],
+                    in_=picked_scales[BLOCKS * g + r : BLOCKS * (g + 1) : 4, :],
                 )
 
-        carry_scales(0, 0, 4)
-        nc.sync.dma_start(out=w1_raw[1][:], in_=w1_rows(1, 0, H))
-        carry_scales(1, 0, 4)
+        def gather_words(g):
+            nc.vector.tensor_copy(v_words[g][:], words[g][:].bitcast(U32).indirect(offs_sb[:]))
+
+        carry_scales(0)
+        load_w1(1)
+        carry_scales(1)
+        nc.sync.dma_start(out=gain_sb[:], in_=gain.rearrange("(p t) -> p t", t=PACK))
         gather_words(0)
-        nc.scalar.copy(
-            w1_bf0[:].rearrange("p t m j -> p m j t"),
-            w1_raw[0][:].rearrange("p j (m t) -> p m j t", t=PACK),
-        )
+
+        w1_codes = [keep.tile([P, H], U32, name="w1_codes%d" % g, align_bytes=64) for g in range(PASSES)]
+        w1_scales = keep.tile([P, PASSES, H], U8, name="w1_scales", align_bytes=64)
+
+        def round_w1(copy, rounded, g, t0, t1):
+            copy(
+                rounded[:].rearrange("p t m j -> p m j t"),
+                w1_raw[g][:].rearrange("p j (m t) -> p m j t", t=PACK)[:, :, :, t0:t1],
+            )
+
+        def quantise_w1(rounded, g, t0, t1):
+            nc.vector.quantize_mx(
+                out=w1_codes[g][:, t0 * P : t1 * P].bitcast(FP8X4),
+                scales=w1_scales[:, g, t0 * P : t1 * P],
+                in_=rounded[:].rearrange("p t m j -> p (t m j)"),
+            )
+
+        rounded0 = keep.tile([P, PACK, P, PACK], BF16, name="rounded0", align_bytes=64)
+        round_w1(nc.scalar.copy, rounded0, 0, 0, PACK)
+
+        w2_codes = keep.tile([P, PACK, 2 * P], U8, name="w2_codes", align_bytes=64)
+        w2_scale_bytes = keep.tile([P, PACK, P], U8, name="w2_scale_bytes", align_bytes=64)
         nc.vector.tensor_copy(
             w2_codes[:].rearrange("p t (m b) -> p t m b", b=2),
-            w2_raw[:].bitcast(U8).rearrange("p (m t b) -> p t m b", t=PACK, b=2),
+            w2_words_raw[:].bitcast(U8).rearrange("p (m t b) -> p t m b", t=PACK, b=2),
         )
         nc.vector.tensor_copy(
-            w2_sc[:], w2s_raw[:].bitcast(U8).rearrange("p (m t) -> p t m", t=PACK)
+            w2_scale_bytes[:], w2_scales_raw[:].bitcast(U8).rearrange("p (m t) -> p t m", t=PACK)
         )
-        quant_w1(0, 0, 4)
-        for t, s in groups[:8]:
+        quantise_w1(rounded0, 0, 0, PACK)
+
+        groups = [(t, s) for t in range(PACK) for s in range(SLICES)]
+        h_banks = {}
+        h = [keep.tile([P, S], F32, name="h%d" % t) for t in range(PACK)]
+
+        def h_pass(t, s, g):
+            if g == 0:
+                h_banks[(t, s)] = psum.tile([P, BANK], F32, name="bank%d" % (groups.index((t, s)) % BANKS))
+            cols = slice(s * BANK, (s + 1) * BANK)
+            nc.tensor.matmul_mx(
+                out=h_banks[(t, s)][:],
+                lhsT=w1_codes[g][:, t * P : (t + 1) * P].bitcast(FP8X4),
+                lhsT_scale=w1_scales[:, g, t * P : (t + 1) * P],
+                rhs=v_words[g][:, cols].bitcast(FP8X4),
+                rhs_scale=v_scales[g][:].bitcast(U8)[4 * g :, cols],
+                start=(g == 0),
+                stop=(g == PASSES - 1),
+            )
+
+        def empty_bank(t, s):
+            copy = nc.vector.tensor_copy if (t, s) == (0, 1) else nc.scalar.copy
+            copy(h[t][:, s * BANK : (s + 1) * BANK], h_banks[(t, s)][:])
+
+        for t, s in groups[:BANKS]:
             h_pass(t, s, 0)
         gather_words(1)
-        for t0, t1, copy in ((0, 1, nc.scalar.copy), (1, 2, nc.scalar.copy), (2, 4, nc.vector.tensor_copy)):
-            copy(
-                w1_bf1[t0][:].rearrange("p t m j -> p m j t"),
-                w1_raw[1][:].rearrange("p j (m t) -> p m j t", t=PACK)[:, :, :, t0:t1],
-            )
-            quant_w1(1, t0, t1)
-        for t, s in groups[:8]:
+        for t0, t1, copy, rounded in (
+            (0, 1, nc.scalar.copy, shared.tile([P, 1, P, PACK], BF16, name="rounded1_0", align_bytes=64, offset=AT_ROUNDED)),
+            (1, 2, nc.scalar.copy, keep.tile([P, 1, P, PACK], BF16, name="rounded1_1", align_bytes=64)),
+            (2, 4, nc.vector.tensor_copy, shared.tile([P, 2, P, PACK], BF16, name="rounded1_23", align_bytes=64, offset=AT_ROUNDED)),
+        ):
+            round_w1(copy, rounded, 1, t0, t1)
+            quantise_w1(rounded, 1, t0, t1)
+        for t, s in groups[:BANKS]:
             h_pass(t, s, 1)
-            h_copy(t, s)
-        for t, s in groups[8:]:
+            empty_bank(t, s)
+        for t, s in groups[BANKS:]:
             h_pass(t, s, 0)
             h_pass(t, s, 1)
-            h_copy(t, s)
+            empty_bank(t, s)
 
-        WIDE = 2 * CHUNK
+        row_bytes = 4 * LAST
+
+        def row_on_wide_planes(name, place):
+            return shared.tile([P, LAST], F32, name=name, align_bytes=64, offset=AT_WIDE_PLANES + place * row_bytes)
+
         a_wide = keep.tile([P, PACK, WIDE], F32, name="a_wide")
         d_wide = keep.tile([P, PACK, WIDE], F32, name="d_wide")
-        th_first = keep.tile([P, WIDE], F32, name="th_first")
-        ring = keep.tile([P, PACK, CHUNK], F32, name="ring")
+        tanh_wide0 = keep.tile([P, WIDE], F32, name="tanh_wide0")
+        ring = keep.tile([P, PACK, LAST], F32, name="ring")
+        z_planes_wide = shared.tile([P, PACK, WIDE], BF16, name="z_planes_wide", align_bytes=64, offset=AT_WIDE_PLANES)
+        z_planes_last = keep.tile([P, PACK, LAST], BF16, name="z_planes_last")
         d_last = [
-            keep.tile([P, CHUNK], F32, name="d_last0"),
-            keep.tile([P, CHUNK], F32, name="d_last1"),
-            keep.tile([P, CHUNK], F32, name="d_last2"),
-            reuse.tile([P, CHUNK], F32, name="d_last3", align_bytes=64, offset=0),
+            keep.tile([P, LAST], F32, name="d_last0"),
+            keep.tile([P, LAST], F32, name="d_last1"),
+            row_on_wide_planes("d_last2", 2),
+            row_on_wide_planes("d_last3", 3),
         ]
-        th_last = [
-            reuse.tile([P, CHUNK], F32, name="th_last%d" % t, align_bytes=64, offset=14336 + 1024 * t)
-            for t in range(PACK)
+        tanh_last = [
+            row_on_wide_planes("tanh_last0", 0),
+            row_on_wide_planes("tanh_last1", 1),
+            keep.tile([P, LAST], F32, name="tanh_last2"),
+            keep.tile([P, LAST], F32, name="tanh_last3"),
         ]
-        z_wide = reuse.tile([P, PACK, WIDE], BF16, name="z_wide", align_bytes=64, offset=14336)
-        z_last = keep.tile([P, PACK, CHUNK], BF16, name="z_last")
-        z_bf = [
-            reuse.tile([P, WIDE, PACK], BF16, name="z_bf0", align_bytes=64, offset=0),
-            reuse.tile([P, P, PACK], BF16, name="z_bf2", align_bytes=64, offset=10240),
-            keep.tile([P, P, PACK], BF16, name="z_bf3", align_bytes=64),
-        ]
+        z_words = keep.tile([P, NP, PACK], BF16, name="z_words", align_bytes=64)
         z_codes = keep.tile([P, NP], U32, name="z_codes", align_bytes=64)
         z_scales = keep.tile([P, NP], U8, name="z_scales", align_bytes=64)
-        o_sb = keep.tile([P, PACK, NP], F32, name="o_sb")
-        o_late = reuse.tile([P, 1, WIDE], F32, name="o_late", align_bytes=64, offset=10240)
-        out_v = out.rearrange("(p t) j -> p t j", t=PACK)
+        result = keep.tile([P, PACK, NP], F32, name="result")
+        out_rows = out.rearrange("(p t) j -> p t j", t=PACK)
+
+        def flat(ap):
+            return ap.rearrange("p t n -> p (t n)")
 
         def a_of(t0, t1, j0, j1):
             if j0 < WIDE:
@@ -221,26 +219,18 @@ def tile_list_pairwise_state_correction_kernel(
                 return d_wide[:, t, j0:j1]
             return d_last[t][:, j0 - WIDE : j1 - WIDE]
 
-        def flat(ap):
-            return ap.rearrange("p t n -> p (t n)")
-
-        def th_of(t, j0, j1):
+        def tanh_of(t, j0, j1):
             if j0 >= WIDE:
-                return th_last[t][:, j0 - WIDE : j1 - WIDE]
+                return tanh_last[t][:, j0 - WIDE : j1 - WIDE]
             if t == 0:
-                return th_first[:, j0:j1]
-            row = 2 * min(t - 1, 1)
+                return tanh_wide0[:, j0:j1]
+            row = 0 if t == 1 else 2
             return flat(ring[:, row : row + 2, :])[:, j0:j1]
 
         def planes_of(t0, t1, j0, j1):
             if j0 < WIDE:
-                return z_wide[:, t0:t1, j0:j1]
-            return z_last[:, t0:t1, j0 - WIDE : j1 - WIDE]
-
-        def z_of(j0, j1):
-            if j0 < WIDE:
-                return z_bf[0][:, j0:j1, :]
-            return z_bf[j0 // P - 3][:]
+                return z_planes_wide[:, t0:t1, j0:j1]
+            return z_planes_last[:, t0:t1, j0 - WIDE : j1 - WIDE]
 
         def pick_a(t, j0, j1):
             nc.vector.tensor_copy(flat(a_of(t, t + 1, j0, j1)), h[t][:].indirect(pos1_sb[:, j0 // 16 : j1 // 16]))
@@ -254,39 +244,35 @@ def tile_list_pairwise_state_correction_kernel(
             )
 
         def saturate(t, j0, j1):
-            nc.scalar.activation(th_of(t, j0, j1), d_of(t, j0, j1), ACT.Tanh, scale=-1.0)
-
-        def squash(t, j0, j1):
-            saturate(t, j0, j1)
-            apply_gain(t, j0, j1)
+            nc.scalar.activation(tanh_of(t, j0, j1), d_of(t, j0, j1), ACT.Tanh, scale=-1.0)
 
         def apply_gain(t, j0, j1):
             nc.scalar.activation(
-                flat(planes_of(t, t + 1, j0, j1)), th_of(t, j0, j1), ACT.Copy, scale=gain_sb[:, t : t + 1]
+                flat(planes_of(t, t + 1, j0, j1)), tanh_of(t, j0, j1), ACT.Copy, scale=gain_sb[:, t : t + 1]
             )
 
         def interleave(j0, j1):
             nc.scalar.copy(
-                z_of(j0, j1).rearrange("p (c i) t -> p c t i", i=4),
+                z_words[:, j0:j1, :].rearrange("p (c i) t -> p c t i", i=4),
                 planes_of(0, PACK, j0, j1).rearrange("p t (c i) -> p c t i", i=4),
             )
 
-        def quant_z(j0, j1):
+        def quantise_z(j0, j1):
             nc.vector.quantize_mx(
                 out=z_codes[:, j0:j1].bitcast(FP8X4),
                 scales=z_scales[:, j0:j1],
-                in_=z_of(j0, j1).rearrange("p n t -> p (n t)"),
+                in_=z_words[:, j0:j1, :].rearrange("p n t -> p (n t)"),
             )
 
-        ybanks = {}
+        y_banks = {}
 
         def correct(j0, j1, t0, t1, bank):
-            ybanks[(j0, t0)] = psum.tile([P, t1 - t0, j1 - j0], F32, name="bank%d" % bank)
+            y_banks[(j0, t0)] = psum.tile([P, t1 - t0, j1 - j0], F32, name="bank%d" % bank)
             for t in range(t0, t1):
                 nc.tensor.matmul_mx(
-                    out=ybanks[(j0, t0)][:, t - t0, :],
+                    out=y_banks[(j0, t0)][:, t - t0, :],
                     lhsT=w2_codes[:, t, :].bitcast(FP4X4),
-                    lhsT_scale=w2_sc[:, t, :],
+                    lhsT_scale=w2_scale_bytes[:, t, :],
                     rhs=z_codes[:, j0:j1].bitcast(FP8X4),
                     rhs_scale=z_scales[:, j0:j1],
                     start=True,
@@ -294,50 +280,52 @@ def tile_list_pairwise_state_correction_kernel(
                 )
 
         def finish(j0, j1, t0, t1):
-            dst = o_sb[:, t0:t1, j0:j1]
-            if (j0, t0) == (0, PACK - 1):
-                dst = o_late[:]
-            nc.vector.tensor_tensor(dst, ybanks[(j0, t0)][:], a_of(t0, t1, j0, j1), ALU.add)
-            nc.sync.dma_start(out=out_v[:, t0:t1, j0:j1], in_=dst)
+            rows = result[:, t0:t1, j0:j1]
+            nc.vector.tensor_tensor(rows, y_banks[(j0, t0)][:], a_of(t0, t1, j0, j1), ALU.add)
+            nc.sync.dma_start(out=out_rows[:, t0:t1, j0:j1], in_=rows)
 
-        HALF = WIDE + P
+        pieces = [(j0, j0 + PIECE) for j0 in range(0, WIDE, PIECE)]
         for t in range(PACK):
-            pick_a(t, 0, CHUNK)
-            pick_a(t, CHUNK, WIDE)
-            pick_d(t, 0, CHUNK)
-            pick_d(t, CHUNK, WIDE)
+            for pick in (pick_a, pick_d):
+                for j0, j1 in pieces:
+                    pick(t, j0, j1)
         for t in range(PACK - 1):
-            squash(t, 0, WIDE)
-        for j0 in (0, CHUNK):
-            squash(PACK - 1, j0, j0 + CHUNK)
-        for j0 in (0, CHUNK):
-            interleave(j0, j0 + CHUNK)
-        for t in range(2):
-            pick_a(t, WIDE, NP)
-        for t in range(2):
-            pick_d(t, WIDE, NP)
+            saturate(t, 0, WIDE)
+            apply_gain(t, 0, WIDE)
+        for j0, j1 in pieces:
+            saturate(PACK - 1, j0, j1)
+            apply_gain(PACK - 1, j0, j1)
+        for j0, j1 in pieces:
+            interleave(j0, j1)
+
+        halves = [(WIDE, HALF), (HALF, NP)]
+        for pick in (pick_a, pick_d):
+            for t in range(2):
+                pick(t, WIDE, NP)
         for t in range(2, PACK):
             pick_a(t, WIDE, NP)
-        pick_d(2, WIDE, NP)
-        quant_z(0, WIDE)
+        quantise_z(0, WIDE)
         for t in range(PACK):
-            correct(0, WIDE, t, t + 1, 4 + t)
-        pick_d(3, WIDE, HALF)
-        pick_d(3, HALF, NP)
+            correct(0, WIDE, t, t + 1, BANKS - PACK + t)
+        pick_d(2, WIDE, NP)
+        for j0, j1 in halves:
+            pick_d(PACK - 1, j0, j1)
         for t in range(PACK - 1):
-            squash(t, WIDE, NP)
+            saturate(t, WIDE, NP)
+            apply_gain(t, WIDE, NP)
         for step in (saturate, apply_gain):
-            step(PACK - 1, WIDE, HALF)
-            step(PACK - 1, HALF, NP)
-        interleave(WIDE, HALF)
-        interleave(HALF, NP)
-        quant_z(WIDE, HALF)
-        correct(WIDE, HALF, 0, 4, 0)
-        quant_z(HALF, NP)
+            for j0, j1 in halves:
+                step(PACK - 1, j0, j1)
+        for j0, j1 in halves:
+            interleave(j0, j1)
+
+        quantise_z(WIDE, HALF)
+        correct(WIDE, HALF, 0, PACK, 0)
+        quantise_z(HALF, NP)
         correct(HALF, NP, 0, 2, 1)
-        correct(HALF, NP, 2, 4, 2)
+        correct(HALF, NP, 2, PACK, 2)
         for t in range(PACK):
             finish(0, WIDE, t, t + 1)
-        finish(WIDE, HALF, 0, 4)
+        finish(WIDE, HALF, 0, PACK)
         finish(HALF, NP, 0, 2)
-        finish(HALF, NP, 2, 4)
+        finish(HALF, NP, 2, PACK)

@@ -23,6 +23,7 @@ BLOCKS = 16
 QUAD = 32
 BANK = 512
 BANKS = 8
+H_BANKS = 2 * S // BANK
 SLICES = S // BANK
 WIDE = 512
 LAST = NP - WIDE
@@ -75,8 +76,6 @@ def tile_list_pairwise_state_correction_kernel(
 
         nc.sync.dma_start(out=scale_window[0:QUAD, :], in_=tab_scales.rearrange("g q n -> (g q) n").bitcast(I32))
         nc.sync.dma_start(offs_sb[:], offs)
-        nc.sync.dma_start(pos1_sb[:], pos1)
-        nc.sync.dma_start(pos2_sb[:], pos2)
         nc.sync.dma_start(out=w2_words_raw[:], in_=w2_words[0].bitcast(I32))
         load_words(0)
         for quad in range(P // QUAD):
@@ -86,6 +85,8 @@ def tile_list_pairwise_state_correction_kernel(
             )
         load_w1(0)
         load_words(1)
+        nc.sync.dma_start(pos1_sb[:], pos1)
+        nc.sync.dma_start(pos2_sb[:], pos2)
 
         picked_scales = shared.tile([P, S // 4], I32, name="picked_scales", align_bytes=64, offset=AT_PICKED_SCALES)
         v_words = [keep.tile([P, S], U32, name="v_words%d" % g, align_bytes=64) for g in range(PASSES)]
@@ -110,11 +111,14 @@ def tile_list_pairwise_state_correction_kernel(
         w1_codes = [keep.tile([P, H], U32, name="w1_codes%d" % g, align_bytes=64) for g in range(PASSES)]
         w1_scales = keep.tile([P, PASSES, H], U8, name="w1_scales", align_bytes=64)
 
-        def round_w1(copy, rounded, g, t0, t1):
+        def round_w1(copy, rounded, g, t0, t1, m0=0, m1=P):
             copy(
-                rounded[:].rearrange("p t m j -> p m j t"),
-                w1_raw[g][:].rearrange("p j (m t) -> p m j t", t=PACK)[:, :, :, t0:t1],
+                rounded[:].rearrange("p t m j -> p m j t")[:, m0:m1, :, :],
+                w1_raw[g][:].rearrange("p j (m t) -> p m j t", t=PACK)[:, m0:m1, :, t0:t1],
             )
+
+        def gpsimd_round(dst, src):
+            nc.gpsimd.tensor_scalar(dst, src, 1.0, 0.0, ALU.mult, ALU.add)
 
         def quantise_w1(rounded, g, t0, t1):
             nc.vector.quantize_mx(
@@ -143,7 +147,7 @@ def tile_list_pairwise_state_correction_kernel(
 
         def h_pass(t, s, g):
             if g == 0:
-                h_banks[(t, s)] = psum.tile([P, BANK], F32, name="bank%d" % (groups.index((t, s)) % BANKS))
+                h_banks[(t, s)] = psum.tile([P, BANK], F32, name="bank%d" % (groups.index((t, s)) % H_BANKS))
             cols = slice(s * BANK, (s + 1) * BANK)
             nc.tensor.matmul_mx(
                 out=h_banks[(t, s)][:],
@@ -159,20 +163,23 @@ def tile_list_pairwise_state_correction_kernel(
             copy = nc.vector.tensor_copy if (t, s) == (0, 1) else nc.scalar.copy
             copy(h[t][:, s * BANK : (s + 1) * BANK], h_banks[(t, s)][:])
 
-        for t, s in groups[:BANKS]:
+        for t, s in groups[:H_BANKS]:
             h_pass(t, s, 0)
         gather_words(1)
-        for t0, t1, copy, rounded in (
-            (0, 1, nc.scalar.copy, shared.tile([P, 1, P, PACK], BF16, name="rounded1_0", align_bytes=64, offset=AT_ROUNDED)),
-            (1, 2, nc.scalar.copy, keep.tile([P, 1, P, PACK], BF16, name="rounded1_1", align_bytes=64)),
-            (2, 4, nc.vector.tensor_copy, shared.tile([P, 2, P, PACK], BF16, name="rounded1_23", align_bytes=64, offset=AT_ROUNDED)),
-        ):
-            round_w1(copy, rounded, 1, t0, t1)
-            quantise_w1(rounded, 1, t0, t1)
-        for t, s in groups[:BANKS]:
+        rounded1_0 = shared.tile([P, 1, P, PACK], BF16, name="rounded1_0", align_bytes=64, offset=AT_ROUNDED)
+        round_w1(nc.scalar.copy, rounded1_0, 1, 0, 1, 0, P // 2)
+        round_w1(gpsimd_round, rounded1_0, 1, 0, 1, P // 2, P)
+        quantise_w1(rounded1_0, 1, 0, 1)
+        rounded1_1 = keep.tile([P, 1, P, PACK], BF16, name="rounded1_1", align_bytes=64)
+        rounded1_23 = shared.tile([P, 2, P, PACK], BF16, name="rounded1_23", align_bytes=64, offset=AT_ROUNDED)
+        round_w1(nc.scalar.copy, rounded1_1, 1, 1, 2)
+        quantise_w1(rounded1_1, 1, 1, 2)
+        round_w1(nc.vector.tensor_copy, rounded1_23, 1, 2, PACK)
+        quantise_w1(rounded1_23, 1, 2, PACK)
+        for t, s in groups[:H_BANKS]:
             h_pass(t, s, 1)
             empty_bank(t, s)
-        for t, s in groups[BANKS:]:
+        for t, s in groups[H_BANKS:]:
             h_pass(t, s, 0)
             h_pass(t, s, 1)
             empty_bank(t, s)

@@ -33,7 +33,12 @@ PIECE = 256
 AT_SCALE_WINDOW = 0
 AT_PICKED_SCALES = 8192
 AT_ROUNDED = 10240
-AT_WIDE_PLANES = 12288
+AT_LATE_WORDS = 16384
+RING = 4
+AT_PLANES_A = 13312
+AT_D_WIDE2 = 22528
+AT_PLANES_B = 26624
+AT_PLANES_C = 29696
 
 
 def tile_list_pairwise_state_correction_kernel(
@@ -89,7 +94,10 @@ def tile_list_pairwise_state_correction_kernel(
         nc.sync.dma_start(pos2_sb[:], pos2)
 
         picked_scales = shared.tile([P, S // 4], I32, name="picked_scales", align_bytes=64, offset=AT_PICKED_SCALES)
-        v_words = [keep.tile([P, S], U32, name="v_words%d" % g, align_bytes=64) for g in range(PASSES)]
+        v_words = [
+            keep.tile([P, S], U32, name="v_words0", align_bytes=64),
+            shared.tile([P, S], U32, name="v_words1", align_bytes=64, offset=AT_LATE_WORDS),
+        ]
         nc.vector.tensor_copy(picked_scales[:].bitcast(U8), scale_window[:].bitcast(U8).indirect(offs_sb[:]))
 
         def carry_scales(g):
@@ -147,7 +155,9 @@ def tile_list_pairwise_state_correction_kernel(
 
         def h_pass(t, s, g):
             if g == 0:
-                h_banks[(t, s)] = psum.tile([P, BANK], F32, name="bank%d" % (groups.index((t, s)) % H_BANKS))
+                i = groups.index((t, s))
+                bank = i if i < H_BANKS else H_BANKS - RING + (i - H_BANKS) % RING
+                h_banks[(t, s)] = psum.tile([P, BANK], F32, name="bank%d" % bank)
             cols = slice(s * BANK, (s + 1) * BANK)
             nc.tensor.matmul_mx(
                 out=h_banks[(t, s)][:],
@@ -186,24 +196,45 @@ def tile_list_pairwise_state_correction_kernel(
 
         row_bytes = 4 * LAST
 
-        def row_on_wide_planes(name, place):
-            return shared.tile([P, LAST], F32, name=name, align_bytes=64, offset=AT_WIDE_PLANES + place * row_bytes)
+        def on(name, shape, dtype, offset):
+            return shared.tile(shape, dtype, name=name, align_bytes=64, offset=offset)
+
+        def row_on(name, planes_at, place):
+            return on(name, [P, LAST], F32, planes_at + place * row_bytes - 3 * row_bytes // 4)
 
         a_wide = keep.tile([P, PACK, WIDE], F32, name="a_wide")
-        d_wide = keep.tile([P, PACK, WIDE], F32, name="d_wide")
-        tanh_wide0 = keep.tile([P, WIDE], F32, name="tanh_wide0")
-        ring = keep.tile([P, PACK, LAST], F32, name="ring")
-        z_planes_wide = shared.tile([P, PACK, WIDE], BF16, name="z_planes_wide", align_bytes=64, offset=AT_WIDE_PLANES)
-        z_planes_last = keep.tile([P, PACK, LAST], BF16, name="z_planes_last")
+        a_last = keep.tile([P, PACK, LAST], F32, name="a_last")
+        d_wide = [
+            keep.tile([P, WIDE], F32, name="d_wide0"),
+            on("d_wide1", [P, WIDE], F32, AT_LATE_WORDS),
+            on("d_wide2", [P, WIDE], F32, AT_D_WIDE2),
+            keep.tile([P, WIDE], F32, name="d_wide3"),
+        ]
+        early_tanh = a_last[:].rearrange("p t n -> p (t n)")[:, 3 * LAST // 2 : 3 * LAST // 2 + WIDE]
+        tanh_wide = [
+            early_tanh,
+            early_tanh,
+            on("tanh_wide2", [P, WIDE], F32, AT_LATE_WORDS)[:],
+            on("tanh_wide3", [P, WIDE], F32, AT_D_WIDE2)[:],
+        ]
+        planes_wide = [
+            on("planes_a", [P, PACK, PIECE], BF16, AT_PLANES_A),
+            on("planes_b", [P, PACK, PIECE], BF16, AT_PLANES_B),
+        ]
+        planes_last = [
+            on("planes_c", [P, PACK, P], BF16, AT_PLANES_C),
+            keep.tile([P, PACK, P], BF16, name="planes_d"),
+        ]
+        result_wide3 = on("result_wide3", [P, 1, WIDE], F32, AT_PLANES_C)
         d_last = [
-            keep.tile([P, LAST], F32, name="d_last0"),
+            row_on("d_last0", AT_PLANES_A, 0),
             keep.tile([P, LAST], F32, name="d_last1"),
-            row_on_wide_planes("d_last2", 2),
-            row_on_wide_planes("d_last3", 3),
+            row_on("d_last2", AT_PLANES_A, 1),
+            row_on("d_last3", AT_PLANES_B, 0),
         ]
         tanh_last = [
-            row_on_wide_planes("tanh_last0", 0),
-            row_on_wide_planes("tanh_last1", 1),
+            keep.tile([P, LAST], F32, name="tanh_last0"),
+            row_on("tanh_last1", AT_PLANES_A, 2),
             keep.tile([P, LAST], F32, name="tanh_last2"),
             keep.tile([P, LAST], F32, name="tanh_last3"),
         ]
@@ -219,25 +250,22 @@ def tile_list_pairwise_state_correction_kernel(
         def a_of(t0, t1, j0, j1):
             if j0 < WIDE:
                 return a_wide[:, t0:t1, j0:j1]
-            return ring[:, t0:t1, j0 - WIDE : j1 - WIDE]
+            return a_last[:, t0:t1, j0 - WIDE : j1 - WIDE]
 
         def d_of(t, j0, j1):
             if j0 < WIDE:
-                return d_wide[:, t, j0:j1]
+                return d_wide[t][:, j0:j1]
             return d_last[t][:, j0 - WIDE : j1 - WIDE]
 
         def tanh_of(t, j0, j1):
-            if j0 >= WIDE:
-                return tanh_last[t][:, j0 - WIDE : j1 - WIDE]
-            if t == 0:
-                return tanh_wide0[:, j0:j1]
-            row = 0 if t == 1 else 2
-            return flat(ring[:, row : row + 2, :])[:, j0:j1]
+            if j0 < WIDE:
+                return tanh_wide[t][:, j0:j1]
+            return tanh_last[t][:, j0 - WIDE : j1 - WIDE]
 
         def planes_of(t0, t1, j0, j1):
             if j0 < WIDE:
-                return z_planes_wide[:, t0:t1, j0:j1]
-            return z_planes_last[:, t0:t1, j0 - WIDE : j1 - WIDE]
+                return planes_wide[j0 // PIECE][:, t0:t1, :]
+            return planes_last[(j0 - WIDE) // P][:, t0:t1, :]
 
         def pick_a(t, j0, j1):
             nc.vector.tensor_copy(flat(a_of(t, t + 1, j0, j1)), h[t][:].indirect(pos1_sb[:, j0 // 16 : j1 // 16]))
@@ -273,11 +301,13 @@ def tile_list_pairwise_state_correction_kernel(
 
         y_banks = {}
 
-        def correct(j0, j1, t0, t1, bank):
+        def open_bank(j0, j1, t0, t1, bank):
             y_banks[(j0, t0)] = psum.tile([P, t1 - t0, j1 - j0], F32, name="bank%d" % bank)
+
+        def correct(bank_j0, t0, t1, j0, j1):
             for t in range(t0, t1):
                 nc.tensor.matmul_mx(
-                    out=y_banks[(j0, t0)][:, t - t0, :],
+                    out=y_banks[(bank_j0, t0)][:, t - t0, j0 - bank_j0 : j1 - bank_j0],
                     lhsT=w2_codes[:, t, :].bitcast(FP4X4),
                     lhsT_scale=w2_scale_bytes[:, t, :],
                     rhs=z_codes[:, j0:j1].bitcast(FP8X4),
@@ -287,52 +317,63 @@ def tile_list_pairwise_state_correction_kernel(
                 )
 
         def finish(j0, j1, t0, t1):
-            rows = result[:, t0:t1, j0:j1]
+            rows = result_wide3[:] if (j0, t0) == (0, PACK - 1) else result[:, t0:t1, j0:j1]
             nc.vector.tensor_tensor(rows, y_banks[(j0, t0)][:], a_of(t0, t1, j0, j1), ALU.add)
             nc.sync.dma_start(out=out_rows[:, t0:t1, j0:j1], in_=rows)
 
         pieces = [(j0, j0 + PIECE) for j0 in range(0, WIDE, PIECE)]
-        for t in range(PACK):
-            for pick in (pick_a, pick_d):
-                for j0, j1 in pieces:
-                    pick(t, j0, j1)
+        halves = [(WIDE, HALF), (HALF, NP)]
+        pick_a(0, 0, WIDE)
+        pick_a(0, WIDE, NP)
+        pick_d(0, 0, WIDE)
+        for pick in (pick_a, pick_d):
+            for t in (1, 2):
+                pick(t, 0, WIDE)
+        for pick in (pick_a, pick_d):
+            for j0, j1 in pieces:
+                pick(PACK - 1, j0, j1)
         for t in range(PACK - 1):
             saturate(t, 0, WIDE)
-            apply_gain(t, 0, WIDE)
-        for j0, j1 in pieces:
-            saturate(PACK - 1, j0, j1)
-            apply_gain(PACK - 1, j0, j1)
+            for j0, j1 in pieces:
+                apply_gain(t, j0, j1)
+        for step in (saturate, apply_gain):
+            for j0, j1 in pieces:
+                step(PACK - 1, j0, j1)
         for j0, j1 in pieces:
             interleave(j0, j1)
 
-        halves = [(WIDE, HALF), (HALF, NP)]
-        for pick in (pick_a, pick_d):
-            for t in range(2):
-                pick(t, WIDE, NP)
-        for t in range(2, PACK):
-            pick_a(t, WIDE, NP)
-        quantise_z(0, WIDE)
+        pick_a(1, WIDE, NP)
+        pick_a(2, WIDE, NP)
+        pick_d(1, WIDE, NP)
+        pick_a(3, WIDE, NP)
+        quantise_z(*pieces[0])
         for t in range(PACK):
-            correct(0, WIDE, t, t + 1, BANKS - PACK + t)
+            open_bank(0, WIDE, t, t + 1, BANKS - PACK + t)
+            correct(0, t, t + 1, *pieces[0])
+        pick_d(0, WIDE, NP)
         pick_d(2, WIDE, NP)
+        quantise_z(*pieces[1])
+        for t in range(PACK):
+            correct(0, t, t + 1, *pieces[1])
         for j0, j1 in halves:
             pick_d(PACK - 1, j0, j1)
-        for t in range(PACK - 1):
+        for t in (1, 0, 2):
             saturate(t, WIDE, NP)
-            apply_gain(t, WIDE, NP)
+            for j0, j1 in halves:
+                apply_gain(t, j0, j1)
         for step in (saturate, apply_gain):
             for j0, j1 in halves:
                 step(PACK - 1, j0, j1)
         for j0, j1 in halves:
             interleave(j0, j1)
 
-        quantise_z(WIDE, HALF)
-        correct(WIDE, HALF, 0, PACK, 0)
-        quantise_z(HALF, NP)
-        correct(HALF, NP, 0, 2, 1)
-        correct(HALF, NP, 2, PACK, 2)
+        for i, (j0, j1) in enumerate(halves):
+            quantise_z(j0, j1)
+            for t in (0, 2):
+                open_bank(j0, j1, t, t + 2, 2 * i + t // 2)
+                correct(j0, t, t + 2, j0, j1)
         for t in range(PACK):
             finish(0, WIDE, t, t + 1)
-        finish(WIDE, HALF, 0, PACK)
-        finish(HALF, NP, 0, 2)
-        finish(HALF, NP, 2, PACK)
+        for j0, j1 in halves:
+            for t in (0, 2):
+                finish(j0, j1, t, t + 2)

@@ -35,6 +35,7 @@ AT_PICKED_SCALES = 8192
 AT_ROUNDED = 10240
 AT_LATE_WORDS = 16384
 RING = 4
+SCALAR_SHARE = 96
 AT_PLANES_A = 13312
 AT_D_WIDE2 = 22528
 AT_PLANES_B = 26624
@@ -75,14 +76,14 @@ def tile_list_pairwise_state_correction_kernel(
         def load_words(g):
             nc.sync.dma_start(out=words[g][:], in_=tab_words[g].rearrange("p n i -> p (n i)").bitcast(I32))
 
-        def load_w1(g):
-            rows = w1[g * P * PACK : (g + 1) * P * PACK, :]
-            nc.sync.dma_start(out=w1_raw[g][:], in_=rows.rearrange("(p j) c -> p j c", j=PACK))
+        def load_w1(g, j0=0, j1=PACK):
+            rows = w1[g * P * PACK : (g + 1) * P * PACK, :].rearrange("(p j) c -> p j c", j=PACK)
+            nc.sync.dma_start(out=w1_raw[g][:, j0:j1, :], in_=rows[:, j0:j1, :])
 
         nc.sync.dma_start(out=scale_window[0:QUAD, :], in_=tab_scales.rearrange("g q n -> (g q) n").bitcast(I32))
         nc.sync.dma_start(offs_sb[:], offs)
-        nc.sync.dma_start(out=w2_words_raw[:], in_=w2_words[0].bitcast(I32))
         load_words(0)
+        nc.sync.dma_start(out=w2_words_raw[:], in_=w2_words[0].bitcast(I32))
         for quad in range(P // QUAD):
             nc.sync.dma_start(
                 out=w2_scales_raw[QUAD * quad : QUAD * quad + 4, :],
@@ -90,8 +91,6 @@ def tile_list_pairwise_state_correction_kernel(
             )
         load_w1(0)
         load_words(1)
-        nc.sync.dma_start(pos1_sb[:], pos1)
-        nc.sync.dma_start(pos2_sb[:], pos2)
 
         picked_scales = shared.tile([P, S // 4], I32, name="picked_scales", align_bytes=64, offset=AT_PICKED_SCALES)
         v_words = [
@@ -111,18 +110,21 @@ def tile_list_pairwise_state_correction_kernel(
             nc.vector.tensor_copy(v_words[g][:], words[g][:].bitcast(U32).indirect(offs_sb[:]))
 
         carry_scales(0)
-        load_w1(1)
+        load_w1(1, 0, 2)
+        load_w1(1, 2, PACK)
         carry_scales(1)
+        nc.sync.dma_start(pos1_sb[:], pos1)
+        nc.sync.dma_start(pos2_sb[:], pos2)
         nc.sync.dma_start(out=gain_sb[:], in_=gain.rearrange("(p t) -> p t", t=PACK))
         gather_words(0)
 
         w1_codes = [keep.tile([P, H], U32, name="w1_codes%d" % g, align_bytes=64) for g in range(PASSES)]
         w1_scales = keep.tile([P, PASSES, H], U8, name="w1_scales", align_bytes=64)
 
-        def round_w1(copy, rounded, g, t0, t1, m0=0, m1=P):
+        def round_w1(copy, rounded, g, t0, t1, m0=0, m1=P, j0=0, j1=PACK):
             copy(
-                rounded[:].rearrange("p t m j -> p m j t")[:, m0:m1, :, :],
-                w1_raw[g][:].rearrange("p j (m t) -> p m j t", t=PACK)[:, m0:m1, :, t0:t1],
+                rounded[:].rearrange("p t m j -> p m j t")[:, m0:m1, j0:j1, :],
+                w1_raw[g][:].rearrange("p j (m t) -> p m j t", t=PACK)[:, m0:m1, j0:j1, t0:t1],
             )
 
         def gpsimd_round(dst, src):
@@ -177,8 +179,9 @@ def tile_list_pairwise_state_correction_kernel(
             h_pass(t, s, 0)
         gather_words(1)
         rounded1_0 = shared.tile([P, 1, P, PACK], BF16, name="rounded1_0", align_bytes=64, offset=AT_ROUNDED)
-        round_w1(nc.scalar.copy, rounded1_0, 1, 0, 1, 0, P // 2)
-        round_w1(gpsimd_round, rounded1_0, 1, 0, 1, P // 2, P)
+        round_w1(nc.scalar.copy, rounded1_0, 1, 0, 1, 0, P, 0, 2)
+        round_w1(nc.scalar.copy, rounded1_0, 1, 0, 1, 0, SCALAR_SHARE, 2, PACK)
+        round_w1(gpsimd_round, rounded1_0, 1, 0, 1, SCALAR_SHARE, P, 2, PACK)
         quantise_w1(rounded1_0, 1, 0, 1)
         rounded1_1 = keep.tile([P, 1, P, PACK], BF16, name="rounded1_1", align_bytes=64)
         rounded1_23 = shared.tile([P, 2, P, PACK], BF16, name="rounded1_23", align_bytes=64, offset=AT_ROUNDED)
@@ -221,11 +224,8 @@ def tile_list_pairwise_state_correction_kernel(
             on("planes_a", [P, PACK, PIECE], BF16, AT_PLANES_A),
             on("planes_b", [P, PACK, PIECE], BF16, AT_PLANES_B),
         ]
-        planes_last = [
-            on("planes_c", [P, PACK, P], BF16, AT_PLANES_C),
-            keep.tile([P, PACK, P], BF16, name="planes_d"),
-        ]
-        result_wide3 = on("result_wide3", [P, 1, WIDE], F32, AT_PLANES_C)
+        planes_last = on("planes_last", [P, PACK, LAST], BF16, AT_PLANES_C)
+        result_held = on("result_held", [P, 1, PIECE], F32, AT_PLANES_C)
         d_last = [
             row_on("d_last0", AT_PLANES_A, 0),
             keep.tile([P, LAST], F32, name="d_last1"),
@@ -236,8 +236,9 @@ def tile_list_pairwise_state_correction_kernel(
             keep.tile([P, LAST], F32, name="tanh_last0"),
             row_on("tanh_last1", AT_PLANES_A, 2),
             keep.tile([P, LAST], F32, name="tanh_last2"),
-            keep.tile([P, LAST], F32, name="tanh_last3"),
+            keep.tile([P, P], F32, name="tanh_last3"),
         ]
+        tanh_end = on("tanh_end", [P, P], F32, AT_PLANES_A + row_bytes // 4)
         z_words = keep.tile([P, NP, PACK], BF16, name="z_words", align_bytes=64)
         z_codes = keep.tile([P, NP], U32, name="z_codes", align_bytes=64)
         z_scales = keep.tile([P, NP], U8, name="z_scales", align_bytes=64)
@@ -260,12 +261,14 @@ def tile_list_pairwise_state_correction_kernel(
         def tanh_of(t, j0, j1):
             if j0 < WIDE:
                 return tanh_wide[t][:, j0:j1]
+            if j0 == HALF:
+                return tanh_end[:]
             return tanh_last[t][:, j0 - WIDE : j1 - WIDE]
 
         def planes_of(t0, t1, j0, j1):
             if j0 < WIDE:
                 return planes_wide[j0 // PIECE][:, t0:t1, :]
-            return planes_last[(j0 - WIDE) // P][:, t0:t1, :]
+            return planes_last[:, t0:t1, j0 - WIDE : j1 - WIDE]
 
         def pick_a(t, j0, j1):
             nc.vector.tensor_copy(flat(a_of(t, t + 1, j0, j1)), h[t][:].indirect(pos1_sb[:, j0 // 16 : j1 // 16]))
@@ -286,8 +289,8 @@ def tile_list_pairwise_state_correction_kernel(
                 flat(planes_of(t, t + 1, j0, j1)), tanh_of(t, j0, j1), ACT.Copy, scale=gain_sb[:, t : t + 1]
             )
 
-        def interleave(j0, j1):
-            nc.scalar.copy(
+        def interleave(j0, j1, copy=nc.scalar.copy):
+            copy(
                 z_words[:, j0:j1, :].rearrange("p (c i) t -> p c t i", i=4),
                 planes_of(0, PACK, j0, j1).rearrange("p t (c i) -> p c t i", i=4),
             )
@@ -317,8 +320,10 @@ def tile_list_pairwise_state_correction_kernel(
                 )
 
         def finish(j0, j1, t0, t1):
-            rows = result_wide3[:] if (j0, t0) == (0, PACK - 1) else result[:, t0:t1, j0:j1]
-            nc.vector.tensor_tensor(rows, y_banks[(j0, t0)][:], a_of(t0, t1, j0, j1), ALU.add)
+            rows = result_held[:] if j0 == PIECE else result[:, t0:t1, j0:j1]
+            bank_j0 = j0 // WIDE * WIDE
+            y = y_banks[(bank_j0, t0)][:, :, j0 - bank_j0 : j1 - bank_j0]
+            nc.vector.tensor_tensor(rows, y, a_of(t0, t1, j0, j1), ALU.add)
             nc.sync.dma_start(out=out_rows[:, t0:t1, j0:j1], in_=rows)
 
         pieces = [(j0, j0 + PIECE) for j0 in range(0, WIDE, PIECE)]
@@ -359,21 +364,20 @@ def tile_list_pairwise_state_correction_kernel(
             pick_d(PACK - 1, j0, j1)
         for t in (1, 0, 2):
             saturate(t, WIDE, NP)
-            for j0, j1 in halves:
-                apply_gain(t, j0, j1)
+            apply_gain(t, WIDE, NP)
         for step in (saturate, apply_gain):
             for j0, j1 in halves:
                 step(PACK - 1, j0, j1)
-        for j0, j1 in halves:
-            interleave(j0, j1)
+        gpsimd_round(z_words[:, WIDE:HALF, :], planes_of(0, PACK, WIDE, HALF).rearrange("p t n -> p n t"))
+        interleave(*halves[1])
 
-        for i, (j0, j1) in enumerate(halves):
-            quantise_z(j0, j1)
-            for t in (0, 2):
-                open_bank(j0, j1, t, t + 2, 2 * i + t // 2)
-                correct(j0, t, t + 2, j0, j1)
+        quantise_z(WIDE, NP)
         for t in range(PACK):
+            open_bank(WIDE, NP, t, t + 1, t)
+            correct(WIDE, t, t + 1, WIDE, NP)
+        for t in range(PACK - 1):
             finish(0, WIDE, t, t + 1)
-        for j0, j1 in halves:
-            for t in (0, 2):
-                finish(j0, j1, t, t + 2)
+        for j0, j1 in pieces:
+            finish(j0, j1, PACK - 1, PACK)
+        for t in range(PACK):
+            finish(WIDE, NP, t, t + 1)

@@ -224,8 +224,11 @@ def tile_list_pairwise_state_correction_kernel(
             on("planes_a", [P, PACK, PIECE], BF16, AT_PLANES_A),
             on("planes_b", [P, PACK, PIECE], BF16, AT_PLANES_B),
         ]
-        planes_last = on("planes_last", [P, PACK, LAST], BF16, AT_PLANES_C)
-        result_held = on("result_held", [P, 1, PIECE], F32, AT_PLANES_C)
+        planes_last = [
+            on("planes_c", [P, PACK, P], BF16, AT_PLANES_C),
+            keep.tile([P, PACK, P], BF16, name="planes_d"),
+        ]
+        result_wide3 = on("result_wide3", [P, 1, WIDE], F32, AT_PLANES_C)
         d_last = [
             row_on("d_last0", AT_PLANES_A, 0),
             keep.tile([P, LAST], F32, name="d_last1"),
@@ -236,9 +239,8 @@ def tile_list_pairwise_state_correction_kernel(
             keep.tile([P, LAST], F32, name="tanh_last0"),
             row_on("tanh_last1", AT_PLANES_A, 2),
             keep.tile([P, LAST], F32, name="tanh_last2"),
-            keep.tile([P, P], F32, name="tanh_last3"),
+            keep.tile([P, LAST], F32, name="tanh_last3"),
         ]
-        tanh_end = on("tanh_end", [P, P], F32, AT_PLANES_A + row_bytes // 4)
         z_words = keep.tile([P, NP, PACK], BF16, name="z_words", align_bytes=64)
         z_codes = keep.tile([P, NP], U32, name="z_codes", align_bytes=64)
         z_scales = keep.tile([P, NP], U8, name="z_scales", align_bytes=64)
@@ -261,14 +263,12 @@ def tile_list_pairwise_state_correction_kernel(
         def tanh_of(t, j0, j1):
             if j0 < WIDE:
                 return tanh_wide[t][:, j0:j1]
-            if j0 == HALF:
-                return tanh_end[:]
             return tanh_last[t][:, j0 - WIDE : j1 - WIDE]
 
         def planes_of(t0, t1, j0, j1):
             if j0 < WIDE:
                 return planes_wide[j0 // PIECE][:, t0:t1, :]
-            return planes_last[:, t0:t1, j0 - WIDE : j1 - WIDE]
+            return planes_last[(j0 - WIDE) // P][:, t0:t1, :]
 
         def pick_a(t, j0, j1):
             nc.vector.tensor_copy(flat(a_of(t, t + 1, j0, j1)), h[t][:].indirect(pos1_sb[:, j0 // 16 : j1 // 16]))
@@ -289,8 +289,8 @@ def tile_list_pairwise_state_correction_kernel(
                 flat(planes_of(t, t + 1, j0, j1)), tanh_of(t, j0, j1), ACT.Copy, scale=gain_sb[:, t : t + 1]
             )
 
-        def interleave(j0, j1, copy=nc.scalar.copy):
-            copy(
+        def interleave(j0, j1):
+            nc.scalar.copy(
                 z_words[:, j0:j1, :].rearrange("p (c i) t -> p c t i", i=4),
                 planes_of(0, PACK, j0, j1).rearrange("p t (c i) -> p c t i", i=4),
             )
@@ -320,10 +320,8 @@ def tile_list_pairwise_state_correction_kernel(
                 )
 
         def finish(j0, j1, t0, t1):
-            rows = result_held[:] if j0 == PIECE else result[:, t0:t1, j0:j1]
-            bank_j0 = j0 // WIDE * WIDE
-            y = y_banks[(bank_j0, t0)][:, :, j0 - bank_j0 : j1 - bank_j0]
-            nc.vector.tensor_tensor(rows, y, a_of(t0, t1, j0, j1), ALU.add)
+            rows = result_wide3[:] if (j0, t0) == (0, PACK - 1) else result[:, t0:t1, j0:j1]
+            nc.vector.tensor_tensor(rows, y_banks[(j0, t0)][:], a_of(t0, t1, j0, j1), ALU.add)
             nc.sync.dma_start(out=out_rows[:, t0:t1, j0:j1], in_=rows)
 
         pieces = [(j0, j0 + PIECE) for j0 in range(0, WIDE, PIECE)]
@@ -364,20 +362,21 @@ def tile_list_pairwise_state_correction_kernel(
             pick_d(PACK - 1, j0, j1)
         for t in (1, 0, 2):
             saturate(t, WIDE, NP)
-            apply_gain(t, WIDE, NP)
+            for j0, j1 in halves:
+                apply_gain(t, j0, j1)
         for step in (saturate, apply_gain):
             for j0, j1 in halves:
                 step(PACK - 1, j0, j1)
-        gpsimd_round(z_words[:, WIDE:HALF, :], planes_of(0, PACK, WIDE, HALF).rearrange("p t n -> p n t"))
-        interleave(*halves[1])
+        for j0, j1 in halves:
+            interleave(j0, j1)
 
-        quantise_z(WIDE, NP)
+        for i, (j0, j1) in enumerate(halves):
+            quantise_z(j0, j1)
+            for t in (0, 2):
+                open_bank(j0, j1, t, t + 2, 2 * i + t // 2)
+                correct(j0, t, t + 2, j0, j1)
         for t in range(PACK):
-            open_bank(WIDE, NP, t, t + 1, t)
-            correct(WIDE, t, t + 1, WIDE, NP)
-        for t in range(PACK - 1):
             finish(0, WIDE, t, t + 1)
-        for j0, j1 in pieces:
-            finish(j0, j1, PACK - 1, PACK)
-        for t in range(PACK):
-            finish(WIDE, NP, t, t + 1)
+        for j0, j1 in halves:
+            for t in (0, 2):
+                finish(j0, j1, t, t + 2)

@@ -23,23 +23,22 @@ BLOCKS = 16
 QUAD = 32
 BANK = 512
 BANKS = 8
-H_BANKS = 2 * S // BANK
 SLICES = S // BANK
+FIRST_BANKS = 2 * SLICES
+RING = SLICES + 1
 WIDE = 512
+PIECE = WIDE // 2
 LAST = NP - WIDE
 HALF = WIDE + P
-PIECE = 256
 
 AT_SCALE_WINDOW = 0
 AT_PICKED_SCALES = 8192
 AT_ROUNDED = 10240
+AT_PLANES_PIECE0 = 13312
 AT_LATE_WORDS = 16384
-RING = 4
-SCALAR_SHARE = 96
-AT_PLANES_A = 13312
 AT_D_WIDE2 = 22528
-AT_PLANES_B = 26624
-AT_PLANES_C = 29696
+AT_PLANES_PIECE1 = 26624
+AT_PLANES_HALF0 = 29696
 
 
 def tile_list_pairwise_state_correction_kernel(
@@ -76,7 +75,7 @@ def tile_list_pairwise_state_correction_kernel(
         def load_words(g):
             nc.sync.dma_start(out=words[g][:], in_=tab_words[g].rearrange("p n i -> p (n i)").bitcast(I32))
 
-        def load_w1(g, j0=0, j1=PACK):
+        def load_w1(g, j0, j1):
             rows = w1[g * P * PACK : (g + 1) * P * PACK, :].rearrange("(p j) c -> p j c", j=PACK)
             nc.sync.dma_start(out=w1_raw[g][:, j0:j1, :], in_=rows[:, j0:j1, :])
 
@@ -89,7 +88,7 @@ def tile_list_pairwise_state_correction_kernel(
                 out=w2_scales_raw[QUAD * quad : QUAD * quad + 4, :],
                 in_=w2_scales[0, 4 * quad : 4 * quad + 4, :].bitcast(I32),
             )
-        load_w1(0)
+        load_w1(0, 0, PACK)
         load_words(1)
 
         picked_scales = shared.tile([P, S // 4], I32, name="picked_scales", align_bytes=64, offset=AT_PICKED_SCALES)
@@ -110,8 +109,9 @@ def tile_list_pairwise_state_correction_kernel(
             nc.vector.tensor_copy(v_words[g][:], words[g][:].bitcast(U32).indirect(offs_sb[:]))
 
         carry_scales(0)
-        load_w1(1, 0, 2)
-        load_w1(1, 2, PACK)
+        w1_halves = [(0, PACK // 2), (PACK // 2, PACK)]
+        for j0, j1 in w1_halves:
+            load_w1(1, j0, j1)
         carry_scales(1)
         nc.sync.dma_start(pos1_sb[:], pos1)
         nc.sync.dma_start(pos2_sb[:], pos2)
@@ -121,14 +121,11 @@ def tile_list_pairwise_state_correction_kernel(
         w1_codes = [keep.tile([P, H], U32, name="w1_codes%d" % g, align_bytes=64) for g in range(PASSES)]
         w1_scales = keep.tile([P, PASSES, H], U8, name="w1_scales", align_bytes=64)
 
-        def round_w1(copy, rounded, g, t0, t1, m0=0, m1=P, j0=0, j1=PACK):
+        def round_w1(copy, rounded, g, t0, t1, j0=0, j1=PACK):
             copy(
-                rounded[:].rearrange("p t m j -> p m j t")[:, m0:m1, j0:j1, :],
-                w1_raw[g][:].rearrange("p j (m t) -> p m j t", t=PACK)[:, m0:m1, j0:j1, t0:t1],
+                rounded[:].rearrange("p t m j -> p m j t")[:, :, j0:j1, :],
+                w1_raw[g][:].rearrange("p j (m t) -> p m j t", t=PACK)[:, :, j0:j1, t0:t1],
             )
-
-        def gpsimd_round(dst, src):
-            nc.gpsimd.tensor_scalar(dst, src, 1.0, 0.0, ALU.mult, ALU.add)
 
         def quantise_w1(rounded, g, t0, t1):
             nc.vector.quantize_mx(
@@ -158,7 +155,7 @@ def tile_list_pairwise_state_correction_kernel(
         def h_pass(t, s, g):
             if g == 0:
                 i = groups.index((t, s))
-                bank = i if i < H_BANKS else H_BANKS - RING + (i - H_BANKS) % RING
+                bank = i if i < FIRST_BANKS else FIRST_BANKS - RING + (i - FIRST_BANKS) % RING
                 h_banks[(t, s)] = psum.tile([P, BANK], F32, name="bank%d" % bank)
             cols = slice(s * BANK, (s + 1) * BANK)
             nc.tensor.matmul_mx(
@@ -175,13 +172,12 @@ def tile_list_pairwise_state_correction_kernel(
             copy = nc.vector.tensor_copy if (t, s) == (0, 1) else nc.scalar.copy
             copy(h[t][:, s * BANK : (s + 1) * BANK], h_banks[(t, s)][:])
 
-        for t, s in groups[:H_BANKS]:
+        for t, s in groups[:FIRST_BANKS]:
             h_pass(t, s, 0)
         gather_words(1)
         rounded1_0 = shared.tile([P, 1, P, PACK], BF16, name="rounded1_0", align_bytes=64, offset=AT_ROUNDED)
-        round_w1(nc.scalar.copy, rounded1_0, 1, 0, 1, 0, P, 0, 2)
-        round_w1(nc.scalar.copy, rounded1_0, 1, 0, 1, 0, SCALAR_SHARE, 2, PACK)
-        round_w1(gpsimd_round, rounded1_0, 1, 0, 1, SCALAR_SHARE, P, 2, PACK)
+        for j0, j1 in w1_halves:
+            round_w1(nc.scalar.copy, rounded1_0, 1, 0, 1, j0, j1)
         quantise_w1(rounded1_0, 1, 0, 1)
         rounded1_1 = keep.tile([P, 1, P, PACK], BF16, name="rounded1_1", align_bytes=64)
         rounded1_23 = shared.tile([P, 2, P, PACK], BF16, name="rounded1_23", align_bytes=64, offset=AT_ROUNDED)
@@ -189,10 +185,10 @@ def tile_list_pairwise_state_correction_kernel(
         quantise_w1(rounded1_1, 1, 1, 2)
         round_w1(nc.vector.tensor_copy, rounded1_23, 1, 2, PACK)
         quantise_w1(rounded1_23, 1, 2, PACK)
-        for t, s in groups[:H_BANKS]:
+        for t, s in groups[:FIRST_BANKS]:
             h_pass(t, s, 1)
             empty_bank(t, s)
-        for t, s in groups[H_BANKS:]:
+        for t, s in groups[FIRST_BANKS:]:
             h_pass(t, s, 0)
             h_pass(t, s, 1)
             empty_bank(t, s)
@@ -221,23 +217,23 @@ def tile_list_pairwise_state_correction_kernel(
             on("tanh_wide3", [P, WIDE], F32, AT_D_WIDE2)[:],
         ]
         planes_wide = [
-            on("planes_a", [P, PACK, PIECE], BF16, AT_PLANES_A),
-            on("planes_b", [P, PACK, PIECE], BF16, AT_PLANES_B),
+            on("planes_piece0", [P, PACK, PIECE], BF16, AT_PLANES_PIECE0),
+            on("planes_piece1", [P, PACK, PIECE], BF16, AT_PLANES_PIECE1),
         ]
         planes_last = [
-            on("planes_c", [P, PACK, P], BF16, AT_PLANES_C),
-            keep.tile([P, PACK, P], BF16, name="planes_d"),
+            on("planes_half0", [P, PACK, P], BF16, AT_PLANES_HALF0),
+            keep.tile([P, PACK, P], BF16, name="planes_half1"),
         ]
-        result_wide3 = on("result_wide3", [P, 1, WIDE], F32, AT_PLANES_C)
+        result_wide3 = on("result_wide3", [P, 1, WIDE], F32, AT_PLANES_HALF0)
         d_last = [
-            row_on("d_last0", AT_PLANES_A, 0),
+            row_on("d_last0", AT_PLANES_PIECE0, 0),
             keep.tile([P, LAST], F32, name="d_last1"),
-            row_on("d_last2", AT_PLANES_A, 1),
-            row_on("d_last3", AT_PLANES_B, 0),
+            row_on("d_last2", AT_PLANES_PIECE0, 1),
+            row_on("d_last3", AT_PLANES_PIECE1, 0),
         ]
         tanh_last = [
             keep.tile([P, LAST], F32, name="tanh_last0"),
-            row_on("tanh_last1", AT_PLANES_A, 2),
+            row_on("tanh_last1", AT_PLANES_PIECE0, 2),
             keep.tile([P, LAST], F32, name="tanh_last2"),
             keep.tile([P, LAST], F32, name="tanh_last3"),
         ]
@@ -326,6 +322,7 @@ def tile_list_pairwise_state_correction_kernel(
 
         pieces = [(j0, j0 + PIECE) for j0 in range(0, WIDE, PIECE)]
         halves = [(WIDE, HALF), (HALF, NP)]
+
         pick_a(0, 0, WIDE)
         pick_a(0, WIDE, NP)
         pick_d(0, 0, WIDE)

@@ -55,8 +55,8 @@ def tile_list_pairwise_state_correction_kernel(
         pos1_sb = lists.tile([P, NP // 16], U16, name="pos1_sb")
         pos2_sb = lists.tile([P, NP // 16], U16, name="pos2_sb")
 
-        scale_window = shared.tile([P, T // 4], I32, name="scale_window", align_bytes=64, offset=AT_SCALE_WINDOW)
-        v_scales = [keep.tile([P, S // 4], I32, name="v_scales%d" % g, align_bytes=64) for g in range(PASSES)]
+        scale_window = shared.tile([P, T // 4], I32, name="scale_window", align_bytes=256, offset=AT_SCALE_WINDOW)
+        v_scales = [keep.tile([P, S // 4], I32, name="v_scales%d" % g, align_bytes=256) for g in range(PASSES)]
         w2_scales_raw = keep.tile([P, H // 4], I32, name="w2_scales_raw", align_bytes=64)
         nc.vector.memset(w2_scales_raw[:], 0)
         nc.vector.memset(scale_window[QUAD : 2 * QUAD, :], 0)
@@ -64,12 +64,12 @@ def tile_list_pairwise_state_correction_kernel(
         for g in range(PASSES):
             nc.vector.memset(v_scales[g][:], 0)
 
-        words = [keep.tile([P, T], I32, name="words%d" % g, align_bytes=64) for g in range(PASSES)]
+        words = [keep.tile([P, T], I32, name="words%d" % g, align_bytes=256) for g in range(PASSES)]
         w1_raw = [
-            keep.tile([P, PACK, H], F32, name="w1_raw0"),
-            shared.tile([P, PACK, H], F32, name="w1_raw1", align_bytes=64, offset=AT_SCALE_WINDOW),
+            keep.tile([P, PACK, H], F32, name="w1_raw0", align_bytes=256),
+            shared.tile([P, PACK, H], F32, name="w1_raw1", align_bytes=256, offset=AT_SCALE_WINDOW),
         ]
-        w2_words_raw = keep.tile([P, 2 * H // 4], I32, name="w2_words_raw")
+        w2_words_raw = keep.tile([P, 2 * H // 4], I32, name="w2_words_raw", align_bytes=256)
         gain_sb = shared.tile([P, PACK], F32, name="gain_sb", align_bytes=64, offset=AT_PICKED_SCALES)
 
         def load_words(g):
@@ -240,7 +240,7 @@ def tile_list_pairwise_state_correction_kernel(
         z_words = keep.tile([P, NP, PACK], BF16, name="z_words", align_bytes=64)
         z_codes = keep.tile([P, NP], U32, name="z_codes", align_bytes=64)
         z_scales = keep.tile([P, NP], U8, name="z_scales", align_bytes=64)
-        result = keep.tile([P, PACK, NP], F32, name="result")
+        result = keep.tile([P, PACK, NP], F32, name="result", align_bytes=256)
         out_rows = out.rearrange("(p t) j -> p t j", t=PACK)
 
         def flat(ap):

@@ -24,6 +24,7 @@ QUAD = 32
 BANK = 512
 BANKS = 8
 SLICES = S // BANK
+SPLIT = S - BANK // 2
 FIRST_BANKS = 2 * SLICES
 RING = SLICES + 1
 WIDE = 512
@@ -33,6 +34,9 @@ HALF = WIDE + P
 
 AT_SCALE_WINDOW = 0
 AT_PICKED_SCALES = 8192
+AT_LAST_WORDS = 9728
+AT_ROUNDED23 = 10752
+AT_CODES = 32768
 AT_ROUNDED = 10240
 AT_PLANES_PIECE0 = 13312
 AT_LATE_WORDS = 16384
@@ -94,8 +98,9 @@ def tile_list_pairwise_state_correction_kernel(
         picked_scales = shared.tile([P, S // 4], I32, name="picked_scales", align_bytes=64, offset=AT_PICKED_SCALES)
         v_words = [
             keep.tile([P, S], U32, name="v_words0", align_bytes=64),
-            shared.tile([P, S], U32, name="v_words1", align_bytes=64, offset=AT_LATE_WORDS),
+            shared.tile([P, SPLIT], U32, name="v_words1", align_bytes=64, offset=AT_LATE_WORDS),
         ]
+        last_words = shared.tile([P, S - SPLIT], U32, name="last_words", align_bytes=64, offset=AT_LAST_WORDS)
         nc.vector.tensor_copy(picked_scales[:].bitcast(U8), scale_window[:].bitcast(U8).indirect(offs_sb[:]))
 
         def carry_scales(g):
@@ -105,8 +110,8 @@ def tile_list_pairwise_state_correction_kernel(
                     in_=picked_scales[BLOCKS * g + r : BLOCKS * (g + 1) : 4, :],
                 )
 
-        def gather_words(g):
-            nc.vector.tensor_copy(v_words[g][:], words[g][:].bitcast(U32).indirect(offs_sb[:]))
+        def gather_words(picked, g, c0, c1):
+            nc.vector.tensor_copy(picked[:], words[g][:].bitcast(U32).indirect(offs_sb[:, c0 // 16 : c1 // 16]))
 
         carry_scales(0)
         w1_halves = [(0, PACK // 2), (PACK // 2, PACK)]
@@ -116,9 +121,21 @@ def tile_list_pairwise_state_correction_kernel(
         nc.sync.dma_start(pos1_sb[:], pos1)
         nc.sync.dma_start(pos2_sb[:], pos2)
         nc.sync.dma_start(out=gain_sb[:], in_=gain.rearrange("(p t) -> p t", t=PACK))
-        gather_words(0)
+        gather_words(v_words[0], 0, 0, S)
 
-        w1_codes = [keep.tile([P, H], U32, name="w1_codes%d" % g, align_bytes=64) for g in range(PASSES)]
+        codes0 = keep.tile([P, H], U32, name="codes0", align_bytes=64)
+        codes1 = [
+            shared.tile([P, P], U32, name="codes1_0", align_bytes=64, offset=AT_CODES),
+            keep.tile([P, P], U32, name="codes1_1", align_bytes=64),
+            shared.tile([P, 2 * P], U32, name="codes1_23", align_bytes=64, offset=AT_CODES),
+        ]
+
+        def w1_codes(g, t0, t1):
+            if g == 0:
+                return codes0[:, t0 * P : t1 * P]
+            first = min(t0, 2)
+            return codes1[first][:, (t0 - first) * P : (t1 - first) * P]
+
         w1_scales = keep.tile([P, PASSES, H], U8, name="w1_scales", align_bytes=64)
 
         def round_w1(copy, rounded, g, t0, t1, j0=0, j1=PACK):
@@ -129,7 +146,7 @@ def tile_list_pairwise_state_correction_kernel(
 
         def quantise_w1(rounded, g, t0, t1):
             nc.vector.quantize_mx(
-                out=w1_codes[g][:, t0 * P : t1 * P].bitcast(FP8X4),
+                out=w1_codes(g, t0, t1).bitcast(FP8X4),
                 scales=w1_scales[:, g, t0 * P : t1 * P],
                 in_=rounded[:].rearrange("p t m j -> p (t m j)"),
             )
@@ -157,16 +174,21 @@ def tile_list_pairwise_state_correction_kernel(
                 i = groups.index((t, s))
                 bank = i if i < FIRST_BANKS else FIRST_BANKS - RING + (i - FIRST_BANKS) % RING
                 h_banks[(t, s)] = psum.tile([P, BANK], F32, name="bank%d" % bank)
-            cols = slice(s * BANK, (s + 1) * BANK)
-            nc.tensor.matmul_mx(
-                out=h_banks[(t, s)][:],
-                lhsT=w1_codes[g][:, t * P : (t + 1) * P].bitcast(FP8X4),
-                lhsT_scale=w1_scales[:, g, t * P : (t + 1) * P],
-                rhs=v_words[g][:, cols].bitcast(FP8X4),
-                rhs_scale=v_scales[g][:].bitcast(U8)[4 * g :, cols],
-                start=(g == 0),
-                stop=(g == PASSES - 1),
-            )
+            c0, c1 = s * BANK, (s + 1) * BANK
+            cuts = [(c0, c1, v_words[g][:, c0:c1])] if g == 0 or c1 <= SPLIT else [
+                (c0, SPLIT, v_words[g][:, c0:SPLIT]),
+                (SPLIT, c1, last_words[:]),
+            ]
+            for k0, k1, moving in cuts:
+                nc.tensor.matmul_mx(
+                    out=h_banks[(t, s)][:, k0 - c0 : k1 - c0],
+                    lhsT=w1_codes(g, t, t + 1).bitcast(FP8X4),
+                    lhsT_scale=w1_scales[:, g, t * P : (t + 1) * P],
+                    rhs=moving.bitcast(FP8X4),
+                    rhs_scale=v_scales[g][:].bitcast(U8)[4 * g :, k0:k1],
+                    start=(g == 0),
+                    stop=(g == PASSES - 1 and k1 == c1),
+                )
 
         def empty_bank(t, s):
             copy = nc.vector.tensor_copy if (t, s) == (0, 1) else nc.scalar.copy
@@ -174,18 +196,22 @@ def tile_list_pairwise_state_correction_kernel(
 
         for t, s in groups[:FIRST_BANKS]:
             h_pass(t, s, 0)
-        gather_words(1)
+        gather_words(v_words[1], 1, 0, SPLIT)
         rounded1_0 = shared.tile([P, 1, P, PACK], BF16, name="rounded1_0", align_bytes=64, offset=AT_ROUNDED)
         for j0, j1 in w1_halves:
             round_w1(nc.scalar.copy, rounded1_0, 1, 0, 1, j0, j1)
         quantise_w1(rounded1_0, 1, 0, 1)
+        gather_words(last_words, 1, SPLIT, S)
         rounded1_1 = keep.tile([P, 1, P, PACK], BF16, name="rounded1_1", align_bytes=64)
-        rounded1_23 = shared.tile([P, 2, P, PACK], BF16, name="rounded1_23", align_bytes=64, offset=AT_ROUNDED)
+        rounded1_23 = shared.tile([P, 2, P, PACK], BF16, name="rounded1_23", align_bytes=64, offset=AT_ROUNDED23)
         round_w1(nc.scalar.copy, rounded1_1, 1, 1, 2)
         quantise_w1(rounded1_1, 1, 1, 2)
         round_w1(nc.vector.tensor_copy, rounded1_23, 1, 2, PACK)
+        for t, s in groups[:SLICES]:
+            h_pass(t, s, 1)
+            empty_bank(t, s)
         quantise_w1(rounded1_23, 1, 2, PACK)
-        for t, s in groups[:FIRST_BANKS]:
+        for t, s in groups[SLICES:FIRST_BANKS]:
             h_pass(t, s, 1)
             empty_bank(t, s)
         for t, s in groups[FIRST_BANKS:]:

@@ -37,6 +37,8 @@ AT_PICKED_SCALES = 8192
 AT_LAST_WORDS = 9728
 AT_ROUNDED23 = 10752
 AT_CODES = 32768
+AT_W2_RAW = 8448
+AT_EARLY_WORDS = 34816
 AT_ROUNDED = 10240
 AT_PLANES_PIECE0 = 13312
 AT_LATE_WORDS = 16384
@@ -73,7 +75,7 @@ def tile_list_pairwise_state_correction_kernel(
             keep.tile([P, PACK, H], F32, name="w1_raw0", align_bytes=256),
             shared.tile([P, PACK, H], F32, name="w1_raw1", align_bytes=256, offset=AT_SCALE_WINDOW),
         ]
-        w2_words_raw = keep.tile([P, 2 * H // 4], I32, name="w2_words_raw", align_bytes=256)
+        w2_words_raw = shared.tile([P, 2 * H // 4], I32, name="w2_words_raw", align_bytes=256, offset=AT_W2_RAW)
         gain_sb = shared.tile([P, PACK], F32, name="gain_sb", align_bytes=64, offset=AT_PICKED_SCALES)
 
         def load_words(g):
@@ -83,10 +85,10 @@ def tile_list_pairwise_state_correction_kernel(
             rows = w1[g * P * PACK : (g + 1) * P * PACK, :].rearrange("(p j) c -> p j c", j=PACK)
             nc.sync.dma_start(out=w1_raw[g][:, j0:j1, :], in_=rows[:, j0:j1, :])
 
-        nc.sync.dma_start(out=scale_window[0:QUAD, :], in_=tab_scales.rearrange("g q n -> (g q) n").bitcast(I32))
+        for g in range(PASSES):
+            nc.sync.dma_start(out=scale_window[BLOCKS * g : BLOCKS * (g + 1), :], in_=tab_scales[g].bitcast(I32))
         nc.sync.dma_start(offs_sb[:], offs)
         load_words(0)
-        nc.sync.dma_start(out=w2_words_raw[:], in_=w2_words[0].bitcast(I32))
         for quad in range(P // QUAD):
             nc.sync.dma_start(
                 out=w2_scales_raw[QUAD * quad : QUAD * quad + 4, :],
@@ -97,7 +99,7 @@ def tile_list_pairwise_state_correction_kernel(
 
         picked_scales = shared.tile([P, S // 4], I32, name="picked_scales", align_bytes=64, offset=AT_PICKED_SCALES)
         v_words = [
-            keep.tile([P, S], U32, name="v_words0", align_bytes=64),
+            shared.tile([P, S], U32, name="v_words0", align_bytes=64, offset=AT_EARLY_WORDS),
             shared.tile([P, SPLIT], U32, name="v_words1", align_bytes=64, offset=AT_LATE_WORDS),
         ]
         last_words = shared.tile([P, S - SPLIT], U32, name="last_words", align_bytes=64, offset=AT_LAST_WORDS)
@@ -120,6 +122,7 @@ def tile_list_pairwise_state_correction_kernel(
         carry_scales(1)
         nc.sync.dma_start(pos1_sb[:], pos1)
         nc.sync.dma_start(pos2_sb[:], pos2)
+        nc.sync.dma_start(out=w2_words_raw[:], in_=w2_words[0].bitcast(I32))
         nc.sync.dma_start(out=gain_sb[:], in_=gain.rearrange("(p t) -> p t", t=PACK))
         gather_words(v_words[0], 0, 0, S)
 
@@ -154,12 +157,8 @@ def tile_list_pairwise_state_correction_kernel(
         rounded0 = keep.tile([P, PACK, P, PACK], BF16, name="rounded0", align_bytes=64)
         round_w1(nc.scalar.copy, rounded0, 0, 0, PACK)
 
-        w2_codes = keep.tile([P, PACK, 2 * P], U8, name="w2_codes", align_bytes=64)
+        w2_codes = shared.tile([P, PACK, 2 * P], U8, name="w2_codes", align_bytes=64, offset=AT_EARLY_WORDS)
         w2_scale_bytes = keep.tile([P, PACK, P], U8, name="w2_scale_bytes", align_bytes=64)
-        nc.vector.tensor_copy(
-            w2_codes[:].rearrange("p t (m b) -> p t m b", b=2),
-            w2_words_raw[:].bitcast(U8).rearrange("p (m t b) -> p t m b", t=PACK, b=2),
-        )
         nc.vector.tensor_copy(
             w2_scale_bytes[:], w2_scales_raw[:].bitcast(U8).rearrange("p (m t) -> p t m", t=PACK)
         )
@@ -169,30 +168,36 @@ def tile_list_pairwise_state_correction_kernel(
         h_banks = {}
         h = [keep.tile([P, S], F32, name="h%d" % t) for t in range(PACK)]
 
-        def h_pass(t, s, g):
-            if g == 0:
-                i = groups.index((t, s))
-                bank = i if i < FIRST_BANKS else FIRST_BANKS - RING + (i - FIRST_BANKS) % RING
-                h_banks[(t, s)] = psum.tile([P, BANK], F32, name="bank%d" % bank)
+        def bank_cuts(t, s):
             c0, c1 = s * BANK, (s + 1) * BANK
-            cuts = [(c0, c1, v_words[g][:, c0:c1])] if g == 0 or c1 <= SPLIT else [
-                (c0, SPLIT, v_words[g][:, c0:SPLIT]),
-                (SPLIT, c1, last_words[:]),
-            ]
-            for k0, k1, moving in cuts:
-                nc.tensor.matmul_mx(
-                    out=h_banks[(t, s)][:, k0 - c0 : k1 - c0],
-                    lhsT=w1_codes(g, t, t + 1).bitcast(FP8X4),
-                    lhsT_scale=w1_scales[:, g, t * P : (t + 1) * P],
-                    rhs=moving.bitcast(FP8X4),
-                    rhs_scale=v_scales[g][:].bitcast(U8)[4 * g :, k0:k1],
-                    start=(g == 0),
-                    stop=(g == PASSES - 1 and k1 == c1),
-                )
+            return [(c0, SPLIT), (SPLIT, c1)] if t == 0 and c1 > SPLIT else [(c0, c1)]
+
+        def moving(g, c0, c1):
+            return last_words[:] if g == 1 and c0 == SPLIT else v_words[g][:, c0:c1]
+
+        def h_pass(t, s, g):
+            for c0, c1 in bank_cuts(t, s):
+                if g == 0:
+                    i = groups.index((t, s))
+                    bank = i if i < FIRST_BANKS else FIRST_BANKS - RING + (i - FIRST_BANKS) % RING
+                    bank = FIRST_BANKS if c0 == SPLIT else bank
+                    h_banks[(t, c0)] = psum.tile([P, c1 - c0], F32, name="bank%d" % bank)
+                cuts = [(c0, SPLIT), (SPLIT, c1)] if g == 1 and c0 < SPLIT < c1 else [(c0, c1)]
+                for k0, k1 in cuts:
+                    nc.tensor.matmul_mx(
+                        out=h_banks[(t, c0)][:, k0 - c0 : k1 - c0],
+                        lhsT=w1_codes(g, t, t + 1).bitcast(FP8X4),
+                        lhsT_scale=w1_scales[:, g, t * P : (t + 1) * P],
+                        rhs=moving(g, k0, k1).bitcast(FP8X4),
+                        rhs_scale=v_scales[g][:].bitcast(U8)[4 * g :, k0:k1],
+                        start=(g == 0),
+                        stop=(g == PASSES - 1 and k1 == c1),
+                    )
 
         def empty_bank(t, s):
-            copy = nc.vector.tensor_copy if (t, s) == (0, 1) else nc.scalar.copy
-            copy(h[t][:, s * BANK : (s + 1) * BANK], h_banks[(t, s)][:])
+            for c0, c1 in bank_cuts(t, s):
+                copy = nc.vector.tensor_copy if c0 == SPLIT else nc.scalar.copy
+                copy(h[t][:, c0:c1], h_banks[(t, c0)][:])
 
         for t, s in groups[:FIRST_BANKS]:
             h_pass(t, s, 0)
@@ -218,6 +223,11 @@ def tile_list_pairwise_state_correction_kernel(
             h_pass(t, s, 0)
             h_pass(t, s, 1)
             empty_bank(t, s)
+
+        nc.scalar.copy(
+            w2_codes[:].bitcast(U16).rearrange("p t m -> p m t"),
+            w2_words_raw[:].bitcast(U16).rearrange("p (m t) -> p m t", t=PACK),
+        )
 
         row_bytes = 4 * LAST
 

@@ -85,8 +85,7 @@ def tile_list_pairwise_state_correction_kernel(
             rows = w1[g * P * PACK : (g + 1) * P * PACK, :].rearrange("(p j) c -> p j c", j=PACK)
             nc.sync.dma_start(out=w1_raw[g][:, j0:j1, :], in_=rows[:, j0:j1, :])
 
-        for g in range(PASSES):
-            nc.sync.dma_start(out=scale_window[BLOCKS * g : BLOCKS * (g + 1), :], in_=tab_scales[g].bitcast(I32))
+        nc.sync.dma_start(out=scale_window[0:QUAD, :], in_=tab_scales.rearrange("g q n -> (g q) n").bitcast(I32))
         nc.sync.dma_start(offs_sb[:], offs)
         load_words(0)
         for quad in range(P // QUAD):
@@ -393,13 +392,17 @@ def tile_list_pairwise_state_correction_kernel(
             correct(0, t, t + 1, *pieces[1])
         for j0, j1 in halves:
             pick_d(PACK - 1, j0, j1)
-        for t in (1, 0, 2):
-            saturate(t, WIDE, NP)
-            for j0, j1 in halves:
-                apply_gain(t, j0, j1)
-        for step in (saturate, apply_gain):
-            for j0, j1 in halves:
-                step(PACK - 1, j0, j1)
+        steps = [(t, WIDE, NP) for t in (1, 0, 2)] + [(PACK - 1, j0, j1) for j0, j1 in halves]
+
+        def gains(t, j0, j1):
+            for c0 in range(j0, j1, P):
+                apply_gain(t, c0, c0 + P)
+
+        for i, step in enumerate(steps):
+            saturate(*step)
+            if i > 0:
+                gains(*steps[i - 1])
+        gains(*steps[-1])
         for j0, j1 in halves:
             interleave(j0, j1)
 

@@ -322,8 +322,8 @@ def tile_list_pairwise_state_correction_kernel(
 
         def interleave(j0, j1):
             nc.scalar.copy(
-                z_words[:, j0:j1, :].rearrange("p (c i) t -> p c t i", i=4),
-                planes_of(0, PACK, j0, j1).rearrange("p t (c i) -> p c t i", i=4),
+                z_words[:, j0:j1, :].rearrange("p (c i) t -> p c t i", i=8),
+                planes_of(0, PACK, j0, j1).rearrange("p t (c i) -> p c t i", i=8),
             )
 
         def quantise_z(j0, j1):

from contextlib import ExitStack

import concourse.mybir as mybir

K, T, S, NP, H = 1024, 4096, 1536, 768, 512
FLOPS = 2 * K * H * S + 2 * H * H * NP

F32 = mybir.dt.float32
BF16 = mybir.dt.bfloat16
I32 = mybir.dt.int32
U32 = mybir.dt.uint32
U16 = mybir.dt.uint16
U8 = mybir.dt.uint8
FP8X4 = mybir.dt.float8_e4m3fn_x4
FP4X4 = mybir.dt.float4_e2m1fn_x4
ALU = mybir.AluOpType
ACT = mybir.ActivationFunctionType

P = 128
PACK = 4
PASSES = K // (P * PACK)
BLOCKS = 16
QUAD = 32
BANK = 512
BANKS = 8
SLICES = S // BANK
SPLIT = S - BANK // 2
FIRST_BANKS = 2 * SLICES
RING = SLICES + 1
WIDE = 512
PIECE = WIDE // 2
LAST = NP - WIDE
HALF = WIDE + P

AT_SCALE_WINDOW = 0
AT_PICKED_SCALES = 8192
AT_LAST_WORDS = 9728
AT_ROUNDED23 = 10752
AT_CODES = 32768
AT_W2_RAW = 8448
AT_EARLY_WORDS = 34816
AT_ROUNDED = 10240
AT_PLANES_PIECE0 = 13312
AT_LATE_WORDS = 16384
AT_D_WIDE2 = 22528
AT_PLANES_PIECE1 = 26624
AT_PLANES_HALF0 = 29696


def tile_list_pairwise_state_correction_kernel(
    tc, tab_words, tab_scales, offs, pos1, pos2, w1, gain, w2_words, w2_scales, out
):
    nc = tc.nc
    with ExitStack() as ctx:
        lists = ctx.enter_context(tc.tile_pool(name="lists", bufs=1))
        keep = ctx.enter_context(tc.tile_pool(name="keep", bufs=1))
        shared = ctx.enter_context(tc.tile_pool(name="shared", bufs=1))
        psum = ctx.enter_context(tc.psum_pool(name="psum", bufs=1))

        offs_sb = lists.tile([P, S // 16], U16, name="offs_sb")
        pos1_sb = lists.tile([P, NP // 16], U16, name="pos1_sb")
        pos2_sb = lists.tile([P, NP // 16], U16, name="pos2_sb")

        scale_window = shared.tile([P, T // 4], I32, name="scale_window", align_bytes=256, offset=AT_SCALE_WINDOW)
        v_scales = [keep.tile([P, S // 4], I32, name="v_scales%d" % g, align_bytes=256) for g in range(PASSES)]
        w2_scales_raw = keep.tile([P, H // 4], I32, name="w2_scales_raw", align_bytes=64)
        nc.vector.memset(w2_scales_raw[:], 0)
        nc.vector.memset(scale_window[QUAD : 2 * QUAD, :], 0)
        nc.vector.memset(scale_window[2 * QUAD : P, :], 0)
        for g in range(PASSES):
            nc.vector.memset(v_scales[g][:], 0)

        words = [keep.tile([P, T], I32, name="words%d" % g, align_bytes=256) for g in range(PASSES)]
        w1_raw = [
            keep.tile([P, PACK, H], F32, name="w1_raw0", align_bytes=256),
            shared.tile([P, PACK, H], F32, name="w1_raw1", align_bytes=256, offset=AT_SCALE_WINDOW),
        ]
        w2_words_raw = shared.tile([P, 2 * H // 4], I32, name="w2_words_raw", align_bytes=256, offset=AT_W2_RAW)
        gain_sb = shared.tile([P, PACK], F32, name="gain_sb", align_bytes=64, offset=AT_PICKED_SCALES)

        def load_words(g):
            nc.sync.dma_start(out=words[g][:], in_=tab_words[g].rearrange("p n i -> p (n i)").bitcast(I32))

        def load_w1(g, j0, j1):
            rows = w1[g * P * PACK : (g + 1) * P * PACK, :].rearrange("(p j) c -> p j c", j=PACK)
            nc.sync.dma_start(out=w1_raw[g][:, j0:j1, :], in_=rows[:, j0:j1, :])

        nc.sync.dma_start(out=scale_window[0:QUAD, :], in_=tab_scales.rearrange("g q n -> (g q) n").bitcast(I32))
        nc.sync.dma_start(offs_sb[:], offs)
        load_words(0)
        for quad in range(P // QUAD):
            nc.sync.dma_start(
                out=w2_scales_raw[QUAD * quad : QUAD * quad + 4, :],
                in_=w2_scales[0, 4 * quad : 4 * quad + 4, :].bitcast(I32),
            )
        load_w1(0, 0, PACK)
        load_words(1)

        picked_scales = shared.tile([P, S // 4], I32, name="picked_scales", align_bytes=64, offset=AT_PICKED_SCALES)
        v_words = [
            shared.tile([P, S], U32, name="v_words0", align_bytes=64, offset=AT_EARLY_WORDS),
            shared.tile([P, SPLIT], U32, name="v_words1", align_bytes=64, offset=AT_LATE_WORDS),
        ]
        last_words = shared.tile([P, S - SPLIT], U32, name="last_words", align_bytes=64, offset=AT_LAST_WORDS)
        nc.vector.tensor_copy(picked_scales[:].bitcast(U8), scale_window[:].bitcast(U8).indirect(offs_sb[:]))

        def carry_scales(g):
            for r in range(4):
                nc.sync.dma_start(
                    out=v_scales[g][4 * g + r : P : QUAD, :],
                    in_=picked_scales[BLOCKS * g + r : BLOCKS * (g + 1) : 4, :],
                )

        def gather_words(picked, g, c0, c1):
            nc.vector.tensor_copy(picked[:], words[g][:].bitcast(U32).indirect(offs_sb[:, c0 // 16 : c1 // 16]))

        carry_scales(0)
        w1_halves = [(0, PACK // 2), (PACK // 2, PACK)]
        for j0, j1 in w1_halves:
            load_w1(1, j0, j1)
        carry_scales(1)
        nc.sync.dma_start(pos1_sb[:], pos1)
        nc.sync.dma_start(pos2_sb[:], pos2)
        nc.sync.dma_start(out=w2_words_raw[:], in_=w2_words[0].bitcast(I32))
        nc.sync.dma_start(out=gain_sb[:], in_=gain.rearrange("(p t) -> p t", t=PACK))
        gather_words(v_words[0], 0, 0, S)

        codes0 = keep.tile([P, H], U32, name="codes0", align_bytes=64)
        codes1 = [
            shared.tile([P, P], U32, name="codes1_0", align_bytes=64, offset=AT_CODES),
            keep.tile([P, P], U32, name="codes1_1", align_bytes=64),
            shared.tile([P, 2 * P], U32, name="codes1_23", align_bytes=64, offset=AT_CODES),
        ]

        def w1_codes(g, t0, t1):
            if g == 0:
                return codes0[:, t0 * P : t1 * P]
            first = min(t0, 2)
            return codes1[first][:, (t0 - first) * P : (t1 - first) * P]

        w1_scales = keep.tile([P, PASSES, H], U8, name="w1_scales", align_bytes=64)

        def round_w1(copy, rounded, g, t0, t1, j0=0, j1=PACK):
            copy(
                rounded[:].rearrange("p t m j -> p m j t")[:, :, j0:j1, :],
                w1_raw[g][:].rearrange("p j (m t) -> p m j t", t=PACK)[:, :, j0:j1, t0:t1],
            )

        def quantise_w1(rounded, g, t0, t1):
            nc.vector.quantize_mx(
                out=w1_codes(g, t0, t1).bitcast(FP8X4),
                scales=w1_scales[:, g, t0 * P : t1 * P],
                in_=rounded[:].rearrange("p t m j -> p (t m j)"),
            )

        rounded0 = keep.tile([P, PACK, P, PACK], BF16, name="rounded0", align_bytes=64)
        round_w1(nc.scalar.copy, rounded0, 0, 0, PACK)

        w2_codes = shared.tile([P, PACK, 2 * P], U8, name="w2_codes", align_bytes=64, offset=AT_EARLY_WORDS)
        w2_scale_bytes = keep.tile([P, PACK, P], U8, name="w2_scale_bytes", align_bytes=64)
        nc.vector.tensor_copy(
            w2_scale_bytes[:], w2_scales_raw[:].bitcast(U8).rearrange("p (m t) -> p t m", t=PACK)
        )
        quantise_w1(rounded0, 0, 0, PACK)

        groups = [(t, s) for t in range(PACK) for s in range(SLICES)]
        h_banks = {}
        h = [keep.tile([P, S], F32, name="h%d" % t) for t in range(PACK)]

        def bank_cuts(t, s):
            c0, c1 = s * BANK, (s + 1) * BANK
            return [(c0, SPLIT), (SPLIT, c1)] if t == 0 and c1 > SPLIT else [(c0, c1)]

        def moving(g, c0, c1):
            return last_words[:] if g == 1 and c0 == SPLIT else v_words[g][:, c0:c1]

        def h_pass(t, s, g):
            for c0, c1 in bank_cuts(t, s):
                if g == 0:
                    i = groups.index((t, s))
                    bank = i if i < FIRST_BANKS else FIRST_BANKS - RING + (i - FIRST_BANKS) % RING
                    bank = FIRST_BANKS if c0 == SPLIT else bank
                    h_banks[(t, c0)] = psum.tile([P, c1 - c0], F32, name="bank%d" % bank)
                cuts = [(c0, SPLIT), (SPLIT, c1)] if g == 1 and c0 < SPLIT < c1 else [(c0, c1)]
                for k0, k1 in cuts:
                    nc.tensor.matmul_mx(
                        out=h_banks[(t, c0)][:, k0 - c0 : k1 - c0],
                        lhsT=w1_codes(g, t, t + 1).bitcast(FP8X4),
                        lhsT_scale=w1_scales[:, g, t * P : (t + 1) * P],
                        rhs=moving(g, k0, k1).bitcast(FP8X4),
                        rhs_scale=v_scales[g][:].bitcast(U8)[4 * g :, k0:k1],
                        start=(g == 0),
                        stop=(g == PASSES - 1 and k1 == c1),
                    )

        def empty_bank(t, s):
            for c0, c1 in bank_cuts(t, s):
                copy = nc.vector.tensor_copy if c0 == SPLIT else nc.scalar.copy
                copy(h[t][:, c0:c1], h_banks[(t, c0)][:])

        for t, s in groups[:FIRST_BANKS]:
            h_pass(t, s, 0)
        gather_words(v_words[1], 1, 0, SPLIT)
        rounded1_0 = shared.tile([P, 1, P, PACK], BF16, name="rounded1_0", align_bytes=64, offset=AT_ROUNDED)
        for j0, j1 in w1_halves:
            round_w1(nc.scalar.copy, rounded1_0, 1, 0, 1, j0, j1)
        quantise_w1(rounded1_0, 1, 0, 1)
        gather_words(last_words, 1, SPLIT, S)
        rounded1_1 = keep.tile([P, 1, P, PACK], BF16, name="rounded1_1", align_bytes=64)
        rounded1_23 = shared.tile([P, 2, P, PACK], BF16, name="rounded1_23", align_bytes=64, offset=AT_ROUNDED23)
        round_w1(nc.scalar.copy, rounded1_1, 1, 1, 2)
        quantise_w1(rounded1_1, 1, 1, 2)
        round_w1(nc.vector.tensor_copy, rounded1_23, 1, 2, PACK)
        for t, s in groups[:SLICES]:
            h_pass(t, s, 1)
            empty_bank(t, s)
        quantise_w1(rounded1_23, 1, 2, PACK)
        for t, s in groups[SLICES:FIRST_BANKS]:
            h_pass(t, s, 1)
            empty_bank(t, s)
        for t, s in groups[FIRST_BANKS:]:
            h_pass(t, s, 0)
            h_pass(t, s, 1)
            empty_bank(t, s)

        nc.scalar.copy(
            w2_codes[:].bitcast(U16).rearrange("p t m -> p m t"),
            w2_words_raw[:].bitcast(U16).rearrange("p (m t) -> p m t", t=PACK),
        )

        row_bytes = 4 * LAST

        def on(name, shape, dtype, offset):
            return shared.tile(shape, dtype, name=name, align_bytes=64, offset=offset)

        def row_on(name, planes_at, place):
            return on(name, [P, LAST], F32, planes_at + place * row_bytes - 3 * row_bytes // 4)

        a_wide = keep.tile([P, PACK, WIDE], F32, name="a_wide")
        a_last = keep.tile([P, PACK, LAST], F32, name="a_last")
        d_wide = [
            keep.tile([P, WIDE], F32, name="d_wide0"),
            on("d_wide1", [P, WIDE], F32, AT_LATE_WORDS),
            on("d_wide2", [P, WIDE], F32, AT_D_WIDE2),
            keep.tile([P, WIDE], F32, name="d_wide3"),
        ]
        early_tanh = a_last[:].rearrange("p t n -> p (t n)")[:, 3 * LAST // 2 : 3 * LAST // 2 + WIDE]
        tanh_wide = [
            early_tanh,
            early_tanh,
            on("tanh_wide2", [P, WIDE], F32, AT_LATE_WORDS)[:],
            on("tanh_wide3", [P, WIDE], F32, AT_D_WIDE2)[:],
        ]
        planes_wide = [
            on("planes_piece0", [P, PACK, PIECE], BF16, AT_PLANES_PIECE0),
            on("planes_piece1", [P, PACK, PIECE], BF16, AT_PLANES_PIECE1),
        ]
        planes_last = [
            on("planes_half0", [P, PACK, P], BF16, AT_PLANES_HALF0),
            keep.tile([P, PACK, P], BF16, name="planes_half1"),
        ]
        result_wide3 = on("result_wide3", [P, 1, WIDE], F32, AT_PLANES_HALF0)
        d_last = [
            row_on("d_last0", AT_PLANES_PIECE0, 0),
            keep.tile([P, LAST], F32, name="d_last1"),
            row_on("d_last2", AT_PLANES_PIECE0, 1),
            row_on("d_last3", AT_PLANES_PIECE1, 0),
        ]
        tanh_last = [
            keep.tile([P, LAST], F32, name="tanh_last0"),
            row_on("tanh_last1", AT_PLANES_PIECE0, 2),
            keep.tile([P, LAST], F32, name="tanh_last2"),
            keep.tile([P, LAST], F32, name="tanh_last3"),
        ]
        z_words = keep.tile([P, NP, PACK], BF16, name="z_words", align_bytes=64)
        z_codes = keep.tile([P, NP], U32, name="z_codes", align_bytes=64)
        z_scales = keep.tile([P, NP], U8, name="z_scales", align_bytes=64)
        result = keep.tile([P, PACK, NP], F32, name="result", align_bytes=256)
        out_rows = out.rearrange("(p t) j -> p t j", t=PACK)

        def flat(ap):
            return ap.rearrange("p t n -> p (t n)")

        def a_of(t0, t1, j0, j1):
            if j0 < WIDE:
                return a_wide[:, t0:t1, j0:j1]
            return a_last[:, t0:t1, j0 - WIDE : j1 - WIDE]

        def d_of(t, j0, j1):
            if j0 < WIDE:
                return d_wide[t][:, j0:j1]
            return d_last[t][:, j0 - WIDE : j1 - WIDE]

        def tanh_of(t, j0, j1):
            if j0 < WIDE:
                return tanh_wide[t][:, j0:j1]
            return tanh_last[t][:, j0 - WIDE : j1 - WIDE]

        def planes_of(t0, t1, j0, j1):
            if j0 < WIDE:
                return planes_wide[j0 // PIECE][:, t0:t1, :]
            return planes_last[(j0 - WIDE) // P][:, t0:t1, :]

        def pick_a(t, j0, j1):
            nc.vector.tensor_copy(flat(a_of(t, t + 1, j0, j1)), h[t][:].indirect(pos1_sb[:, j0 // 16 : j1 // 16]))

        def pick_d(t, j0, j1):
            nc.vector.tensor_tensor(
                d_of(t, j0, j1),
                h[t][:].indirect(pos2_sb[:, j0 // 16 : j1 // 16]),
                flat(a_of(t, t + 1, j0, j1)),
                ALU.subtract,
            )

        def saturate(t, j0, j1):
            nc.scalar.activation(tanh_of(t, j0, j1), d_of(t, j0, j1), ACT.Tanh, scale=-1.0)

        def apply_gain(t, j0, j1):
            nc.scalar.activation(
                flat(planes_of(t, t + 1, j0, j1)), tanh_of(t, j0, j1), ACT.Copy, scale=gain_sb[:, t : t + 1]
            )

        def interleave(j0, j1):
            nc.scalar.copy(
                z_words[:, j0:j1, :].rearrange("p (c i) t -> p c t i", i=8),
                planes_of(0, PACK, j0, j1).rearrange("p t (c i) -> p c t i", i=8),
            )

        def quantise_z(j0, j1):
            nc.vector.quantize_mx(
                out=z_codes[:, j0:j1].bitcast(FP8X4),
                scales=z_scales[:, j0:j1],
                in_=z_words[:, j0:j1, :].rearrange("p n t -> p (n t)"),
            )

        y_banks = {}

        def open_bank(j0, j1, t0, t1, bank):
            y_banks[(j0, t0)] = psum.tile([P, t1 - t0, j1 - j0], F32, name="bank%d" % bank)

        def correct(bank_j0, t0, t1, j0, j1):
            for t in range(t0, t1):
                nc.tensor.matmul_mx(
                    out=y_banks[(bank_j0, t0)][:, t - t0, j0 - bank_j0 : j1 - bank_j0],
                    lhsT=w2_codes[:, t, :].bitcast(FP4X4),
                    lhsT_scale=w2_scale_bytes[:, t, :],
                    rhs=z_codes[:, j0:j1].bitcast(FP8X4),
                    rhs_scale=z_scales[:, j0:j1],
                    start=True,
                    stop=True,
                )

        def finish(j0, j1, t0, t1):
            rows = result_wide3[:] if (j0, t0) == (0, PACK - 1) else result[:, t0:t1, j0:j1]
            nc.vector.tensor_tensor(rows, y_banks[(j0, t0)][:], a_of(t0, t1, j0, j1), ALU.add)
            nc.sync.dma_start(out=out_rows[:, t0:t1, j0:j1], in_=rows)

        pieces = [(j0, j0 + PIECE) for j0 in range(0, WIDE, PIECE)]
        halves = [(WIDE, HALF), (HALF, NP)]

        pick_a(0, 0, WIDE)
        pick_a(0, WIDE, NP)
        pick_d(0, 0, WIDE)
        for pick in (pick_a, pick_d):
            for t in (1, 2):
                pick(t, 0, WIDE)
        for pick in (pick_a, pick_d):
            for j0, j1 in pieces:
                pick(PACK - 1, j0, j1)
        for t in range(PACK - 1):
            saturate(t, 0, WIDE)
            for j0, j1 in pieces:
                apply_gain(t, j0, j1)
        for step in (saturate, apply_gain):
            for j0, j1 in pieces:
                step(PACK - 1, j0, j1)
        for j0, j1 in pieces:
            interleave(j0, j1)

        pick_a(1, WIDE, NP)
        pick_a(2, WIDE, NP)
        pick_d(1, WIDE, NP)
        pick_a(3, WIDE, NP)
        quantise_z(*pieces[0])
        for t in range(PACK):
            open_bank(0, WIDE, t, t + 1, BANKS - PACK + t)
            correct(0, t, t + 1, *pieces[0])
        pick_d(0, WIDE, NP)
        pick_d(2, WIDE, NP)
        quantise_z(*pieces[1])
        for t in range(PACK):
            correct(0, t, t + 1, *pieces[1])
        for j0, j1 in halves:
            pick_d(PACK - 1, j0, j1)
        steps = [(t, WIDE, NP) for t in (1, 0, 2)] + [(PACK - 1, j0, j1) for j0, j1 in halves]

        def gains(t, j0, j1):
            for c0 in range(j0, j1, P):
                apply_gain(t, c0, c0 + P)

        for i, step in enumerate(steps):
            saturate(*step)
            if i > 0:
                gains(*steps[i - 1])
        gains(*steps[-1])
        for j0, j1 in halves:
            interleave(j0, j1)

        for i, (j0, j1) in enumerate(halves):
            quantise_z(j0, j1)
            for t in (0, 2):
                open_bank(j0, j1, t, t + 2, 2 * i + t // 2)
                correct(j0, t, t + 2, j0, j1)
        for t in range(PACK):
            finish(0, WIDE, t, t + 1)
        for j0, j1 in halves:
            for t in (0, 2):
                finish(j0, j1, t, t + 2)
